import numpy as np, ml_dtypes
CORES = [2,3,42,43,82,83,122,123]
N = 8
BF = ml_dtypes.bfloat16
def gentries(a):
    return np.ascontiguousarray(a.reshape(8, 16, -1).transpose(0, 2, 1)).reshape(8, -1)
def gtable(e):
    e = np.asarray(e); return np.ascontiguousarray(e.reshape(8, -1, 16).transpose(0, 2, 1)).reshape(128, -1).astype(np.int32)
V, H, I, L, R, CAP, MV, RO = 3072, 1024, 256, 2560, 1024, 256, 4, 2
Z = V + I * RO
W = Z + I * (RO - 1)
def grow(rng, few=0):
    S = H // 8; n = (V - H) // S
    lo = 0.1 + 0.25 * rng.random((N, 8, 1, S)); wd = 0.2 + 0.4 * rng.random((N, 8, 1, S)); sh = 1.5 * rng.standard_normal((N, 8, 16, S))
    def keys(pos):
        x = 15 * (lo[..., None] + wd[..., None] * pos) + sh[..., None] + 0.7 * rng.standard_normal((N, 8, 16, S, 8 + n), dtype=np.float32)
        x = np.clip(np.rint(x), 0, 15).astype(np.int64)
        return np.concatenate([x[..., :8].reshape(N, 8, 16, H), x[..., 8:].reshape(N, 8, 16, V - H)], axis=3)
    half = np.linspace(0.0, 1.0, 2 * n + 1)
    pa = np.concatenate([np.array([0.5, 0.25, 0.75, 0.1, 0.3, 0.5, 0.7, 0.9]), half[1::2]])
    pb = np.concatenate([np.array([1.0, 0.5, 1.0, 0.2, 0.4, 0.6, 0.8, 1.0]), half[2::2]])
    ids = np.concatenate([8 * np.arange(S)[:, None] + np.arange(8), H + n * np.arange(S)[:, None] + np.arange(n)], axis=1)
    kids = [[1, 3, 5] + [8 + 2 * i * n // 10 for i in range(5)], [2, 4, 6] + [8 + (2 * i + 1) * n // 10 for i in range(5)]]
    lk = [np.concatenate([ids[:, k].reshape(-1), np.zeros(V - H, np.int64)]) for k in kids]
    r = np.array([-1, 2, -1, 4, 5, 6, 7, -1] + list(range(9, 8 + n)) + [-1])
    lr = np.where(r >= 0, ids[:, r], -1); lr = np.concatenate([lr[:, :8].reshape(-1), lr[:, 8:].reshape(-1)])
    ph = np.concatenate([np.argsort(rng.random((N, 8, H)), axis=-1), H + np.argsort(rng.random((N, 8, V - H)), axis=-1)], axis=2); inv = np.argsort(ph, axis=-1)
    ka = np.take_along_axis(keys(pa), inv[:, :, None, :], 3); kb = np.take_along_axis(keys(pb), inv[:, :, None, :], 3)
    ca, cb = [np.where(np.arange(V) < H, np.take_along_axis(ph, k[inv], 2), rng.integers(0, R, (N, 8, V))) for k in lk]
    rr = lr[inv]; rt = np.where((rr >= 0) & (rng.random((N, 8, V)) < 0.94), np.take_along_axis(ph, np.maximum(rr, 0), 2), -1)
    it = np.where(rng.random((N, 8, 1, R)) < 0.5, rng.integers(0, 3, (N, 8, 16, R)), rng.integers(0, 16, (N, 8, 16, R)))
    if few:
        pool = 8 * rng.integers(0, S, (N, 8, few)) + rng.integers(3, 8, (N, 8, few)); s = np.take_along_axis(pool, rng.integers(0, few, (N, 8, L)), 2)
    else: s = rng.integers(0, H, (N, 8, L))
    g = s >> 3; top = rng.choice(np.array([1.05, 1.2, 1.5, 2.0]), (N, 8, 1)); top[0, 0] = 2.0; top[1, 0] = 1.05
    u = (top + 0.1) * rng.random((N, 8, L)) - 0.1
    x = 15 * (np.take_along_axis(lo[:, :, 0], g, 2) + np.take_along_axis(wd[:, :, 0], g, 2) * u)
    q = np.clip(np.rint(x[:, :, None] + np.take_along_axis(sh, g[:, :, None, :], 3) + 0.7 * rng.standard_normal((N, 8, 16, L), dtype=np.float32)), 0, 15).astype(np.int64)
    v = np.take_along_axis(ph, s, 2); w = rng.integers(0, 1024, (N, 8, 16))
    return ka, kb, ca, cb, rt, it, q, v, w
def pack(ka, kb, ca, cb, rt, it, q, v, w):
    return {"kk": (ka + 16 * kb).reshape(N, 128, V).astype(np.float32).astype(BF), "c0": ca.astype(np.int32), "c1": cb.astype(np.int32), "rt": rt.astype(np.int32),
            "rec": it.reshape(N, 128, R).astype(np.float32).astype(BF), "qs": q.reshape(N, 128, L).astype(np.float32).astype(BF),
            "v0": np.stack([gtable(a) for a in v]), "wt": w.reshape(N, 128, 1).astype(np.int32)}
def setup_inputs(rng):
    return pack(*grow(rng))
def setup_inputs_room(rng):
    ka, kb, ca, cb, rt, it, q, v, w = grow(rng)
    for a in range(N):
        for g in range(8):
            e = rng.permutation(H)[:8]; z = H + rng.permutation(V - H)[:8]
            ca[a, g, e] = z; cb[a, g, e] = z; rt[a, g, e] = -1; rt[a, g, z] = -1; kb[a, g][:, z] = np.minimum(kb[a, g][:, z], 14)
            n = int(rng.choice(np.array([0, 1, CAP - 1, CAP, CAP + 1, 2 * CAP])))
            if a == 0: n = (CAP, CAP + 1, 2 * CAP, CAP - 1, 1, 0, CAP, CAP + 1)[g]
            if a == 1: n = (CAP, CAP, CAP + 1, 2 * CAP, CAP, CAP, 0, 1)[g]
            o = rng.permutation(L)
            if g % 2 == 0: o = np.concatenate([np.array([0, L - 1]), o[(o > 0) & (o < L - 1)]])
            hot, cool = o[:n], o[n:]
            m = np.argsort(rng.random((16, n)), axis=0); q[a, g][:, hot] = np.where(m < rng.integers(9, 17, n), 15, rng.integers(0, 16, (16, n)))
            m = np.argsort(rng.random((16, L - n)), axis=0); q[a, g][:, cool] = np.where(m < rng.integers(8, 17, L - n), 0, q[a, g][:, cool])
            v[a, g, hot] = rng.choice(e, n)
    return pack(ka, kb, ca, cb, rt, it, q, v, w)
def setup_inputs_crowd(rng):
    ka, kb, ca, cb, rt, it, q, v, w = grow(rng, 6)
    for a in range(N):
        for g in (5, 6, 7):
            if g < 7 or a % 2 == 0:
                z = H + rng.permutation(V - H)[:H + 1]; kb[a, g] = 15; rt[a, g] = -1; ca[a, g, :H] = z[:H]; cb[a, g, :H] = z[:H]
            if g == 5: v[a, g, :I] = rng.permutation(H)[:I]
            if g == 6: v[a, g] = int(rng.integers(0, H))
            if g == 7 and a % 2 == 0:
                e = int(rng.integers(0, H // 4)); y = int(z[H]); ca[a, g, e] = y; cb[a, g, e] = y; kb[a, g, :, y] = rng.integers(0, 14, 16)
                hot = np.concatenate([np.array([0]), 1 + rng.permutation(L - 1)[:CAP - 1]])
                q[a, g][:, hot] = rng.integers(14, 16, (16, CAP)); q[a, g, :, 0] = 15; w[a, g] = 1023
                v[a, g] = rng.integers(H // 4, H, L); v[a, g, hot] = e
            if g == 7 and a % 2 == 1:
                o = rng.permutation(H)[:MV + 2]; y = int(rng.integers(H, V)); kb[a, g][:, o] = 0; kb[a, g, :, y] = 0
                rt[a, g, o[:-1]] = o[1:]; rt[a, g, o[-1]] = -1; rt[a, g, y] = -1; ca[a, g, o[-1]] = y; cb[a, g, o[-1]] = y
                v[a, g] = int(o[0]); q[a, g] = rng.integers(1, 16, (16, L))
    return pack(ka, kb, ca, cb, rt, it, q, v, w)
def setup_inputs_votes(rng):
    ka, kb, ca, cb, rt, it, q, v, w = grow(rng)
    base = rng.integers(2, 12, (N, 8, 16, 1)); kb = base + rng.integers(0, 2, (N, 8, 1, V)); ka = base - rng.integers(0, 2, (N, 8, 1, V))
    m = np.argsort(rng.random((N, 8, 16, L)), axis=2) < rng.choice(np.array([8, 9]), (N, 8, 1, L))
    q = np.where(m, base + 1 + rng.integers(0, 2, (N, 8, 1, L)), base - rng.integers(0, 2, (N, 8, 16, L)))
    it[..., ::2] = 0
    return pack(ka, kb, ca, cb, rt, it, q, v, w)
def setup_inputs_ends(rng):
    ka, kb, ca, cb, rt, it, q, v, w = grow(rng); inner = np.arange(V) < H
    for a in range(N):
        for g in range(8):
            if g % 4 == 0: rt[a, g] = -1
            if g % 4 == 1:
                o = rng.permutation(H); rt[a, g, o] = np.roll(o, -1); o = H + rng.permutation(V - H); rt[a, g, o] = np.roll(o, -1)
            if g % 4 == 2:
                e = np.array([0, H - 1, H, V - 1]); z = np.array([0, R - 1])
                ca[a, g] = np.where(inner, rng.choice(e, V), rng.choice(z, V)); cb[a, g] = np.where(inner, rng.choice(e, V), rng.choice(z, V))
            if g % 4 == 3: rt[a, g] = np.where(rng.random(V) < 0.3, np.arange(V), rt[a, g])
    v[:, :, 0] = 0; v[:, :, L - 1] = H - 1
    return pack(ka, kb, ca, cb, rt, it, q, v, w)
def setup_inputs_spread(rng):
    inner = np.arange(V) < H
    def some(n):
        return np.minimum((16 * rng.random((N, 8, 16, n)) ** rng.choice(np.array([0.4, 1.0, 2.0, 4.0]), (N, 8, 1, n))).astype(np.int64), 15)
    ka, kb, q, it = some(V), some(V), some(L), some(R)
    ca = np.where(inner, rng.integers(0, V, (N, 8, V)), rng.integers(0, R, (N, 8, V))); cb = np.where(inner, rng.integers(0, V, (N, 8, V)), rng.integers(0, R, (N, 8, V)))
    rt = np.where(inner, rng.integers(0, H, (N, 8, V)), rng.integers(H, V, (N, 8, V))); rt = np.where(rng.random((N, 8, V)) < rng.choice(np.array([0.05, 0.2, 0.5]), (N, 8, 1)), -1, rt)
    v = rng.integers(0, H, (N, 8, L))
    for a in range(N):
        for g in range(8):
            o = 1 + rng.permutation(H - 1)[:2]; e = int(o[0]); u = 0 if g % 2 == 0 else int(o[1])
            o = H + rng.permutation(V - H)[:2]; z = int(o[0]); y = int(o[1])
            v[a, g, 0] = e; v[a, g, 1] = u; q[a, g, :, :2] = 0
            kb[a, g, :, e] = 0; ka[a, g, :, z] = np.maximum(ka[a, g, :, z], 1); rt[a, g, e] = u; ca[a, g, e] = z; cb[a, g, e] = z
            ka[a, g, :, u] = 0; kb[a, g, :, u] = 15; ka[a, g, :, y] = 0; ca[a, g, u] = y; cb[a, g, u] = z
    return pack(ka, kb, ca, cb, rt, it, q, v, rng.integers(0, 1024, (N, 8, 16)))
def check_inputs(d):
    bad = []
    for k, hi in (("kk", 255), ("rec", 15), ("qs", 15), ("v0", H - 1), ("wt", 1023)):
        x = np.asarray(d[k]).astype(np.float64)
        if not np.all((x >= 0) & (x <= hi) & (x == np.floor(x))): bad.append("range of " + k)
    for k in ("c0", "c1"):
        x = np.asarray(d[k]).astype(np.int64)
        if not (np.all((x[..., :H] >= 0) & (x[..., :H] < V)) and np.all((x[..., H:] >= 0) & (x[..., H:] < R))): bad.append("range of " + k)
    x = np.asarray(d["rt"]).astype(np.int64); y = x[..., H:]
    if not (np.all((x[..., :H] >= -1) & (x[..., :H] < H)) and np.all((y == -1) | ((y >= H) & (y < V)))): bad.append("range of rt")
    return bad
def above(a, b):
    return np.sum(a > b, axis=2) >= 9
def pick(t, ix):
    return np.take_along_axis(t, ix[:, :, None, :] if t.ndim == 4 else ix, -1)
def lowest(ok, u):
    i = np.arange(u.shape[2]); key = np.where(ok, u, W + i)
    return ok & ~np.any((key[..., :, None] == key[..., None, :]) & (i[None, :] < i[:, None]), axis=3)
def insert(ka, kb, ca, cb, gr, win, n, m, p, cn, new):
    a, e, i = np.nonzero(win); n = n[a, e, i]; m = m[a, e, :, i]; p = p[a, e, i]; cn = cn[a, e, i]; x = new[i]
    k0 = ka[a, e, :, n]; k1 = kb[a, e, :, n]; b = np.sum(m > k0, axis=1) >= 9
    o0 = np.where(b, ca[a, e, n], cn); o1 = np.where(b, cn, cb[a, e, n])
    ka[a, e, :, x] = k1; kb[a, e, :, x] = k1; ca[a, e, x] = o1; cb[a, e, x] = o1; gr[a, e, x] = gr[a, e, n]; gr[a, e, n] = x
    kb[a, e, :, n] = np.where(b[:, None], m, k0); ka[a, e, :, n] = np.where(b[:, None], k0, m)
    cb[a, e, n] = np.where(b, p, o0); ca[a, e, n] = np.where(b, o0, p)
def reference(kk, c0, c1, rt, rec, qs, v0, wt):
    k = kk.astype(np.float32).astype(np.int16).reshape(N, 8, 16, V)
    ka = np.zeros((N, 8, 16, W), np.int16); kb = np.zeros((N, 8, 16, W), np.int16); ka[..., :V] = k & 15; kb[..., :V] = k >> 4
    ca = np.zeros((N, 8, W), np.int64); cb = np.zeros((N, 8, W), np.int64); gr = np.zeros((N, 8, W), np.int64)
    ca[..., :V] = c0; cb[..., :V] = c1; gr[..., :V] = rt
    it = rec.astype(np.float32).astype(np.int16).reshape(N, 8, 16, R); q = qs.astype(np.float32).astype(np.int16).reshape(N, 8, 16, L)
    wg = wt.astype(np.int64).reshape(N, 8, 16); v = np.stack([gentries(a) for a in v0]).astype(np.int64); fi = np.array(v)
    pon = np.zeros((N, 8, I), bool); pv = np.zeros((N, 8, I), np.int64); pf = np.zeros((N, 8, I), np.int64); lane = np.arange(I)
    for t in range(RO):
        for step in range(MV + 1):
            hi = above(q, pick(kb, v)); b = above(q, pick(ka, v)); g = pick(gr, v); c = np.where(b, pick(cb, v), pick(ca, v)); leaf = (v >= H) & (v < Z)
            if step == MV: break
            right = hi & (g >= 0); down = ~right & ~leaf
            fi = np.where(down, v, fi); v = np.where(right, g, np.where(down, c, v))
        done = leaf & ~hi; over = hi & (g < 0)
        if t > 0:
            m = pick(kb, pv); gu = pick(gr, pf); u = np.where(above(m, pick(kb, pf)) & (gu >= 0), gu, pf)
            cu = np.where(above(m, pick(ka, u)), pick(cb, u), pick(ca, u)); ok = pon & (cu == pv)
            insert(ka, kb, ca, cb, gr, lowest(ok, u), u, m, pv, np.broadcast_to(V + I * (t - 1) + lane, pv.shape), Z + I * (t - 1) + lane)
        pv = np.array(v[:, :, :I]); pf = np.array(fi[:, :, :I]); pon = lowest(done[:, :, :I], pv)
        insert(ka, kb, ca, cb, gr, pon, pv, q[..., :I], c[:, :, :I], c[:, :, :I], V + I * t + lane)
        q = np.where(done[:, :, None, :], (q + pick(it, np.where(done, c, 0)) + t) & 15, q).astype(np.int16); v = np.where(done, fi, v)
        before = np.add.accumulate(over.astype(np.int64), axis=2) - over
        a, e, l = np.nonzero(over & (before < CAP)); s = before[a, e, l]
        box = np.zeros((N, 8, 16, CAP), np.int16); have = np.zeros((N, 8, CAP), bool); box[a, e, :, s] = q[a, e, :, l]; have[a, e, s] = True
        src = (a - 1) % N; nq = np.where(have[src, e, s][:, None], box[src, e, :, s], q[a, e, :, l])
        q[a, e, :, l] = nq; st = np.sum(nq.astype(np.int64) * wg[a, e], axis=1) & (H - 1); v[a, e, l] = st; fi[a, e, l] = st
    return {"yk": (ka + 16 * kb).reshape(N, 128, W).astype(np.float32).astype(BF), "y0": ca.astype(np.float32), "y1": cb.astype(np.float32), "yr": gr.astype(np.float32),
            "yq": q.reshape(N, 128, L).astype(np.float32).astype(BF)}

@@ -1,0 +1,748 @@
+from concourse.mybir import AluOpType, ActivationFunctionType
+
+AL = AluOpType
+AF = ActivationFunctionType
+BF, F32, I32, U16 = "bfloat16", "float32", "int32", "uint16"
+V, H, I, L, R = 3072, 1024, 256, 2560, 1024
+W = 3840
+HL = 1280
+N1 = 896
+CR = 1.5 * 2.0 ** 35
+OFS = 1792.0
+HB = 2064.0
+rA, rC1, rR, rS, rC0, rK, rLF, rO1, rO2, rNO = 0, 2, 4, 6, 8, 10, 11, 12, 13, 14
+
+SB = {
+    "kt": ([128, 4096], BF), "tt": ([128, 4096], F32), "pt": ([128, 4096], F32), "hh": ([128, V], BF),
+    "rct": ([128, 1040], BF), "qa": ([128, 2832], BF), "qb": ([128, 2832], BF), "qq": ([128, L], F32),
+    "rb": ([128, L], BF), "b1": ([128, L], BF), "gp": ([128, L], BF),
+    "cx": ([128, 576], I32), "chi": ([128, 960], BF), "cf": ([128, 192 * 15], F32), "ci": ([128, 192], I32),
+    "v0i": ([128, 160], I32), "wti": ([128, 4], I32), "wcol": ([128, 8], F32), "wcb": ([128, 8], BF),
+    "off": ([128, 160], U16), "idx": ([128, 160], U16),
+    "lc": ([128, 256], BF), "xt": ([128, 256], F32), "ht": ([128, 256], BF), "ft": ([128, 256], F32), "ot": ([128, 256], BF),
+    "hs": ([128, 512], F32),
+    "ones": ([128, 256], BF), "idb": ([128, 128], BF), "idf": ([128, 128], F32), "ids": ([128, 128 * 11], BF),
+    "bd8": ([128, 8], BF), "bd": ([128, 128], BF), "bda": ([128, 128], BF), "bdb": ([128, 128], BF), "tri": ([128, 128], BF),
+    "z1": ([128, 144], BF), "z8": ([128, 144], BF), "zs": ([128, 144], BF), "zr": ([128, 144], BF),
+    "wm": ([128, 32], BF), "wl": ([128, 32], BF), "wr": ([128, 8], BF), "wb": ([128, 16], BF), "wq": ([128, 24], BF),
+    "mm": ([128, 128 * 19], BF), "tl": ([128, 128 * 15], BF), "eq": ([128, 4096], BF), "kw": ([128, 256], U16),
+    "pi": ([128, 4], I32), "pc": ([128, 16], F32), "sw": ([128, 256], BF),
+    "xb": ([128, 256], BF), "t1": ([128, 256], BF), "t2": ([128, 256], BF), "il": ([128, 64], F32),
+    "ovl": ([128, 160], BF), "inc": ([128, 176], BF), "incl": ([128, 176], F32), "junk": ([128, 256], BF),
+    "sm": ([128, 16 * 24], F32), "su": ([128, 16 * 8], U16),
+    "cmp": ([128, 256], BF), "box": ([128, 512], BF), "own": ([128, 256], BF), "rcv": ([128, 512], BF),
+    "nw": ([128, 256], BF), "nh": ([128, 256], BF),
+    "f32": ([128, 160], F32), "v32": ([128, 160], F32), "dn": ([128, 160], F32), "sl": ([128, 160], F32),
+    "la": ([128, 160], F32), "lb": ([128, 160], F32), "li": ([128, 160], I32),
+    "gz": ([128, 256], BF), "mk": ([128, 256], BF), "thm": ([128, 256], BF), "qm": ([128, 256], F32),
+    "cm3": ([128, 256], BF), "ge": ([128, 256], BF), "ru": ([128, 256], BF), "gu": ([128, 256], BF), "xbb": ([128, 256], BF),
+    "wz": ([128, 256], BF), "tn0": ([128, 256], F32),
+}
+for _k in (0, 1):
+    for _n, _d in (("kv", BF), ("hv", BF), ("hn", BF), ("h17", BF), ("k0", BF), ("bw", BF), ("gb", BF), ("nd", BF), ("dd", BF),
+                   ("kn", BF), ("pn", F32), ("ww", BF)):
+        SB["%s%d" % (_n, _k)] = ([128, 256], _d)
+SCRATCH = {k: ("sbuf", s, d) for k, (s, d) in SB.items()}
+for _k in range(8):
+    SCRATCH["ps%d" % _k] = ("psum", [128, 512], F32)
+SEMAPHORES = ["sv", "ss", "sp", "sg", "got0", "got1", "out0", "out1"] + ["d%d" % k for k in range(40)]
+
+GC, SC, PEC = 1.56, 3.8, 0.55
+VI = ((1, 3), (1, 3))
+TRIES, SEED, AMP = 150, 1, 1000.0
+_PLAN = {}
+
+
+def build(T, dst, msk):
+    ops = []
+    nd = [0]
+
+    def A(n, a=None, b=None, s=1, p0=0, p1=128, ps=1, tag=None):
+        if a is None:
+            a, b = 0, (SB[n][0][1] if n in SB else 512)
+        t = T[n]
+        rows = slice(p0, p1) if ps == 1 else slice(p0, p1, ps)
+        ap = t[rows, a:b] if s == 1 else t[rows, a:b:s]
+        reg = (n, 0, 512, None) if n not in SB else (n, a, b, tag)
+        return (ap, [reg], len(range(a, b, s)), SB[n][1] if n in SB else F32)
+
+    def IND(w, o):
+        return (w[0].indirect(o[0]), w[1] + o[1], o[2] * 16, w[3], "ind")
+
+    def op(eng, fns, rd, wr, cost, lat=0.0, sem=None, inc=1):
+        rr = [r for x in rd if isinstance(x, tuple) for r in x[1]]
+        ww = [r for x in wr for r in x[1]]
+        ops.append({"eng": eng, "fns": fns, "rd": rr, "wr": ww, "cost": cost, "lat": lat, "sem": sem, "inc": inc, "aft": []})
+
+    def val(x):
+        return x[0] if isinstance(x, tuple) else x
+
+    def vcost(out, ins, two=False):
+        if len(out) == 5:
+            return 60 + out[2] * SC
+        if len(ins[0]) == 5:
+            return 60 + out[2] * GC
+        f = 0.5 if all(x[3] in (BF, U16) for x in [out] + ins) else 1.0
+        if two and all(x[1][0][0] in SB for x in ins):
+            f *= 2
+        return 30 + max(64, out[2] * f)
+
+    def split(out):
+        if len(out) == 5:
+            return [(None, out[1][:1])], [(None, out[1][1:])]
+        return [out], []
+
+    def tt(out, a, b, o):
+        w, r = split(out)
+        op("v", [lambda e: e.tensor_tensor(out[0], a[0], b[0], o)], [a, b] + r, w, vcost(out, [a, b], True))
+
+    def ts(out, a, s1, o0, s2=None, o1=None):
+        if s2 is None:
+            f = lambda e: e.tensor_scalar(out[0], a[0], val(s1), None, o0)
+        else:
+            f = lambda e: e.tensor_scalar(out[0], a[0], val(s1), val(s2), o0, o1)
+        op("v", [f], [a, s1, s2], [out], vcost(out, [a]))
+
+    def cp(out, a):
+        w, r = split(out)
+        op("v", [lambda e: e.tensor_copy(out[0], a[0])], [a] + r, w, vcost(out, [a]))
+
+    def ms(out, c):
+        op("v", [lambda e: e.memset(out[0], c)], [], [out], 30 + max(64, out[2] * (0.5 if out[3] == BF else 1)))
+
+    def act(out, a, fn=AF.Identity, bias=0.0, scale=1.0, acc=None):
+        if acc is None:
+            f = lambda e: e.activation(out[0], a[0], fn, bias=val(bias), scale=val(scale))
+        else:
+            f = lambda e: e.activation(out[0], a[0], fn, bias=val(bias), scale=val(scale), accum_out=acc[0])
+        op("s", [f], [a, bias, scale], [out] + ([acc] if acc else []), 80 + out[2] * (GC if len(a) == 5 else 1.0))
+
+    def mmg(items, start=True, stop=True, each=False):
+        fns, rd, c = [], [], 0.0
+        for k, (o, l, r) in enumerate(items):
+            s, t = each or (start and k == 0), each or (stop and k == len(items) - 1)
+            fns.append(lambda e, o=o, l=l, r=r, s=s, t=t: e.matmul(o[0], l[0], r[0], s, t))
+            rd += [l, r]
+            c += 10 + PEC * max(min(64, l[2]), r[2]) * (4 if l[3] == F32 else 1)
+        op("p", fns, rd, [items[0][0]], c, lat=60)
+
+    def dma(q, out, a, nbytes):
+        s = "d%d" % nd[0]
+        nd[0] += 1
+        op(q, [lambda e: e.dma_start(out[0], a[0])], [a], [out], 60, lat=2000 + nbytes / 150.0, sem=s, inc=16)
+
+    def D(n, a=None, b=None):
+        return (T[n][:] if a is None else T[n][:, a:b], [(n + "_hbm", 0, 1, len(ops))], 0, None)
+
+    def iota(out, pat, base, cm):
+        if out[3] == I32:
+            f = lambda e: e.iota(out[0], pat, base, cm)
+        else:
+            f = lambda e: e.iota(out[0], pat, base, cm, allow_small_or_imprecise_dtypes=True)
+        op("g", [f], [], [out], 130 + 2 * out[2])
+
+    def sel(out, a, pat, cmpop, fill, base, cm):
+        op("g", [lambda e: e.affine_select(out[0], a[0], pat, cmpop, fill, base, cm)], [a], [out], 170 + 2 * out[2])
+
+    def put(n, a, b, s, row, w, pat=None):
+        x = A(n, a, b, s)
+        sel(x, x, pat or [[-16, 8]], AL.not_equal, float(w), -row, 1)
+
+    for k in range(3):
+        dma("s", A("kt", 1024 * k, 1024 * k + 1024), D("kk", 1024 * k, 1024 * k + 1024), 300000 * (k + 1))
+    for k, n in enumerate(("c0", "c1", "rt")):
+        dma("y", A("cx", 192 * k, 192 * k + 192), D(n), 98304)
+    dma("y", A("v0i"), D("v0"), 81920)
+    dma("y", A("qa", 0, HL), D("qs", 0, HL), 700000)
+    dma("y", A("qa", HL, L), D("qs", HL, L), 1000000)
+    dma("y", A("wti", 0, 1), D("wt"), 512)
+
+    ms(A("ones"), 1.0)
+    ms(A("pt", 0, 2048), 1.0)
+    for n in ("wm", "wl", "z1"):
+        ms(A(n), 0.0)
+    sel(A("bd8"), A("ones", 0, 8), [[-16, 8]], AL.is_ge, 0.0, 0, 1)
+    sel(A("bd8"), A("bd8"), [[16, 8]], AL.is_ge, 0.0, 15, -1)
+    iota(A("pi", 0, 1), [[0, 1]], 0, 1)
+    iota(A("ci"), [[1, 192]], 0, 192)
+    iota(A("pt", 2048, V), [[0, 1024]], 1, 0)
+    sel(A("idb"), A("ones", 0, 128), [[-1, 128]], AL.is_equal, 0.0, 0, 1)
+    ts(A("pi", 1, 2), A("pi", 0, 1), 15, AL.bitwise_and)
+    ts(A("pi", 2, 3), A("pi", 0, 1), 1, AL.bitwise_and)
+    ts(A("pi", 3, 4), A("pi", 0, 1), 4, AL.logical_shift_right)
+    ROW, CP, TH, GO = A("pc", 0, 1), A("pc", 1, 2), A("pc", 2, 3), A("pc", 3, 4)
+    cp(ROW, A("pi", 1, 2))
+    ts(CP, A("pi", 2, 3), -6144.0, AL.mult, 3072.0 - HB - 7.5, AL.add)
+    ts(TH, A("pi", 2, 3), -6144.0, AL.mult, 3072.0 - 24.0, AL.add)
+    ts(GO, A("pi", 3, 4), -3072.0, AL.mult)
+    act(A("z1", 15, 143, 16), A("bd8"))
+    act(A("wr"), A("bd8"), scale=-512.0)
+    act(A("wb", 0, 8), A("bd8"), scale=2.0 ** 18)
+    act(A("wb", 8, 16), A("bd8"))
+    act(A("wq", 0, 8), A("bd8"))
+    act(A("idf"), A("idb"))
+    IDS = {}
+    for k, w in enumerate((-16384.0, -1.0, 4096.0, 8192.0, 12288.0, 16.0, -15.0, 32.0, -31.0, -8.0, -8192.0)):
+        IDS[w] = k
+        sel(A("ids", 128 * k, 128 * k + 128), A("idb"), [[-1, 128]], AL.not_equal, w, 0, 1)
+
+    def ID(w, n=128):
+        if w == 1:
+            return A("idb", 0, n, p1=n)
+        return A("ids", 128 * IDS[w], 128 * IDS[w] + n, p1=n)
+    put("wm", 0, 32, 1, 0, 1, [[-2, 4], [-16, 8]])
+    put("wm", 0, 32, 1, 1, 1, [[-2, 4], [-16, 8]])
+    put("wm", 0, 32, 1, rO2, -OFS, [[0, 4], [-16, 8]])
+    for w, r, x in ((0, rLF, 65536), (1, rK, 16384), (1, rO1, -69632), (2, rO1, -2 ** 17), (2, rNO, -2 ** 23), (3, rLF, -65536)):
+        put("wm", 8 * w, 8 * w + 8, 1, r, x)
+
+    def CF(k, n=1):
+        return A("cf", 192 * k, 192 * (k + n))
+
+    def row(r, src):
+        dma("y", A("pt", 0, V, p0=r, ps=16, tag=r), src, 400000)
+    ts(CF(6), A("ci"), GO, AL.add)
+    ts(CF(8), CF(6), 1023.5, AL.is_gt)
+    act(A("chi", 576, 768), CF(6))
+    act(CF(13), CF(8), bias=-8192.0, scale=8192.0)
+    act(CF(14), CF(8), scale=-8192.0)
+    tt(CF(13), CF(13), CF(6), AL.add)
+    tt(CF(7), CF(6), A("chi", 576, 768), AL.subtract)
+    row(rS, CF(6)); row(rS + 1, CF(7)); row(rLF, CF(8))
+    cp(CF(0, 3), A("cx"))
+    act(A("chi", 0, 576), CF(0, 3))
+    tt(CF(9), CF(0), CF(14), AL.add)
+    tt(CF(9), CF(9), CF(13), AL.max)
+    row(rC1, CF(1)); row(rR, CF(2)); row(rA, CF(9))
+    tt(CF(3, 3), CF(0, 3), A("chi", 0, 576), AL.subtract)
+    ts(CF(11), CF(2), -0.5, AL.is_lt)
+    act(A("chi", 768, 960), CF(9))
+    tt(CF(10), CF(9), A("chi", 768, 960), AL.subtract)
+    row(rC1 + 1, CF(4)); row(rR + 1, CF(5)); row(rA + 1, CF(10)); row(rNO, CF(11)); row(rC0, CF(0)); row(rC0 + 1, CF(3))
+    for k in range(3):
+        ts(A("hh", 1024 * k, 1024 * k + 1024), A("kt", 1024 * k, 1024 * k + 1024), HB - 7.5, AL.add)
+    for a, n, bank, c in ((0, 64, "ps4", 0), (1024, 128, "ps3", 64)):
+        mmg([(A(bank, 0, n), A("z1", 15 - s, 143 - s), A("hh", a + n * s, a + n * s + n)) for s in range(16)])
+        src = A("cf", 192 * 12 + c, 192 * 12 + c + n)
+        act(src, A(bank, 0, n), bias=-HB, scale=0.0625)
+        dma("s", A("pt", a, a + 16 * n, p0=rK, ps=16, tag=rK), src, 512 * n)
+    for k in range(6):
+        a = 512 * k
+        b = "ps%d" % (5 + k % 3)
+        mmg([(A(b), ID(1), A("kt", a, a + 512)), (A(b), ID(1), A("hh", a, a + 512))])
+        act(A("tt", a, a + 512), A(b))
+    cp(A("off"), A("v0i"))
+    ms(A("qa", L, L + 16), -16.0)
+    ms(A("qb", L, L + 16), -16.0)
+    ms(A("rct", R, R + 16), 0.0)
+
+    def sums(q, X, nw):
+        o = HL * X
+        for a, b in ((0, N1), (N1, HL)):
+            act(A("qq", o + a, o + b), A(q, o + a, o + b), bias=CP, scale=-33.0)
+        mmg([(A("ps%d" % X, j, 128 * nw, 16, p1=80), A(q, o + j, o + HL, 16), A("wq", 0, 8 * nw)) for j in range(16)], each=True)
+        act(A("lc", 128 * X, 128 * X + 128, p1=80), A("ps%d" % X, 0, 128, p1=80))
+    for X in (0, 1):
+        sums("qa", X, 1)
+
+    for n in ("z8", "zs", "zr", "mm"):
+        iota(A(n), [[0, SB[n][0][1]]], 0, 0)
+    put("wl", 0, 8, 1, rC0, 1); put("wl", 0, 8, 1, rC0 + 1, 1); put("wl", 8, 16, 1, rC1, 1); put("wl", 8, 16, 1, rC1 + 1, 1)
+    put("wl", 0, 16, 1, rO2, -OFS, [[0, 2], [-16, 8]])
+    for w, r, x in ((1, rK, 16384), (1, rO1, -69632), (2, rO1, 63 * 2 ** 17), (2, rO2, 1024 - OFS), (2, rLF, -2 ** 23), (3, rO1, -64.5), (3, rNO, 64)):
+        put("wl", 8 * w, 8 * w + 8, 1, r, x)
+    sel(A("bd"), A("ones", 0, 128), [[-16, 8], [0, 16]], AL.is_ge, 0.0, 0, 1)
+    sel(A("bd"), A("bd"), [[16, 8], [0, 16]], AL.is_ge, 0.0, 15, -1)
+    sel(A("tri"), A("bd"), [[1, 128]], AL.is_ge, 0.0, 0, -1)
+    iota(A("sw"), [[1, 256]], 0, 0)
+    for j in range(1, 16):
+        sel(A("tl", 128 * j - 128, 128 * j), A("bd"), [[16, 8], [0, 16]], AL.is_ge, 0.0, j - 1, -1)
+    iota(A("il", 48, 64), [[16, 16]], 0, 0)
+    MN = {"sum": 18}
+
+    def M(name):
+        return A("mm", 128 * MN[name], 128 * MN[name] + 128)
+
+    def me(name, *ent):
+        MN[name] = len(MN) - 1
+        b = 128 * MN[name]
+        for rin, rout, w in ent:
+            if rout is None:
+                put("mm", b, b + 128, 1, rin, w, [[-16, 8], [0, 16]])
+            else:
+                put("mm", b + rout, b + 128, 16, rin, w)
+    me("sk", (rK, None, 2))
+    me("lf", (rLF, None, -64))
+    me("sf", (rS, None, 1), (rS + 1, None, 1))
+    me("n1", *[(a, b, 1) for a, b in ((0, 0), (1, 0), (1, 1), (6, 6), (7, 6), (7, 7), (8, 8), (9, 8), (9, 9), (8, 2), (9, 2), (9, 3), (11, 11), (12, 12), (13, 13))])
+    me("n2", (2, 2, 1), (3, 2, 1), (8, 2, -1), (9, 2, -1), (3, 3, 1), (9, 3, -1))
+    me("x1", *[(a, b, 1) for a, b in ((2, 8), (3, 8), (3, 9), (2, 2), (3, 2), (3, 3), (4, 4), (5, 4), (5, 5), (10, 10), (14, 14))])
+    me("nx0", (0, 4, 1), (2, 4, V), (1, 5, 1))
+    me("xx0", (0, 0, 1), (2, 0, V), (1, 1, 1), (0, 6, 1), (2, 6, V), (1, 7, 1), (2, 11, 1), (2, 12, 1), (2, 13, 1))
+    me("nx1", (0, 4, 1), (2, 4, V + I))
+    me("c0", (8, None, 1), (9, None, 1))
+    me("cb", (2, None, 1), (3, None, 1), (8, None, -1), (9, None, -1))
+    me("zz", (6, None, -1), (7, None, -1))
+    me("p1", (8, 8, 1), (9, 8, 1))
+    me("p2", (2, 2, 1), (3, 2, 1))
+    me("p3", (0, 2, 1), (2, 2, V), (0, 4, 1), (2, 4, V + 2 * I))
+    me("p4", (0, 2, -1), (2, 2, -V))
+    me("q2", (2, 2, -1), (3, 2, -1), (2, 8, -1), (3, 8, -1))
+    me("q3", (0, 2, 1), (2, 2, V), (0, 8, 1), (2, 8, V))
+    for r, w in ((rR, 1), (rR + 1, 1), (rO1, -69632), (rO2, -OFS), (rNO, -2 ** 23)):
+        put("zr", 15, 143, 16, r, w)
+    act(A("mm", 128 * 18 + rK, 128 * 19, 16), A("bd8"))
+    act(A("bda"), A("bd"), scale=-0.0625)
+    act(A("bdb"), A("bd"), scale=-2.0)
+    act(A("z8", 15, 143, 16), A("bd8"), scale=8192.0)
+    act(A("zs", 15, 143, 16), A("bd8"), scale=0.0625)
+    act(A("il", 0, 16), A("il", 48, 64), bias=ROW)
+    act(A("il", 16, 32), A("il", 0, 16), bias=0.5)
+    act(A("il", 32, 48), A("il", 0, 16), bias=float(W))
+    act(A("il", 48, 64), A("il", 0, 16), bias=16.0)
+    ts(A("pc", 4, 5), ROW, 0.0, AL.is_equal)
+    ts(A("pc", 5, 6), ROW, 1.0, AL.is_equal)
+    ts(A("pc", 6, 7), ROW, 1.5, AL.is_gt)
+    act(A("t1"), A("sw"), bias=3072.0)
+    act(A("t2"), A("t1"), bias=-3072.0)
+    tt(A("t1"), A("sw"), A("t2"), AL.subtract)
+    act(A("t2"), A("t1"), scale=A("pc", 5, 6))
+    act(A("t1"), A("sw"), bias=A("pc", 6, 7), scale=A("pc", 4, 5))
+    tt(A("xb"), A("t1"), A("t2"), AL.add)
+    cp(A("wcol", 0, 1), A("wti", 0, 1))
+    act(A("wcb", 0, 1), A("wcol", 0, 1))
+    act(A("wcol", 2, 3), A("wcb", 0, 1))
+    act(A("wcol", 1, 2), A("wcb", 0, 1), bias=A("wcol", 0, 1), scale=-1.0)
+    act(A("wq", 8, 16), A("bd8"), scale=A("wcol", 2, 3))
+    act(A("wq", 16, 24), A("bd8"), scale=A("wcol", 1, 2))
+    ms(A("inc", 0, 1), 0.0)
+    ms(A("incl", 160, 176), 9999.0)
+    late = [len(ops)]
+    dma("y", A("rct", 0, R), D("rec"), 262144)
+
+    def step(t, k, X):
+        look = k == 4
+        fin = t == 0 and not look
+        o, c = HL * X, 80 * X
+        wd = 1024 if (t == 0 and k == 0) else (V if t == 0 else V + I)
+        ps, pl = "ps%d" % X, "ps%d" % (2 + X)
+        nw = 4 if (look or fin) else 3
+        mk = {}
+        for a, b in ((0, N1), (N1, HL)):
+            mk["g%d" % (a > 0)] = len(ops)
+            tt(A("rb", o + a, o + b), IND(A("tt", 0, wd), A("off", c + a // 16, c + b // 16)), A("qq", o + a, o + b), AL.add)
+        act(A("gp", o, o + HL), IND(A("pt", 0, wd), A("off", c, c + 80)))
+        act(A("b1", o, o + N1), A("rb", o, o + N1), AF.Sign, bias=TH, scale=-1.0)
+        mk["b"] = len(ops)
+        ts(A("b1", o + N1, o + HL), A("rb", o + N1, o + HL), TH, AL.is_lt, 0.5, AL.subtract)
+        wp = "wl" if look else "wm"
+        for h in (0, 8):
+            mmg([(A(ps, j, 128 * nw, 16, p1=80), A("gp", o + j, o + HL, 16), A(wp, 0, 8 * nw)) for j in range(h, h + 8)], h == 0, False)
+        more = [(A(ps, 128, 256, p1=80), ID(-16384.0, 80), A("lc", 128 * X, 128 * X + 128, p1=80))]
+        if fin and k > 0:
+            more.append((A(ps, 384, 512, p1=80), ID(4096.0 * k, 80), A("ones", 0, 128, p1=80)))
+        mmg(more, False, False)
+        for h in (0, 8):
+            mmg([(A(ps, 128 + j, 256, 16, p1=80), A("rb", o + j, o + HL, 16), A("wr")) for j in range(h, h + 8)], False, False)
+        nb = 2 if look else 1
+        for h in (0, 8):
+            mmg([(A(ps, 256 + j, 256 + 128 * nb, 16, p1=80), A("b1", o + j, o + HL, 16), A("wb", 0, 8 * nb)) for j in range(h, h + 8)], False, h == 8)
+        xt, ht = A("xt", 128 * X, 128 * X + 128, p1=80), A("ht", 128 * X, 128 * X + 128, p1=80)
+        mk["t0"] = len(ops)
+        cp(xt, A(ps, 0, 128, p1=80))
+        tt(xt, A(ps, 128, 256, p1=80), xt, AL.max)
+        tt(xt, A(ps, 256, 384, p1=80), xt, AL.max)
+        mk["t1"] = len(ops)
+        ts(ht, xt, CR, AL.add, CR, AL.subtract)
+        mmg([(A(pl, 0, 80), xt, A("idf", 0, 80, p1=80)), (A(pl, 0, 80), ht, ID(-1.0, 80))])
+        ft = A("ft", 128 * X, 128 * X + 128, p1=80)
+        if fin:
+            if k == 0:
+                cp(ft, A(ps, 384, 512, p1=80))
+            else:
+                tt(ft, A(ps, 384, 512, p1=80), ft, AL.max)
+        if look:
+            ot = A("ot", 128 * X, 128 * X + 128, p1=80)
+            ts(ot, A(ps, 384, 512, p1=80), 0.0, AL.is_gt)
+            ts(A("idx", c, c + 80), A(pl, 0, 80), OFS, AL.add)
+            mmg([(A(pl, 128, 208), ot, ID(1, 80))])
+            cp(A("ovl", c, c + 80), A(pl, 128, 208))
+        else:
+            mk["u"] = len(ops)
+            ts(A("off", c, c + 80), A(pl, 0, 80), OFS, AL.add)
+        return mk
+
+    def looks(t):
+        prev, last = None, None
+        for k in range(5):
+            for X in (0, 1):
+                m = step(t, k, X)
+                seq = [m["g0"]] + ([prev["t0"], prev["t1"]] if prev else []) + [m["g1"], m["b"]] + ([prev["u"]] if prev and "u" in prev else [])
+                for a in seq:
+                    if last is not None:
+                        ops[a]["aft"].append(last)
+                    last = a
+                prev = m
+                if len(late) == 1:
+                    late.append(m["g0"])
+
+    def SM(k, a=0, b=16):
+        return A("sm", 16 * k + a, 16 * k + b)
+
+    def SU(k):
+        return A("su", 16 * k, 16 * k + 16)
+
+    def tolist(bank, pairs):
+        mmg([(A(bank, 0, 16), A(z, 15 - j, 143 - j), A(src, j, 256, 16)) for z, src in pairs for j in range(16)])
+
+    def slots(t, q):
+        op("v", [lambda e: e.tensor_tensor_scan(T["inc"][:, 1:161], T["ones"][:, 0:160], T["ovl"][:, 0:160], 0.0, AL.mult, AL.add)],
+           [A("ones"), A("ovl")], [A("inc", 1, 161)], 110)
+        mmg([(A("ps4", 0, 160), A("bd"), A("inc", 1, 161))])
+        mmg([(A("ps5", 0, 160), A("tri"), A("ovl")), (A("ps5", 0, 160), A("bd"), A("inc", 0, 160))])
+        cp(A("incl", 0, 160), A("ps5", 0, 160))
+        for c in range(16):
+            act(A("junk", 0, 160) if c % 2 else A("cmp", 0, 160), A("ps4", 0, 160), AF.Sign, bias=A("il", 16 + c, 17 + c), scale=-1.0, acc=SM(0, c, c + 1))
+        ts(SU(0), SM(0), 0.5, AL.mult, 80.0, AL.add)
+        ts(SM(1), SM(0), 8.0, AL.mult, 1280.0, AL.add)
+        tt(A("cmp"), IND(A("incl"), SU(0)), A("sw"), AL.is_le)
+        tolist("ps5", [("z1", "cmp")])
+        tt(SM(2), A("ps5", 0, 16), SM(1), AL.add)
+        cp(SU(1), SM(2))
+        bx = A("box", 256 * t, 256 * t + 256)
+        ts(bx, IND(A(q, 0, L + 16), SU(1)), 16.0, AL.add)
+        rc = A("rcv", 256 * t, 256 * t + 256)
+        op("g", [lambda e: e.remote_dma(rc[0], bx[0], T.sem["got%d" % t], T.sem["out%d" % t], dst[1], dst[0], msk[0])],
+           [bx], [(None, [("wire%d" % t, 0, 1, None)])], 500, lat=4000, sem="remote%d" % t, inc=len(msk[1]))
+        ts(A("own"), bx, -16.0, AL.add)
+        ts(SM(3), SM(2), L - 0.5, AL.is_gt)
+        tt(SM(3), SM(3), A("il", 48, 64), AL.mult)
+        tt(SM(3), SM(3), SM(2), AL.add)
+        cp(SU(2), SM(3))
+
+    def arrive(t, qn):
+        rc = (T["rcv"][:, 256 * t:256 * t + 256], [("wire%d" % t, 0, 1, None)], 256, BF)
+        op("v", [lambda e: e.tensor_tensor(T["nw"][:, 0:256], rc[0], T["own"][:, 0:256], AL.max)], [rc, A("own")], [A("nw")], 286)
+        ts(A("nh"), A("nw"), 15.5, AL.is_gt, -16.0, AL.mult)
+        tt(IND(A(qn), SU(2)), A("nw"), A("nh"), AL.add)
+
+    def items(t, q, qn):
+        for k in range(5):
+            a, b = 512 * k, 512 * k + 512
+            pa, pb = "ps%d" % (2 * (k % 2)), "ps%d" % (1 + 2 * (k % 2))
+            ix = IND(A("rct"), A("idx", a // 16, b // 16))
+            if k in VI[t]:
+                tt(A("hh", a, b), ix, A(q, a, b), AL.add)
+                ts(A("b1", a, b), A("hh", a, b), 15.5 - t, AL.is_gt, -16.0, AL.mult)
+                mmg([(A(pb), ID(1), A("hh", a, b)), (A(pb), ID(1), A("b1", a, b))])
+                act(A(qn, a, b), A(pb), bias=float(t))
+            else:
+                act(A("hh", a, b), ix)
+                two = lambda bank: [(A(bank), ID(1), A("hh", a, b)), (A(bank), ID(1), A(q, a, b))]
+                mmg(two(pa))
+                act(A("b1", a, b), A(pa), AF.Sign, bias=t - 15.5)
+                mmg(two(pb) + [(A(pb), ID(-8.0), A("b1", a, b))])
+                act(A(qn, a, b), A(pb), bias=t - 8.0)
+
+    def keys(s, ofs, wd):
+        z = str(s)
+        act(A("kv" + z), IND(A("kt", 0, wd), ofs))
+        act(A("hv" + z), A("kv" + z), bias=HB - 7.5)
+        act(A("hn" + z), A("hv" + z), bias=-HB)
+        act(A("h17" + z), A("hn" + z), scale=1.0625)
+        tt(A("k0" + z), A("kv" + z), A("hn" + z), AL.subtract)
+
+    def branch(s, bank, r, gp, m):
+        z = str(s)
+        mmg([(A(bank, 0, 256), A("bda"), r), (A(bank, 0, 256), M("sk"), gp), (A(bank, 0, 256), A("bdb"), m)])
+        ts(A("bw" + z), A(bank, 0, 256), 8.5, AL.is_gt)
+        tt(A("gb" + z), gp, A("bw" + z), AL.mult)
+        mmg([(A(bank, 256, 512), ID(1), A("k0" + z)), (A(bank, 256, 512), ID(-1.0), m)])
+        tt(A("dd" + z), A(bank, 256, 512), A("bw" + z), AL.mult)
+        mmg([(A(bank, 0, 256), ID(1), m), (A(bank, 0, 256), ID(16.0), A("k0" + z)), (A(bank, 0, 256), ID(-15.0), A("dd" + z))])
+        act(A("kn" + z), A(bank, 0, 256))
+
+    def lowest(s, bank, gp, n32, far, base):
+        z = str(s)
+        tt(SM(base), far, n32, AL.add)
+        mmg([(A(bank, 0, 256), M("sf"), gp)])
+        cp(A("kw"), A(bank, 0, 256))
+        mmg([(A(bank, 256, 512), ID(1), A("nd" + z))], True, False)
+        for c in range(16):
+            ts(A("eq", 256 * c, 256 * c + 256 - 16 * c), A("kw", 16 * c, 256), SM(base, c, c + 1), AL.is_equal)
+            if c < 15:
+                mmg([(A(bank, 272 + 16 * c, 512), A("bd"), A("eq", 256 * c + 16, 256 * c + 256 - 16 * c))], False, False)
+        mmg([(A(bank, 256 + j, 512, 16), A("tl", 128 * j - 128, 128 * j), A("eq", j, 4096, 256)) for j in range(1, 16)], False, True)
+        act(A("ww" + z), A(bank, 256, 512), AF.Relu, bias=1.0, scale=-1.0)
+        tt(SM(base + 1), n32, A("il", 32, 48), AL.subtract)
+        tolist(bank, [("zs", "ww" + z)])
+        tt(SM(base + 2), A(bank, 0, 16), SM(base + 1), AL.mult)
+        tt(SM(base + 2), SM(base + 2), A("il", 32, 48), AL.add)
+        cp(SU(3 + s), SM(base + 2))
+
+    def insert_pre(t, q):
+        G, Q = A("gp", 0, 256), A(q, 0, 256)
+        mmg([(A("ps7", 0, 256), A("bd"), A("b1", 0, 256)), (A("ps7", 0, 256), M("lf"), G)])
+        ts(A("nd0"), A("ps7", 0, 256), -63.5, AL.is_gt)
+        cp(SM(5), A("off", 0, 16))
+        ts(SM(6), A("idx", 0, 16), 1023.5, AL.is_gt, 8192.0, AL.mult)
+        keys(0, A("off", 0, 16), V + I * t)
+        branch(0, "ps6", A("rb", 0, 256), G, Q)
+        if t == 0:
+            act(A("gz"), G)
+
+    def insert_post(t, q):
+        G, Q = A("gp", 0, 256), A(q, 0, 256)
+        x = V + I * t
+        lo, hi = A("ps6", 0, 256), A("ps6", 256, 512)
+        lowest(0, "ps7", G, SM(5), SM(6), 7)
+        if t == 0:
+            mmg([(hi, ID(1), Q), (hi, ID(32.0), A("k00")), (hi, ID(-31.0), A("dd0"))])
+            act(A("tn0"), hi, bias=HB)
+            tt(A("mk"), A("k00"), A("dd0"), AL.subtract)
+        mmg([(lo, M("n1"), G), (lo, M("n2"), A("gb0")), (lo, M("nx%d" % t), A("xb"))] + ([(lo, M("sum"), A("mk"))] if t == 0 else []))
+        act(A("pn0"), lo)
+        mmg([(hi, M("x1"), G)] + ([(hi, M("xx0"), A("xb"))] if t == 0 else []))
+        if t == 0:
+            cp(IND(A("tt"), SU(3)), A("tn0"))
+            act(A("tt", x, x + I), A("hn0"), bias=HB, scale=2.0625)
+        cp(IND(A("pt"), SU(3)), A("pn0"))
+        tt(A("pt", x, x + I), hi, A("ww0"), AL.mult)
+        cp(IND(A("kt"), SU(3)), A("kn0"))
+        tt(A("kt", x, x + I), A("h170"), A("ww0"), AL.mult)
+        if t == 0:
+            act(A("wz"), A("ww0"))
+
+    def post_pre():
+        ts(A("thm"), A("mk"), 32.0, AL.mult, HB, AL.add)
+        act(A("qm"), A("mk"), bias=CP, scale=-33.0)
+        cp(SU(5), A("f32", 0, 16))
+        ts(SM(12), A("f32", 0, 16), -OFS, AL.add)
+        tt(A("cm3"), IND(A("tt", 0, V + I), SU(5)), A("thm"), AL.is_lt)
+        act(A("ge"), IND(A("pt", 0, V + I), SU(5)))
+        tolist("ps5", [("z8", "cm3"), ("zr", "ge")])
+        tt(SM(13), A("ps5", 0, 16), SM(12), AL.max)
+        ts(SM(14), SM(13), CR, AL.add, CR, AL.subtract)
+        tt(SM(13), SM(13), SM(14), AL.subtract)
+        ts(SU(6), SM(13), OFS, AL.add)
+        ts(SM(15), SM(13), OFS, AL.add)
+        tt(A("ru"), IND(A("tt", 0, V + I), SU(6)), A("qm"), AL.add)
+        act(A("gu"), IND(A("pt", 0, V + I), SU(6)))
+        keys(1, SU(6), V + I)
+        branch(1, "ps4", A("ru"), A("gu"), A("mk"))
+        lo, hi = A("ps5", 0, 256), A("ps4", 256, 512)
+        mmg([(lo, M("c0"), A("gu")), (lo, M("cb"), A("gb1")), (lo, M("zz"), A("gz")), (lo, ID(-8192.0), A("wz"))])
+        ts(A("nd1"), lo, -8192.0, AL.not_equal)
+        tolist("ps4", [("z8", "nd1")])
+        lowest(1, "ps5", A("gu"), SM(15), A("ps4", 0, 16), 17)
+        tt(A("xbb"), A("xb"), A("bw1"), AL.mult)
+        lo = A("ps4", 0, 256)
+        mmg([(lo, M("p1"), A("gu")), (lo, M("p2"), A("gb1")), (lo, M("p3"), A("xb")), (lo, M("p4"), A("xbb"))])
+        act(A("pn1"), lo)
+        mmg([(hi, M("x1"), A("gu")), (hi, M("q2"), A("gb1")), (hi, M("q3"), A("xbb"))])
+        x = V + 2 * I
+        tt(A("pt", x, x + I), hi, A("ww1"), AL.mult)
+        tt(A("kt", x, x + I), A("h171"), A("ww1"), AL.mult)
+        cp(IND(A("kt"), SU(4)), A("kn1"))
+
+    def restart_pre():
+        for X in (0, 1):
+            c = 80 * X
+            pl = "ps%d" % (2 + X)
+            ft, ht = A("ft", 128 * X, 128 * X + 128, p1=80), A("ht", 128 * X, 128 * X + 128, p1=80)
+            ts(ht, ft, CR, AL.add, CR, AL.subtract)
+            mmg([(A(pl, 0, 80), ft, A("idf", 0, 80, p1=80)), (A(pl, 0, 80), ht, ID(-1.0, 80))])
+            act(A("f32", c, c + 80), A(pl, 0, 80), bias=OFS)
+        cp(A("v32"), A("off"))
+        ts(A("dn"), A("idx"), 1023.5, AL.is_lt)
+        tt(A("la"), A("f32"), A("v32"), AL.subtract)
+        tt(A("la"), A("la"), A("dn"), AL.mult)
+        tt(A("la"), A("la"), A("v32"), AL.add)
+        ts(A("sl"), A("incl", 0, 160), 256.5, AL.is_lt)
+        tt(A("sl"), A("sl"), A("ovl"), AL.mult)
+        act(A("dn"), A("sl"), bias=1.0, scale=-1.0)
+        tt(A("la"), A("la"), A("dn"), AL.mult)
+
+    def restart():
+        for X in (0, 1):
+            c = 80 * X
+            pl = "ps%d" % (2 + X)
+            sums("qb", X, 3)
+            act(A("hs", 256 * X, 256 * X + 256, p1=80), A("ps%d" % X, 128, 384, p1=80))
+            mmg([(A(pl, 0, 80), A("hs", 256 * X + 128 * u, 256 * X + 128 * u + 128, p1=80), A("idf", 0, 80, p1=80)) for u in (0, 1)])
+            cp(A("li", c, c + 80), A(pl, 0, 80))
+            ts(A("li", c, c + 80), A("li", c, c + 80), H - 1, AL.bitwise_and)
+            tt(A("lb", c, c + 80), A("li", c, c + 80), A("sl", c, c + 80), AL.mult)
+            tt(A("lb", c, c + 80), A("lb", c, c + 80), A("la", c, c + 80), AL.add)
+            cp(A("off", c, c + 80), A("lb", c, c + 80))
+
+    looks(0)
+    ops[late[0]]["aft"].append(late[1])
+    insert_pre(0, "qa")
+    slots(0, "qa")
+    insert_post(0, "qa")
+    restart_pre()
+    items(0, "qa", "qb")
+    ms(A("rct", R, R + 16), -1.0)
+    post_pre()
+    arrive(0, "qb")
+    restart()
+    looks(1)
+    insert_pre(1, "qb")
+    slots(1, "qb")
+    cp(IND(A("pt"), SU(4)), A("pn1"))
+    insert_post(1, "qb")
+    items(1, "qb", "qa")
+    arrive(1, "qa")
+    dma("y", D("yk", 0, 1920), A("kt", 0, 1920), 500000)
+    dma("s", D("yk", 1920, W), A("kt", 1920, W), 500000)
+    for n, r in (("y0", rC0), ("y1", rC1), ("yr", rR)):
+        dma("y", D(n), A("pt", 0, W, p0=r, ps=16), 122880)
+    dma("y", D("yq", 0, HL), A("qa", 0, HL), 330000)
+    dma("s", D("yq", HL, L), A("qa", HL, L), 330000)
+    return ops
+
+
+def depend(ops):
+    last = {}
+    deps = []
+    for k, o in enumerate(ops):
+        d = set()
+        for rs, w in ((o["rd"], False), (o["wr"], True)):
+            for (n, a, b, tag) in rs:
+                ps = n.startswith("ps")
+                for (k2, a2, b2, tag2, w2) in last.get(n, []):
+                    if a < b2 and a2 < b and (tag is None or tag2 is None or tag == tag2):
+                        if w or w2 or (ps and ops[k2]["eng"] != o["eng"]):
+                            d.add(k2)
+        for rs, w in ((o["rd"], False), (o["wr"], True)):
+            for (n, a, b, tag) in rs:
+                ent = last.setdefault(n, [])
+                if w and tag is None:
+                    ent[:] = [e for e in ent if not (a <= e[1] and e[2] <= b)]
+                ent.append((k, a, b, tag, w))
+        d.discard(k)
+        deps.append(sorted(d))
+    return deps
+
+
+def place(ops, pred, gap, key):
+    n = len(ops)
+    succ = [[] for _ in ops]
+    for k, d in enumerate(pred):
+        for j in d:
+            succ[j].append(k)
+    left = [len(d) for d in pred]
+    ready = [k for k in range(n) if left[k] == 0]
+    start = [0.0] * n
+    busy = {}
+    while ready:
+        k = min(ready, key=lambda j: key[j])
+        ready.remove(k)
+        s = max([start[j] + gap(j, k) for j in pred[k]] + [gap(None, k)])
+        c = ops[k]["cost"]
+        line = busy.setdefault(ops[k]["eng"], [])
+        at = len(line)
+        while at > 0 and line[at - 1][1] > s:
+            at -= 1
+        while at < len(line) and line[at][0] < s + c:
+            s = max(s, line[at][1])
+            at += 1
+        line.insert(at, (s, s + c))
+        start[k] = s
+        for j in succ[k]:
+            left[j] -= 1
+            if left[j] == 0:
+                ready.append(j)
+    return start
+
+
+def order(ops, deps):
+    n = len(ops)
+    pred = [sorted(set(d) | set(o["aft"])) for d, o in zip(deps, ops)]
+    succ = [[] for _ in ops]
+    for k, d in enumerate(pred):
+        for j in d:
+            succ[j].append(k)
+
+    def lag(j, k):
+        a, b = ops[j], ops[k]
+        if j not in deps[k]:
+            return 0.0
+        if a["eng"] == b["eng"] and a["sem"] is None:
+            return 0.0 if a["eng"] == "p" else 30.0
+        return a["lat"] + 100.0
+
+    def fw(j, k):
+        return 0.0 if j is None else ops[j]["cost"] + lag(j, k)
+
+    def bw(j, k):
+        return ops[k]["lat"] if j is None else ops[j]["cost"] + lag(k, j)
+    pr = place([dict(o, eng=k) for k, o in enumerate(ops)], succ, bw, [0.0] * n)
+    key = [-(pr[k] + ops[k]["cost"]) for k in range(n)]
+    best, state = None, SEED
+    for _ in range(TRIES):
+        st = place(ops, pred, fw, key)
+        back = place(ops, succ, bw, [-(st[k] + ops[k]["cost"] + ops[k]["lat"]) for k in range(n)])
+        st = place(ops, pred, fw, [-(back[k] + ops[k]["cost"]) for k in range(n)])
+        end = max(st[k] + ops[k]["cost"] + ops[k]["lat"] for k in range(n))
+        if best is None or end <= best[1]:
+            best = (st, end)
+        state = (state * 1103515245 + 12345) % 2147483648
+        mid, amp = best[1] * (state >> 8) / 8388608.0, AMP * (1 + (state >> 4) % 4)
+        key = []
+        for k in range(n):
+            state = (state * 1103515245 + 12345) % 2147483648
+            key.append(best[0][k] + (amp * (state >> 8) / 8388608.0 if abs(best[0][k] - mid) < 12000.0 else 0.0))
+    return sorted([(k, best[0][k]) for k in range(n)], key=lambda x: x[1]), best[1]
+
+
+def rank_program(g, core, T, topo):
+    rank = T.rank_of(core)
+    if rank is None:
+        return
+    cores = list(T.cores)
+    nxt, prv = cores[(rank + 1) % len(cores)], cores[(rank - 1) % len(cores)]
+    rid, pid, _ = topo.addr(nxt)
+    ops = build(T, (rid, pid), (topo.mask(core, nxt), topo.engines(core, nxt)))
+    nin = len(topo.engines(prv, core))
+    if "seq" not in _PLAN:
+        _PLAN["deps"] = depend(ops)
+        _PLAN["seq"], _PLAN["end"] = order(ops, _PLAN["deps"])
+    deps = _PLAN["deps"]
+    eng = {"v": g.vector, "s": g.scalar, "p": g.tensor, "g": g, "y": g.sync}
+    own = {"v": "sv", "s": "ss", "p": "sp", "g": "sg"}
+    count, mark, clock = {}, {}, {}
+    known = {e: {} for e in eng}
+    for k, _s in _PLAN["seq"]:
+        o = ops[k]
+        e = o["eng"]
+        kn = known[e]
+        for j in sorted(deps[k], key=lambda j: -mark[j][2]):
+            if e == "p" and ops[j]["eng"] == "p":
+                continue
+            sem, v, _t = mark[j]
+            if kn.get(sem, 0) < v:
+                eng[e].wait_ge(T.sem[sem], v)
+                kn[sem] = v
+                for s2, v2 in clock[j].items():
+                    if kn.get(s2, 0) < v2:
+                        kn[s2] = v2
+        sem = o["sem"]
+        if sem is not None and sem.startswith("remote"):
+            o["fns"][0](eng[e])
+            t = sem[6:]
+            count["out" + t] = o["inc"]
+            count["got" + t] = nin
+            mark[k] = ("got" + t, nin, len(mark))
+            clock[k] = {}
+            continue
+        sem = sem or own[e]
+        for f in o["fns"]:
+            f(eng[e]).then_inc(T.sem[sem], o["inc"])
+            count[sem] = count.get(sem, 0) + o["inc"]
+        mark[k] = (sem, count[sem], len(mark))
+        clock[k] = dict(kn)
+    for sem in sorted(count):
+        if known["g"].get(sem, 0) < count[sem] or sem in own.values():
+            g.wait_ge(T.sem[sem], count[sem])

@@ -19,12 +19,12 @@ SB = {
     "cx": ([128, 576], I32), "chi": ([128, 960], BF), "cf": ([128, 192 * 15], F32), "ci": ([128, 192], I32),
     "v0i": ([128, 160], I32), "wti": ([128, 4], I32), "wcol": ([128, 8], F32), "wcb": ([128, 8], BF),
     "off": ([128, 160], U16), "idx": ([128, 160], U16),
-    "lc": ([128, 256], BF), "xt": ([128, 256], F32), "ht": ([128, 256], BF), "ft": ([128, 256], F32), "ot": ([128, 256], BF),
+    "lc": ([128, 256], F32), "xt": ([128, 256], F32), "ht": ([128, 256], BF), "ft": ([128, 256], F32), "ot": ([128, 256], BF),
     "hs": ([128, 512], F32),
-    "ones": ([128, 256], BF), "idb": ([128, 128], BF), "idf": ([128, 128], F32), "ids": ([128, 128 * 11], BF),
+    "ones": ([128, 256], BF), "idb": ([128, 128], BF), "idf": ([128, 128], F32), "ids": ([128, 128 * 7], BF),
     "bd8": ([128, 8], BF), "bd": ([128, 128], BF), "bda": ([128, 128], BF), "bdb": ([128, 128], BF), "tri": ([128, 128], BF),
     "z1": ([128, 144], BF), "z8": ([128, 144], BF), "zs": ([128, 144], BF), "zr": ([128, 144], BF),
-    "wm": ([128, 32], BF), "wl": ([128, 32], BF), "wr": ([128, 8], BF), "wb": ([128, 16], BF), "wq": ([128, 24], BF),
+    "wm": ([128, 128], BF), "wl": ([128, 32], BF), "wr": ([128, 8], BF), "wb": ([128, 16], BF), "wq": ([128, 24], BF),
     "mm": ([128, 128 * 19], BF), "tl": ([128, 128 * 15], BF), "eq": ([128, 4096], BF), "kw": ([128, 256], U16),
     "pi": ([128, 4], I32), "pc": ([128, 16], F32), "sw": ([128, 256], BF),
     "xb": ([128, 256], BF), "t1": ([128, 256], BF), "t2": ([128, 256], BF), "il": ([128, 64], F32),
@@ -47,9 +47,9 @@ for _k in range(8):
     SCRATCH["ps%d" % _k] = ("psum", [128, 512], F32)
 SEMAPHORES = ["sv", "ss", "sp", "sg", "got0", "got1", "out0", "out1"] + ["d%d" % k for k in range(40)]
 
-GC, SC, PEC = 1.56, 3.8, 0.55
-VI = ((1, 3), (1, 3))
-TRIES, SEED, AMP = 150, 1, 1000.0
+GC, SC, PEC = 1.7, 3.8, 0.6
+VI = (0, 1, 0, 1, 0)
+TRIES, SEED, AMP = 200, 1, 1500.0
 _PLAN = {}
 
 
@@ -81,11 +81,11 @@ def build(T, dst, msk):
         if len(out) == 5:
             return 60 + out[2] * SC
         if len(ins[0]) == 5:
-            return 60 + out[2] * GC
+            return 60 + out[2] * (max(GC, 2.0) if two else GC)
         f = 0.5 if all(x[3] in (BF, U16) for x in [out] + ins) else 1.0
         if two and all(x[1][0][0] in SB for x in ins):
-            f *= 2
-        return 30 + max(64, out[2] * f)
+            f = 2.0
+        return 60 + max(64, out[2] * f)
 
     def split(out):
         if len(out) == 5:
@@ -108,7 +108,7 @@ def build(T, dst, msk):
         op("v", [lambda e: e.tensor_copy(out[0], a[0])], [a] + r, w, vcost(out, [a]))
 
     def ms(out, c):
-        op("v", [lambda e: e.memset(out[0], c)], [], [out], 30 + max(64, out[2] * (0.5 if out[3] == BF else 1)))
+        op("v", [lambda e: e.memset(out[0], c)], [], [out], 60 + max(64, out[2] * (0.5 if out[3] == BF else 1)))
 
     def act(out, a, fn=AF.Identity, bias=0.0, scale=1.0, acc=None):
         if acc is None:
@@ -123,7 +123,7 @@ def build(T, dst, msk):
             s, t = each or (start and k == 0), each or (stop and k == len(items) - 1)
             fns.append(lambda e, o=o, l=l, r=r, s=s, t=t: e.matmul(o[0], l[0], r[0], s, t))
             rd += [l, r]
-            c += 10 + PEC * max(min(64, l[2]), r[2]) * (4 if l[3] == F32 else 1)
+            c += 2 + PEC * max(min(64, l[2]), r[2]) * (4 if l[3] == F32 else 1)
         op("p", fns, rd, [items[0][0]], c, lat=60)
 
     def dma(q, out, a, nbytes):
@@ -160,7 +160,7 @@ def build(T, dst, msk):
     ms(A("ones"), 1.0)
     ms(A("pt", 0, 2048), 1.0)
     for n in ("wm", "wl", "z1"):
-        ms(A(n), 0.0)
+        ms(A(n, 0, 144 if n == "z1" else 32), 0.0)
     sel(A("bd8"), A("ones", 0, 8), [[-16, 8]], AL.is_ge, 0.0, 0, 1)
     sel(A("bd8"), A("bd8"), [[16, 8]], AL.is_ge, 0.0, 15, -1)
     iota(A("pi", 0, 1), [[0, 1]], 0, 1)
@@ -182,7 +182,7 @@ def build(T, dst, msk):
     act(A("wq", 0, 8), A("bd8"))
     act(A("idf"), A("idb"))
     IDS = {}
-    for k, w in enumerate((-16384.0, -1.0, 4096.0, 8192.0, 12288.0, 16.0, -15.0, 32.0, -31.0, -8.0, -8192.0)):
+    for k, w in enumerate((-1.0, 16.0, -15.0, 32.0, -31.0, -8192.0, -8.0)):
         IDS[w] = k
         sel(A("ids", 128 * k, 128 * k + 128), A("idb"), [[-1, 128]], AL.not_equal, w, 0, 1)
 
@@ -195,6 +195,9 @@ def build(T, dst, msk):
     put("wm", 0, 32, 1, rO2, -OFS, [[0, 4], [-16, 8]])
     for w, r, x in ((0, rLF, 65536), (1, rK, 16384), (1, rO1, -69632), (2, rO1, -2 ** 17), (2, rNO, -2 ** 23), (3, rLF, -65536)):
         put("wm", 8 * w, 8 * w + 8, 1, r, x)
+    for k in (1, 2, 3):
+        act(A("wm", 32 * k, 32 * k + 32), A("wm", 0, 32))
+        put("wm", 32 * k + 24, 32 * k + 32, 1, rO1, 4096 * k)
 
     def CF(k, n=1):
         return A("cf", 192 * k, 192 * (k + n))
@@ -241,7 +244,7 @@ def build(T, dst, msk):
         for a, b in ((0, N1), (N1, HL)):
             act(A("qq", o + a, o + b), A(q, o + a, o + b), bias=CP, scale=-33.0)
         mmg([(A("ps%d" % X, j, 128 * nw, 16, p1=80), A(q, o + j, o + HL, 16), A("wq", 0, 8 * nw)) for j in range(16)], each=True)
-        act(A("lc", 128 * X, 128 * X + 128, p1=80), A("ps%d" % X, 0, 128, p1=80))
+        act(A("lc", 128 * X, 128 * X + 128, p1=80), A("ps%d" % X, 0, 128, p1=80), scale=16384.0)
     for X in (0, 1):
         sums("qa", X, 1)
 
@@ -332,16 +335,11 @@ def build(T, dst, msk):
             mk["g%d" % (a > 0)] = len(ops)
             tt(A("rb", o + a, o + b), IND(A("tt", 0, wd), A("off", c + a // 16, c + b // 16)), A("qq", o + a, o + b), AL.add)
         act(A("gp", o, o + HL), IND(A("pt", 0, wd), A("off", c, c + 80)))
-        act(A("b1", o, o + N1), A("rb", o, o + N1), AF.Sign, bias=TH, scale=-1.0)
-        mk["b"] = len(ops)
-        ts(A("b1", o + N1, o + HL), A("rb", o + N1, o + HL), TH, AL.is_lt, 0.5, AL.subtract)
-        wp = "wl" if look else "wm"
+        for a, b in ((0, N1), (N1, HL)):
+            act(A("b1", o + a, o + b), A("rb", o + a, o + b), AF.Sign, bias=TH, scale=-1.0)
+        wp, w0 = ("wl", 0) if look else ("wm", 32 * k if fin else 0)
         for h in (0, 8):
-            mmg([(A(ps, j, 128 * nw, 16, p1=80), A("gp", o + j, o + HL, 16), A(wp, 0, 8 * nw)) for j in range(h, h + 8)], h == 0, False)
-        more = [(A(ps, 128, 256, p1=80), ID(-16384.0, 80), A("lc", 128 * X, 128 * X + 128, p1=80))]
-        if fin and k > 0:
-            more.append((A(ps, 384, 512, p1=80), ID(4096.0 * k, 80), A("ones", 0, 128, p1=80)))
-        mmg(more, False, False)
+            mmg([(A(ps, j, 128 * nw, 16, p1=80), A("gp", o + j, o + HL, 16), A(wp, w0, w0 + 8 * nw)) for j in range(h, h + 8)], h == 0, False)
         for h in (0, 8):
             mmg([(A(ps, 128 + j, 256, 16, p1=80), A("rb", o + j, o + HL, 16), A("wr")) for j in range(h, h + 8)], False, False)
         nb = 2 if look else 1
@@ -349,8 +347,8 @@ def build(T, dst, msk):
             mmg([(A(ps, 256 + j, 256 + 128 * nb, 16, p1=80), A("b1", o + j, o + HL, 16), A("wb", 0, 8 * nb)) for j in range(h, h + 8)], False, h == 8)
         xt, ht = A("xt", 128 * X, 128 * X + 128, p1=80), A("ht", 128 * X, 128 * X + 128, p1=80)
         mk["t0"] = len(ops)
-        cp(xt, A(ps, 0, 128, p1=80))
-        tt(xt, A(ps, 128, 256, p1=80), xt, AL.max)
+        tt(xt, A(ps, 128, 256, p1=80), A("lc", 128 * X, 128 * X + 128, p1=80), AL.subtract)
+        tt(xt, A(ps, 0, 128, p1=80), xt, AL.max)
         tt(xt, A(ps, 256, 384, p1=80), xt, AL.max)
         mk["t1"] = len(ops)
         ts(ht, xt, CR, AL.add, CR, AL.subtract)
@@ -377,7 +375,7 @@ def build(T, dst, msk):
         for k in range(5):
             for X in (0, 1):
                 m = step(t, k, X)
-                seq = [m["g0"]] + ([prev["t0"], prev["t1"]] if prev else []) + [m["g1"], m["b"]] + ([prev["u"]] if prev and "u" in prev else [])
+                seq = [m["g0"]] + ([prev["t0"], prev["t1"]] if prev else []) + [m["g1"]] + ([prev["u"]] if prev and "u" in prev else [])
                 for a in seq:
                     if last is not None:
                         ops[a]["aft"].append(last)
@@ -413,7 +411,7 @@ def build(T, dst, msk):
         ts(bx, IND(A(q, 0, L + 16), SU(1)), 16.0, AL.add)
         rc = A("rcv", 256 * t, 256 * t + 256)
         op("g", [lambda e: e.remote_dma(rc[0], bx[0], T.sem["got%d" % t], T.sem["out%d" % t], dst[1], dst[0], msk[0])],
-           [bx], [(None, [("wire%d" % t, 0, 1, None)])], 500, lat=4000, sem="remote%d" % t, inc=len(msk[1]))
+           [bx], [(None, [("wire%d" % t, 0, 1, None)])], 500, lat=6000 - 1500 * t, sem="remote%d" % t, inc=len(msk[1]))
         ts(A("own"), bx, -16.0, AL.add)
         ts(SM(3), SM(2), L - 0.5, AL.is_gt)
         tt(SM(3), SM(3), A("il", 48, 64), AL.mult)
@@ -422,7 +420,7 @@ def build(T, dst, msk):
 
     def arrive(t, qn):
         rc = (T["rcv"][:, 256 * t:256 * t + 256], [("wire%d" % t, 0, 1, None)], 256, BF)
-        op("v", [lambda e: e.tensor_tensor(T["nw"][:, 0:256], rc[0], T["own"][:, 0:256], AL.max)], [rc, A("own")], [A("nw")], 286)
+        op("v", [lambda e: e.tensor_tensor(T["nw"][:, 0:256], rc[0], T["own"][:, 0:256], AL.max)], [rc, A("own")], [A("nw")], 542)
         ts(A("nh"), A("nw"), 15.5, AL.is_gt, -16.0, AL.mult)
         tt(IND(A(qn), SU(2)), A("nw"), A("nh"), AL.add)
 
@@ -430,19 +428,12 @@ def build(T, dst, msk):
         for k in range(5):
             a, b = 512 * k, 512 * k + 512
             pa, pb = "ps%d" % (2 * (k % 2)), "ps%d" % (1 + 2 * (k % 2))
-            ix = IND(A("rct"), A("idx", a // 16, b // 16))
-            if k in VI[t]:
-                tt(A("hh", a, b), ix, A(q, a, b), AL.add)
-                ts(A("b1", a, b), A("hh", a, b), 15.5 - t, AL.is_gt, -16.0, AL.mult)
-                mmg([(A(pb), ID(1), A("hh", a, b)), (A(pb), ID(1), A("b1", a, b))])
-                act(A(qn, a, b), A(pb), bias=float(t))
-            else:
-                act(A("hh", a, b), ix)
-                two = lambda bank: [(A(bank), ID(1), A("hh", a, b)), (A(bank), ID(1), A(q, a, b))]
-                mmg(two(pa))
-                act(A("b1", a, b), A(pa), AF.Sign, bias=t - 15.5)
-                mmg(two(pb) + [(A(pb), ID(-8.0), A("b1", a, b))])
-                act(A(qn, a, b), A(pb), bias=t - 8.0)
+            (cp if VI[k] else act)(A("hh", a, b), IND(A("rct"), A("idx", a // 16, b // 16)))
+            two = lambda bank: [(A(bank), ID(1), A("hh", a, b)), (A(bank), ID(1), A(q, a, b))]
+            mmg(two(pa))
+            act(A("b1", a, b), A(pa), AF.Sign, bias=t - 15.5)
+            mmg(two(pb) + [(A(pb), ID(-8.0), A("b1", a, b))])
+            act(A(qn, a, b), A(pb), bias=t - 8.0)
 
     def keys(s, ofs, wd):
         z = str(s)
@@ -670,8 +661,8 @@ def order(ops, deps):
         if j not in deps[k]:
             return 0.0
         if a["eng"] == b["eng"] and a["sem"] is None:
-            return 0.0 if a["eng"] == "p" else 30.0
-        return a["lat"] + 100.0
+            return 0.0 if a["eng"] == "p" else 45.0
+        return a["lat"] + 140.0
 
     def fw(j, k):
         return 0.0 if j is None else ops[j]["cost"] + lag(j, k)

@@ -6,50 +6,66 @@ BF, F32, I32, U16 = "bfloat16", "float32", "int32", "uint16"
 V, H, I, L, R = 3072, 1024, 256, 2560, 1024
 W = 3840
 HL = 1280
-N1 = 896
-CR = 1.5 * 2.0 ** 35
-OFS = 1792.0
+CR = 1.5 * 2.0 ** 36
 HB = 2064.0
-rA, rC1, rR, rS, rC0, rK, rLF, rO1, rO2, rNO = 0, 2, 4, 6, 8, 10, 11, 12, 13, 14
+PH = 4128.0
+U2 = 2.0 ** 18
+SP = L + 16
+rA, rC, rK, rN, rL, rR, rS, rO, rP, rI = 0, 2, 4, 5, 6, 8, 10, 12, 13, 14
 
+N1, NG = 1024, 896
+VB = (896, 800)
+SLOT = ((1, "g0"), (1, "gpa"), (0, "rbm"), (0, "b1m"), (0, "relu"), (0, "max"), (0, "rnd"), (0, "ft"), (1, "gpb"), (1, "g1"),
+        (1, "gpm"), (0, "off"), (1, "bs"), (1, "bv"))
+LAST = ((1, "g0"), (1, "gpa"), (0, "rbm"), (0, "b1m"), (0, "relu"), (1, "gpb"), (0, "rnd"), (1, "g1"), (0, "off"), (1, "gpm"), (1, "bs"),
+        (1, "bv"), (1, "rbm"), (1, "b1m"))
+TLV = 8
+TTV = (2, 3, 4)
+BONUS = 8000.0
+POSTBY = (1, 2, 0)
+VI = ((0, 0, 0, 0, 0), (0, 0, 0, 0, 0))
+VH = ((2, 2, 2, 2, 2), (2, 2, 2, 0, 0))
+
+IDW = (1.0, -1.0, 8.0, 16.0, -16.0, -15.0, 120.0, -33.0, 264.0, 128.0, -8192.0, 1.0625)
 SB = {
     "kt": ([128, 4096], BF), "tt": ([128, 4096], F32), "pt": ([128, 4096], F32), "hh": ([128, V], BF),
-    "rct": ([128, 1040], BF), "qa": ([128, 2832], BF), "qb": ([128, 2832], BF), "qq": ([128, L], F32),
+    "rct": ([128, 1040], BF), "qa": ([128, 2832], BF), "qb": ([128, 2832], BF), "qq": ([128, 2832], BF),
     "rb": ([128, L], BF), "b1": ([128, L], BF), "gp": ([128, L], BF),
-    "cx": ([128, 576], I32), "chi": ([128, 960], BF), "cf": ([128, 192 * 15], F32), "ci": ([128, 192], I32),
-    "v0i": ([128, 160], I32), "wti": ([128, 4], I32), "wcol": ([128, 8], F32), "wcb": ([128, 8], BF),
+    "cx": ([128, 1152], I32), "cf": ([128, 1152 + 192], F32), "lo": ([128, 512], F32),
+    "v0i": ([128, 160], I32), "wti": ([128, 4], I32), "wcol": ([128, 4], F32), "wcb": ([128, 8], BF),
     "off": ([128, 160], U16), "idx": ([128, 160], U16),
-    "lc": ([128, 256], F32), "xt": ([128, 256], F32), "ht": ([128, 256], BF), "ft": ([128, 256], F32), "ot": ([128, 256], BF),
-    "hs": ([128, 512], F32),
-    "ones": ([128, 256], BF), "idb": ([128, 128], BF), "idf": ([128, 128], F32), "ids": ([128, 128 * 7], BF),
+    "lc": ([128, 256], BF), "lcw": ([128, 256], BF), "xa": ([128, 1024], F32), "xt": ([128, 256], F32), "xr": ([128, 256], F32),
+    "ht": ([128, 256], BF), "ft": ([128, 256], F32), "hs": ([128, 512], F32), "ot": ([128, 256], BF),
+    "ones": ([128, 256], BF), "idf": ([128, 128], F32), "idn": ([128, 128], F32), "ids": ([128, 128 * len(IDW)], BF),
     "bd8": ([128, 8], BF), "bd": ([128, 128], BF), "bda": ([128, 128], BF), "bdb": ([128, 128], BF), "tri": ([128, 128], BF),
-    "z1": ([128, 144], BF), "z8": ([128, 144], BF), "zs": ([128, 144], BF), "zr": ([128, 144], BF),
+    "zz": ([128, 144 * 7], BF), "col": ([128, 64], F32),
     "wm": ([128, 128], BF), "wl": ([128, 32], BF), "wr": ([128, 8], BF), "wb": ([128, 16], BF), "wq": ([128, 24], BF),
-    "mm": ([128, 128 * 19], BF), "tl": ([128, 128 * 15], BF), "eq": ([128, 4096], BF), "kw": ([128, 256], U16),
-    "pi": ([128, 4], I32), "pc": ([128, 16], F32), "sw": ([128, 256], BF),
-    "xb": ([128, 256], BF), "t1": ([128, 256], BF), "t2": ([128, 256], BF), "il": ([128, 64], F32),
-    "ovl": ([128, 160], BF), "inc": ([128, 176], BF), "incl": ([128, 176], F32), "junk": ([128, 256], BF),
-    "sm": ([128, 16 * 24], F32), "su": ([128, 16 * 8], U16),
-    "cmp": ([128, 256], BF), "box": ([128, 512], BF), "own": ([128, 256], BF), "rcv": ([128, 512], BF),
-    "nw": ([128, 256], BF), "nh": ([128, 256], BF),
-    "f32": ([128, 160], F32), "v32": ([128, 160], F32), "dn": ([128, 160], F32), "sl": ([128, 160], F32),
-    "la": ([128, 160], F32), "lb": ([128, 160], F32), "li": ([128, 160], I32),
-    "gz": ([128, 256], BF), "mk": ([128, 256], BF), "thm": ([128, 256], BF), "qm": ([128, 256], F32),
-    "cm3": ([128, 256], BF), "ge": ([128, 256], BF), "ru": ([128, 256], BF), "gu": ([128, 256], BF), "xbb": ([128, 256], BF),
-    "wz": ([128, 256], BF), "tn0": ([128, 256], F32),
+    "mm": ([128, 128 * 24], BF), "tl": ([128, 128 * 16], BF), "eq": ([128, 4096], BF), "kw": ([128, 256], U16),
+    "pi": ([128, 4], I32), "pc": ([128, 24], F32), "pb": ([128, 2], BF), "sw": ([128, 256], BF),
+    "x0": ([128, 768], BF), "x1": ([128, 256], BF), "il": ([128, 64], F32),
+    "ovl": ([128, 160], BF), "inc": ([128, 176], BF), "incl": ([128, 176], F32), "tb": ([128, 96], F32), "junk": ([128, 64], F32),
+    "sm": ([128, 16 * 24], F32), "su": ([128, 16 * 12], U16),
+    "cmp": ([128, 768], BF), "box": ([128, 544], BF), "rcv": ([128, 544], BF),
+    "v32": ([128, 160], F32), "sl": ([128, 160], BF), "la": ([128, 160], F32), "lb": ([128, 160], F32), "lh": ([128, 160], F32),
+    "li": ([128, 160], I32),
+    "gz": ([128, 256], BF), "mk": ([128, 256], BF), "thm": ([128, 256], F32), "qm": ([128, 256], BF), "mq": ([128, 256], BF),
+    "cm3": ([128, 256], BF), "ge": ([128, 256], BF), "ru": ([128, 256], BF), "gu": ([128, 256], BF), "cd": ([128, 256], BF),
+    "tn0": ([128, 256], F32),
 }
-for _k in (0, 1):
-    for _n, _d in (("kv", BF), ("hv", BF), ("hn", BF), ("h17", BF), ("k0", BF), ("bw", BF), ("gb", BF), ("nd", BF), ("dd", BF),
-                   ("kn", BF), ("pn", F32), ("ww", BF)):
-        SB["%s%d" % (_n, _k)] = ([128, 256], _d)
+for _k in (0, 1, 2):
+    for _n, _w, _d in (("kv", 256, BF), ("hv", 256, BF), ("sb", 256, BF), ("rp", 512, BF), ("kn", 256, BF), ("pn", 256, F32), ("ww", 256, BF)):
+        SB["%s%d" % (_n, _k)] = ([128, _w], _d)
 SCRATCH = {k: ("sbuf", s, d) for k, (s, d) in SB.items()}
 for _k in range(8):
     SCRATCH["ps%d" % _k] = ("psum", [128, 512], F32)
-SEMAPHORES = ["sv", "ss", "sp", "sg", "got0", "got1", "out0", "out1"] + ["d%d" % k for k in range(40)]
+SEMAPHORES = ["sv", "ss", "sp", "sg", "got0", "got1", "out0", "out1"] + ["d%d" % k for k in range(44)]
 
-GC, SC, PEC = 1.7, 3.8, 0.6
-VI = (0, 1, 0, 1, 0)
-TRIES, SEED, AMP = 200, 1, 1500.0
+GC, SC, PEC = 1.7, 3.8, 0.55
+DROW, DBW, DLAT, RLAT = 300.0, 400.0, 700.0, (3500.0, 2500.0)
+TRIES, SEED, AMP = 5000, 1, 600.0
+SAME = {"p": 0.0, "g": 120.0}
+CASES = (({"sg": 0.75, "vg": 0.8, "vs": 0.6, "g": 1.3, "p": 1.1, "d": 1.3}, 60.0), ({"sg": 1.2, "vs": 1.4, "p": 0.9, "d": 0.7}, 0.0))
+HINT = "vsp"
 _PLAN = {}
 
 
@@ -72,7 +88,8 @@ def build(T, dst, msk):
     def op(eng, fns, rd, wr, cost, lat=0.0, sem=None, inc=1):
         rr = [r for x in rd if isinstance(x, tuple) for r in x[1]]
         ww = [r for x in wr for r in x[1]]
-        ops.append({"eng": eng, "fns": fns, "rd": rr, "wr": ww, "cost": cost, "lat": lat, "sem": sem, "inc": inc, "aft": []})
+        kind = eng + ("g" if len(rd) > 0 and isinstance(rd[0], tuple) and len(rd[0]) == 5 else "s" if wr[0][0] is None and eng == "v" else "")
+        ops.append({"eng": eng, "fns": fns, "rd": rr, "wr": ww, "cost": cost, "lat": lat, "sem": sem, "inc": inc, "aft": [], "kind": kind})
 
     def val(x):
         return x[0] if isinstance(x, tuple) else x
@@ -129,7 +146,9 @@ def build(T, dst, msk):
     def dma(q, out, a, nbytes):
         s = "d%d" % nd[0]
         nd[0] += 1
-        op(q, [lambda e: e.dma_start(out[0], a[0])], [a], [out], 60, lat=2000 + nbytes / 150.0, sem=s, inc=16)
+        op(q, [lambda e: e.dma_start(out[0], a[0])], [a], [out], 90, lat=0.0, sem=s, inc=16)
+        op("d", [], [a], [out], DROW + nbytes / DBW, lat=DLAT, sem=s)
+        ops[-1]["alias"] = len(ops) - 2
 
     def D(n, a=None, b=None):
         return (T[n][:] if a is None else T[n][:, a:b], [(n + "_hbm", 0, 1, len(ops))], 0, None)
@@ -144,124 +163,163 @@ def build(T, dst, msk):
     def sel(out, a, pat, cmpop, fill, base, cm):
         op("g", [lambda e: e.affine_select(out[0], a[0], pat, cmpop, fill, base, cm)], [a], [out], 170 + 2 * out[2])
 
-    def put(n, a, b, s, row, w, pat=None):
-        x = A(n, a, b, s)
+    def put(n, a, b, s, row, w, pat=None, tag=None):
+        x = A(n, a, b, s, tag=tag)
         sel(x, x, pat or [[-16, 8]], AL.not_equal, float(w), -row, 1)
 
     for k in range(3):
-        dma("s", A("kt", 1024 * k, 1024 * k + 1024), D("kk", 1024 * k, 1024 * k + 1024), 300000 * (k + 1))
-    for k, n in enumerate(("c0", "c1", "rt")):
-        dma("y", A("cx", 192 * k, 192 * k + 192), D(n), 98304)
+        dma("s" if k == 0 else "y", A("kt", 1024 * k, 1024 * k + 1024), D("kk", 1024 * k, 1024 * k + 1024), 262144)
+    dma("y", A("cx", 0, 64), D("c0", 0, H), 32768)
+    dma("s", A("cx", 192, 384), D("c1"), 98304)
+    dma("y", A("cx", 384, 576), D("rt"), 98304)
+    dma("s", A("cx", 64, 192), D("c0", H, V), 65536)
     dma("y", A("v0i"), D("v0"), 81920)
-    dma("y", A("qa", 0, HL), D("qs", 0, HL), 700000)
-    dma("y", A("qa", HL, L), D("qs", HL, L), 1000000)
+    dma("y", A("qa", 0, HL), D("qs", 0, HL), 327680)
+    dma("y", A("qa", HL, L), D("qs", HL, L), 327680)
     dma("y", A("wti", 0, 1), D("wt"), 512)
 
+    iota(A("pt", 0, 512), [[1, 512]], 0, 0)
+    ts(A("pt", 512, 1024), A("pt", 0, 512), 512.0, AL.add)
+    act(A("pt", 1024, 2048), A("pt", 0, 1024), bias=1024.0)
+    ts(A("pt", 2048, V), A("pt", 0, 1024), 2048.0, AL.add)
+    iota(A("lo", p1=32), [[0, 16], [1, 32]], 0, 0)
     ms(A("ones"), 1.0)
-    ms(A("pt", 0, 2048), 1.0)
-    for n in ("wm", "wl", "z1"):
-        ms(A(n, 0, 144 if n == "z1" else 32), 0.0)
+    ms(A("wm", 0, 32), 0.0)
+    iota(A("wl"), [[0, 32]], 0, 0)
+    ms(A("zz"), 0.0)
+    ms(A("col"), 0.0)
     sel(A("bd8"), A("ones", 0, 8), [[-16, 8]], AL.is_ge, 0.0, 0, 1)
     sel(A("bd8"), A("bd8"), [[16, 8]], AL.is_ge, 0.0, 15, -1)
     iota(A("pi", 0, 1), [[0, 1]], 0, 1)
-    iota(A("ci"), [[1, 192]], 0, 192)
-    iota(A("pt", 2048, V), [[0, 1024]], 1, 0)
-    sel(A("idb"), A("ones", 0, 128), [[-1, 128]], AL.is_equal, 0.0, 0, 1)
+    sel(A("ids", 0, 128), A("ones", 0, 128), [[-1, 128]], AL.is_equal, 0.0, 0, 1)
     ts(A("pi", 1, 2), A("pi", 0, 1), 15, AL.bitwise_and)
     ts(A("pi", 2, 3), A("pi", 0, 1), 1, AL.bitwise_and)
-    ts(A("pi", 3, 4), A("pi", 0, 1), 4, AL.logical_shift_right)
-    ROW, CP, TH, GO = A("pc", 0, 1), A("pc", 1, 2), A("pc", 2, 3), A("pc", 3, 4)
+
+    def PC(k):
+        return A("pc", k, k + 1)
+    ROW, CP, CPH, CPX, THS, GS, GB, TBB, HC = [PC(k) for k in range(9)]
+    THV = A("pb", 0, 1)
     cp(ROW, A("pi", 1, 2))
-    ts(CP, A("pi", 2, 3), -6144.0, AL.mult, 3072.0 - HB - 7.5, AL.add)
-    ts(TH, A("pi", 2, 3), -6144.0, AL.mult, 3072.0 - 24.0, AL.add)
-    ts(GO, A("pi", 3, 4), -3072.0, AL.mult)
-    act(A("z1", 15, 143, 16), A("bd8"))
-    act(A("wr"), A("bd8"), scale=-512.0)
-    act(A("wb", 0, 8), A("bd8"), scale=2.0 ** 18)
-    act(A("wb", 8, 16), A("bd8"))
+    ts(CP, A("pi", 2, 3), -6144.0, AL.mult, 3072.0 - 222.5, AL.add)
+    act(CPH, CP, bias=-HB)
+    act(CPX, CP, bias=-2.0625 * HB)
+    act(THS, CP, bias=222.5 - 8.0)
+    act(THV, CP, bias=222.5)
+    put("col", 0, 16, 1, rN, -2, [[rN - rI, 2], [-16, 8]])
+    put("col", 32, 64, 1, 0, PH - 15.5, [[-8, 2], [-2, 2], [-16, 8]])
+    put("col", 16, 32, 1, rO, -1, [[-1, 2], [-16, 8]])
+    put("col", 32, 40, 1, rL, 1 - H)
+    put("col", 40, 48, 1, rI, H)
+    put("col", 48, 64, 1, rO, 1, [[-1, 2], [-16, 8]])
+    act(A("junk", 0, 32), A("col", 0, 32), bias=1.0 / 32, acc=GS)
+    act(A("junk", 32, 64), A("col", 32, 64), acc=GB)
+
+    def Z(k, j=None):
+        if j is None:
+            return A("zz", 144 * k + 15, 144 * k + 143, 16)
+        return A("zz", 144 * k + 15 - j, 144 * k + 143 - j)
+    z1, z16, z160, zs, zk, zr, z0 = range(7)
+    act(Z(z1), A("bd8"))
+    act(A("wr"), A("bd8"), scale=-1024.0)
+    act(A("wb", 0, 8), A("bd8"), scale=U2 / 2)
+    act(A("wb", 8, 16), A("bd8"), scale=U2 / 2)
     act(A("wq", 0, 8), A("bd8"))
-    act(A("idf"), A("idb"))
-    IDS = {}
-    for k, w in enumerate((-1.0, 16.0, -15.0, 32.0, -31.0, -8192.0, -8.0)):
-        IDS[w] = k
-        sel(A("ids", 128 * k, 128 * k + 128), A("idb"), [[-1, 128]], AL.not_equal, w, 0, 1)
+    act(A("idf"), A("ids", 0, 128))
 
     def ID(w, n=128):
-        if w == 1:
-            return A("idb", 0, n, p1=n)
-        return A("ids", 128 * IDS[w], 128 * IDS[w] + n, p1=n)
-    put("wm", 0, 32, 1, 0, 1, [[-2, 4], [-16, 8]])
-    put("wm", 0, 32, 1, 1, 1, [[-2, 4], [-16, 8]])
-    put("wm", 0, 32, 1, rO2, -OFS, [[0, 4], [-16, 8]])
-    for w, r, x in ((0, rLF, 65536), (1, rK, 16384), (1, rO1, -69632), (2, rO1, -2 ** 17), (2, rNO, -2 ** 23), (3, rLF, -65536)):
+        k = IDW.index(w)
+        return A("ids", 128 * k, 128 * k + n, p1=n)
+    made = [1.0]
+
+    def ids(*ws):
+        for w in ws:
+            made.append(w)
+            sel(ID(w), ID(1.0), [[-1, 128]], AL.not_equal, w, 0, 1)
+    for u in (0, 1):
+        put("wm", 0, 32, 1, u, 1, [[-8, 2], [-2, 2], [-16, 8]])
+        put("wm", 8, 24, 1, rA + u, -1, [[0, 2], [-16, 8]])
+    for w, r, x in ((0, rO, -PH), (1, rK, 32768), (2, rO, -U2 / 2), (3, rO, -PH), (1, rO, -216 * 16384), (2, rN, -2 ** 23), (3, rL, -65536),
+                    (1, rP, -8192), (1, rL, -2 ** 19)):
         put("wm", 8 * w, 8 * w + 8, 1, r, x)
     for k in (1, 2, 3):
         act(A("wm", 32 * k, 32 * k + 32), A("wm", 0, 32))
-        put("wm", 32 * k + 24, 32 * k + 32, 1, rO1, 4096 * k)
+        put("wm", 32 * k + 24, 32 * k + 32, 1, rP, 8192 * k)
+    ms(A("lcw"), 0.0)
+    for t in (0, 1):
+        x = A("lcw", 128 * t, 128 * t + 128)
+        sel(x, x, [[0, 128]], AL.is_gt, -8 * U2, VB[t] // 16, -1)
 
-    def CF(k, n=1):
-        return A("cf", 192 * k, 192 * (k + n))
-
-    def row(r, src):
-        dma("y", A("pt", 0, V, p0=r, ps=16, tag=r), src, 400000)
-    ts(CF(6), A("ci"), GO, AL.add)
-    ts(CF(8), CF(6), 1023.5, AL.is_gt)
-    act(A("chi", 576, 768), CF(6))
-    act(CF(13), CF(8), bias=-8192.0, scale=8192.0)
-    act(CF(14), CF(8), scale=-8192.0)
-    tt(CF(13), CF(13), CF(6), AL.add)
-    tt(CF(7), CF(6), A("chi", 576, 768), AL.subtract)
-    row(rS, CF(6)); row(rS + 1, CF(7)); row(rLF, CF(8))
-    cp(CF(0, 3), A("cx"))
-    act(A("chi", 0, 576), CF(0, 3))
-    tt(CF(9), CF(0), CF(14), AL.add)
-    tt(CF(9), CF(9), CF(13), AL.max)
-    row(rC1, CF(1)); row(rR, CF(2)); row(rA, CF(9))
-    tt(CF(3, 3), CF(0, 3), A("chi", 0, 576), AL.subtract)
-    ts(CF(11), CF(2), -0.5, AL.is_lt)
-    act(A("chi", 768, 960), CF(9))
-    tt(CF(10), CF(9), A("chi", 768, 960), AL.subtract)
-    row(rC1 + 1, CF(4)); row(rR + 1, CF(5)); row(rA + 1, CF(10)); row(rNO, CF(11)); row(rC0, CF(0)); row(rC0 + 1, CF(3))
+    def row(r, a, b, src):
+        dma("y", A("pt", a, b, p0=r, ps=16, tag=r), src, 32 * (b - a))
+    for u in (0, 1):
+        o = 576 * u
+        if u:
+            ts(A("cx", 576, 1152), A("cx", 0, 576), 31, AL.bitwise_and)
+        cp(A("cf", o, o + 576), A("cx", o, o + 576))
+        row(rA + u, 0, H, A("cf", o, o + 64))
+        row(rC + u, 0, V, A("cf", o + 192, o + 384))
+        row(rR + u, 0, V, A("cf", o + 384, o + 576))
+        if not u:
+            row(rN, 0, V, A("cf", 384, 576))
+            row(rS + 1, 0, H, A("lo", p1=16))
+    for u in (0, 1):
+        row(rS + u, H, V, A("cf", 576 * u + 64, 576 * u + 192))
+    row(rA + 1, H, V, A("lo", p1=32))
     for k in range(3):
         ts(A("hh", 1024 * k, 1024 * k + 1024), A("kt", 1024 * k, 1024 * k + 1024), HB - 7.5, AL.add)
     for a, n, bank, c in ((0, 64, "ps4", 0), (1024, 128, "ps3", 64)):
-        mmg([(A(bank, 0, n), A("z1", 15 - s, 143 - s), A("hh", a + n * s, a + n * s + n)) for s in range(16)])
-        src = A("cf", 192 * 12 + c, 192 * 12 + c + n)
+        mmg([(A(bank, 0, n), Z(z1, s), A("hh", a + n * s, a + n * s + n)) for s in range(16)])
+        src = A("cf", 1152 + c, 1152 + c + n)
         act(src, A(bank, 0, n), bias=-HB, scale=0.0625)
-        dma("s", A("pt", a, a + 16 * n, p0=rK, ps=16, tag=rK), src, 512 * n)
+        dma("y", A("pt", a, a + 16 * n, p0=rK, ps=16, tag=rK), src, 512 * n)
     for k in range(6):
         a = 512 * k
         b = "ps%d" % (5 + k % 3)
-        mmg([(A(b), ID(1), A("kt", a, a + 512)), (A(b), ID(1), A("hh", a, a + 512))])
-        act(A("tt", a, a + 512), A(b))
+        mmg([(A(b), ID(1.0), A("kt", a, a + 512)), (A(b), ID(1.0), A("hh", a, a + 512))])
+        if k in TTV:
+            ts(A("tt", a, a + 512), A(b), CPH, AL.add)
+        else:
+            act(A("tt", a, a + 512), A(b), bias=CPH)
     cp(A("off"), A("v0i"))
-    ms(A("qa", L, L + 16), -16.0)
-    ms(A("qb", L, L + 16), -16.0)
-    ms(A("rct", R, R + 16), 0.0)
+    for X in (0, 1):
+        ts(A("qq", HL * X, HL * X + HL), A("qa", HL * X, HL * X + HL), -33.0, AL.mult, 231.0, AL.add)
+    iota(A("qq", L, L + 16), [[0, 16]], 0, 0)
+    iota(A("qb", L, L + 16), [[0, 16]], 0, 0)
+    iota(A("rct", R, R + 16), [[-1, 16]], 0, 0)
 
     def sums(q, X, nw):
         o = HL * X
-        for a, b in ((0, N1), (N1, HL)):
-            act(A("qq", o + a, o + b), A(q, o + a, o + b), bias=CP, scale=-33.0)
         mmg([(A("ps%d" % X, j, 128 * nw, 16, p1=80), A(q, o + j, o + HL, 16), A("wq", 0, 8 * nw)) for j in range(16)], each=True)
-        act(A("lc", 128 * X, 128 * X + 128, p1=80), A("ps%d" % X, 0, 128, p1=80), scale=16384.0)
+        act(A("lc", 128 * X, 128 * X + 128, p1=80), A("ps%d" % X, 0, 128, p1=80), scale=32768.0 / 33)
     for X in (0, 1):
-        sums("qa", X, 1)
+        sums("qq", X, 1)
 
-    for n in ("z8", "zs", "zr", "mm"):
-        iota(A(n), [[0, SB[n][0][1]]], 0, 0)
-    put("wl", 0, 8, 1, rC0, 1); put("wl", 0, 8, 1, rC0 + 1, 1); put("wl", 8, 16, 1, rC1, 1); put("wl", 8, 16, 1, rC1 + 1, 1)
-    put("wl", 0, 16, 1, rO2, -OFS, [[0, 2], [-16, 8]])
-    for w, r, x in ((1, rK, 16384), (1, rO1, -69632), (2, rO1, 63 * 2 ** 17), (2, rO2, 1024 - OFS), (2, rLF, -2 ** 23), (3, rO1, -64.5), (3, rNO, 64)):
+    ids(-1.0)
+    for u in (0, 1):
+        put("wl", 0, 16, 1, rS + u, 1, [[rS - rC, 2], [-16, 8]])
+        put("wl", 8, 16, 1, rS + u, -1)
+    for w, r, x in ((0, rO, -PH), (1, rK, 32768), (1, rO, -216 * 16384), (1, rP, -8192), (2, rO, -U2 / 2), (2, rI, 2 ** 22),
+                    (3, rO, -65 * 2 ** 17), (3, rN, 2 ** 23)):
         put("wl", 8 * w, 8 * w + 8, 1, r, x)
+    ids(*[w for w in IDW if w not in made])
+    for k in range(6):
+        iota(A("mm", 512 * k, 512 * k + 512), [[0, 512]], 0, 0)
     sel(A("bd"), A("ones", 0, 128), [[-16, 8], [0, 16]], AL.is_ge, 0.0, 0, 1)
     sel(A("bd"), A("bd"), [[16, 8], [0, 16]], AL.is_ge, 0.0, 15, -1)
     sel(A("tri"), A("bd"), [[1, 128]], AL.is_ge, 0.0, 0, -1)
     iota(A("sw"), [[1, 256]], 0, 0)
-    for j in range(1, 16):
-        sel(A("tl", 128 * j - 128, 128 * j), A("bd"), [[16, 8], [0, 16]], AL.is_ge, 0.0, j - 1, -1)
+    iota(A("x0"), [[32, 24], [0, 32]], V, 0)
+    iota(A("x1"), [[0, 8], [1, 32]], 0, 0)
+    ts(A("junk", 0, 16), A("sw", 0, 16), ROW, AL.is_gt)
+    ts(A("junk", 16, 32), A("sw", 0, 16), ROW, AL.is_equal)
+    tt(A("junk", 32, 48), A("junk", 0, 16), A("junk", 16, 32), AL.subtract)
+    for j in range(16):
+        if j < TLV:
+            ts(A("tl", 128 * j, 128 * j + 128), A("bd"), A("junk", 32 + j, 33 + j), AL.mult)
+        else:
+            act(A("tl", 128 * j, 128 * j + 128), A("bd"), scale=A("junk", 32 + j, 33 + j))
     iota(A("il", 48, 64), [[16, 16]], 0, 0)
-    MN = {"sum": 18}
+    MN = {"sum": 23}
 
     def M(name):
         return A("mm", 128 * MN[name], 128 * MN[name] + 128)
@@ -272,56 +330,76 @@ def build(T, dst, msk):
         for rin, rout, w in ent:
             if rout is None:
                 put("mm", b, b + 128, 1, rin, w, [[-16, 8], [0, 16]])
+            elif isinstance(rout, tuple):
+                put("mm", b + rout[0], b + 128, 8, rin, w, [[-16, 8], [0, 2]], rout[0] % 8)
             else:
-                put("mm", b + rout, b + 128, 16, rin, w)
+                put("mm", b + rout, b + 128, 16, rin, w, None, rout % 8)
+
+    def whole(rin, rout, c=-PH):
+        return [(rin, rout, 1), (rin + 1, rout, 1), (rO, rout, c)]
     me("sk", (rK, None, 2))
-    me("lf", (rLF, None, -64))
-    me("sf", (rS, None, 1), (rS + 1, None, 1))
-    me("n1", *[(a, b, 1) for a, b in ((0, 0), (1, 0), (1, 1), (6, 6), (7, 6), (7, 7), (8, 8), (9, 8), (9, 9), (8, 2), (9, 2), (9, 3), (11, 11), (12, 12), (13, 13))])
-    me("n2", (2, 2, 1), (3, 2, 1), (8, 2, -1), (9, 2, -1), (3, 3, 1), (9, 3, -1))
-    me("x1", *[(a, b, 1) for a, b in ((2, 8), (3, 8), (3, 9), (2, 2), (3, 2), (3, 3), (4, 4), (5, 4), (5, 5), (10, 10), (14, 14))])
-    me("nx0", (0, 4, 1), (2, 4, V), (1, 5, 1))
-    me("xx0", (0, 0, 1), (2, 0, V), (1, 1, 1), (0, 6, 1), (2, 6, V), (1, 7, 1), (2, 11, 1), (2, 12, 1), (2, 13, 1))
-    me("nx1", (0, 4, 1), (2, 4, V + I))
-    me("c0", (8, None, 1), (9, None, 1))
-    me("cb", (2, None, 1), (3, None, 1), (8, None, -1), (9, None, -1))
-    me("zz", (6, None, -1), (7, None, -1))
-    me("p1", (8, 8, 1), (9, 8, 1))
-    me("p2", (2, 2, 1), (3, 2, 1))
-    me("p3", (0, 2, 1), (2, 2, V), (0, 4, 1), (2, 4, V + 2 * I))
-    me("p4", (0, 2, -1), (2, 2, -V))
-    me("q2", (2, 2, -1), (3, 2, -1), (2, 8, -1), (3, 8, -1))
-    me("q3", (0, 2, 1), (2, 2, V), (0, 8, 1), (2, 8, V))
-    for r, w in ((rR, 1), (rR + 1, 1), (rO1, -69632), (rO2, -OFS), (rNO, -2 ** 23)):
-        put("zr", 15, 143, 16, r, w)
-    act(A("mm", 128 * 18 + rK, 128 * 19, 16), A("bd8"))
+    CS, CS1, LI = (rC, rS), (rC + 1, rS + 1), (rL, rI)
+    me("k1", (rO, None, HB + 16 - 128))
+    me("sfA", (rA, None, 1), (rA + 1, None, 1))
+    me("sl", (rC, rC, 1 / 32), (rS, rC, -1 / 32), (rC + 1, rC + 1, 1), (rS + 1, rC + 1, -1))
+    me("n1", *(whole(rA, rA) + whole(rS, CS) + [(rA + 1, rA + 1, 1), (rS + 1, CS1, 1), (rP, rC, -2112), (rP, rC + 1, -64), (rO, LI, 2048)]))
+    me("n2", (rC, rC, 32), (rC + 1, rC, 1), (rC + 1, rC + 1, 1))
+    me("n3", (0, rC, -2112), (0, rC + 1, -64))
+    me("nx0", (0, rR, 1))
+    me("nx1", (0, rR, 1), (0, rR + 1, 1))
+    me("x1", *(whole(rC, CS) + whole(rR, rR) + [(rC + 1, CS1, 1), (rR + 1, rR + 1, 1), (rK, rK, 1), (rN, rN, -1), (rO, LI, 2048)]))
+    me("xx0", (0, rA, 1))
+    me("xx1", (0, rA, 1), (0, rA + 1, 1))
+    me("sfS", (rS, None, 1), (rS + 1, None, 1))
+    me("sp", (rC, CS, 1 / 32), (rA, rC, -1 / 32), (rC + 1, CS1, 1), (rA + 1, rC + 1, -1), (rO, rS, -PH / 32))
+    me("xs0", (0, rS, -1 / 32))
+    me("xs1", (0, rS + 1, -1))
+    me("t1", (rA, rC, 1), (rA + 1, rC, 1))
+    me("t4", (rA, rC, -1), (rA + 1, rC, -1), (rO, rC, -2112))
+    me("p1", *(whole(rA, rA) + [(rO, rC, -2112)]))
+    me("p2", (rS, rC, 32), (rS + 1, rC, 1))
+    me("e2", (0, rC, 1))
+    me("q2", (rS, CS, -32), (rS + 1, CS, -1))
+    me("q3", (0, CS, 2112))
+    for r, w in ((rR, 1), (rR + 1, 1), (rO, -PH), (rP, -17 * 8192), (rN, -2 ** 23)):
+        put("zz", 144 * zr + 15, 144 * zr + 143, 16, r, w)
+    put("zz", 144 * z0 + 15, 144 * z0 + 143, 16, rC, 1)
+    act(A("mm", 128 * 23 + rK, 128 * 24, 16), A("bd8"))
     act(A("bda"), A("bd"), scale=-0.0625)
     act(A("bdb"), A("bd"), scale=-2.0)
-    act(A("z8", 15, 143, 16), A("bd8"), scale=8192.0)
-    act(A("zs", 15, 143, 16), A("bd8"), scale=0.0625)
-    act(A("il", 0, 16), A("il", 48, 64), bias=ROW)
-    act(A("il", 16, 32), A("il", 0, 16), bias=0.5)
-    act(A("il", 32, 48), A("il", 0, 16), bias=float(W))
-    act(A("il", 48, 64), A("il", 0, 16), bias=16.0)
-    ts(A("pc", 4, 5), ROW, 0.0, AL.is_equal)
-    ts(A("pc", 5, 6), ROW, 1.0, AL.is_equal)
-    ts(A("pc", 6, 7), ROW, 1.5, AL.is_gt)
-    act(A("t1"), A("sw"), bias=3072.0)
-    act(A("t2"), A("t1"), bias=-3072.0)
-    tt(A("t1"), A("sw"), A("t2"), AL.subtract)
-    act(A("t2"), A("t1"), scale=A("pc", 5, 6))
-    act(A("t1"), A("sw"), bias=A("pc", 6, 7), scale=A("pc", 4, 5))
-    tt(A("xb"), A("t1"), A("t2"), AL.add)
-    cp(A("wcol", 0, 1), A("wti", 0, 1))
-    act(A("wcb", 0, 1), A("wcol", 0, 1))
-    act(A("wcol", 2, 3), A("wcb", 0, 1))
-    act(A("wcol", 1, 2), A("wcb", 0, 1), bias=A("wcol", 0, 1), scale=-1.0)
-    act(A("wq", 8, 16), A("bd8"), scale=A("wcol", 2, 3))
+    for z, w in ((z16, 16.0), (z160, 160.0), (zs, -512.0), (zk, 16384.0)):
+        act(Z(z), A("bd8"), scale=w)
+    put("zz", 144 * z160 + 15, 144 * z160 + 143, 16, 15, 160 + 4096)
+    IL, SPN, SPQ = A("il", 0, 16), A("il", 16, 32), A("il", 32, 48)
+    act(IL, A("il", 48, 64), bias=ROW)
+    act(SPN, IL, bias=W - 8192.0)
+    act(SPQ, IL, bias=float(SP))
+    ts(TBB, ROW, 9.5, AL.is_gt, 9999.0, AL.mult)
+    ts(A("wti", 1, 2), A("wti", 0, 1), 31.0, AL.mult)
+    ts(A("wti", 2, 3), A("wti", 1, 2), 1023 - 31, AL.bitwise_and)
+    ts(A("wti", 3, 4), A("wti", 1, 2), 31, AL.bitwise_and)
+    cp(A("wcol", 0, 2), A("wti", 2, 4))
+    act(A("wq", 8, 16), A("bd8"), scale=A("wcol", 0, 1))
     act(A("wq", 16, 24), A("bd8"), scale=A("wcol", 1, 2))
-    ms(A("inc", 0, 1), 0.0)
-    ms(A("incl", 160, 176), 9999.0)
+    act(A("wcb", 0, 2), A("wcol", 0, 2))
+    mmg([(A("ps7", 0, 1), A("bd"), A("wcb", u, u + 1)) for u in (0, 1)])
+    act(HC, A("ps7", 0, 1), bias=2.0 ** 24 - 1024, scale=-231.0)
+    iota(A("inc", 0, 1), [[0, 1]], 0, 0)
+    iota(A("incl", 160, 176), [[0, 16]], 9999, 0)
+    iota(A("tb"), [[0, 96]], 9999, 0)
     late = [len(ops)]
     dma("y", A("rct", 0, R), D("rec"), 262144)
+    posted = []
+
+    def turned(n, X, w=128, a=0, b=None):
+        return A(n, w * X + a, w * X + (w if b is None else b), p1=80)
+
+    def unround(pl, X, x, more):
+        out, idf = A(pl, 0, 80), A("idf", 0, 80, p1=80)
+        mmg([(out, y, idf) for y in more], True, False)
+        ts(turned("ht", X), x, CR, AL.add, CR, AL.subtract)
+        mmg([(out, x, idf)], False, False)
+        mmg([(out, turned("ht", X), ID(-1.0, 80))], False, True)
 
     def step(t, k, X):
         look = k == 4
@@ -330,59 +408,83 @@ def build(T, dst, msk):
         wd = 1024 if (t == 0 and k == 0) else (V if t == 0 else V + I)
         ps, pl = "ps%d" % X, "ps%d" % (2 + X)
         nw = 4 if (look or fin) else 3
-        mk = {}
-        for a, b in ((0, N1), (N1, HL)):
-            mk["g%d" % (a > 0)] = len(ops)
-            tt(A("rb", o + a, o + b), IND(A("tt", 0, wd), A("off", c + a // 16, c + b // 16)), A("qq", o + a, o + b), AL.add)
-        act(A("gp", o, o + HL), IND(A("pt", 0, wd), A("off", c, c + 80)))
-        for a, b in ((0, N1), (N1, HL)):
-            act(A("b1", o + a, o + b), A("rb", o + a, o + b), AF.Sign, bias=TH, scale=-1.0)
+        q = "qb" if t else "qq"
+        mk, at = {}, [len(ops)]
+
+        def done(name):
+            mk[name] = list(range(at[0], len(ops)))
+            at[0] = len(ops)
+        for a, b, name in ((0, N1, "g0"), (N1, HL, "g1")):
+            tt(A("rb", o + a, o + b), IND(A("tt", 0, wd), A("off", c + a // 16, c + b // 16)), A(q, o + a, o + b), AL.add)
+            done(name)
+        for a, b, name in ((0, NG, "gpa"), (NG, HL, "gpb")):
+            act(A("gp", o + a, o + b), IND(A("pt", 0, wd), A("off", c + a // 16, c + b // 16)), AF.Relu, bias=GB, scale=GS)
+            done(name)
+        nv = VB[t]
+        ts(A("b1", o + nv, o + HL), A("rb", o + nv, o + HL), THV, AL.is_lt, 2.0, AL.mult)
+        done("bv")
+        if nv:
+            act(A("b1", o, o + nv), A("rb", o, o + nv), AF.Sign, bias=THS, scale=-1.0)
+        done("bs")
         wp, w0 = ("wl", 0) if look else ("wm", 32 * k if fin else 0)
-        for h in (0, 8):
-            mmg([(A(ps, j, 128 * nw, 16, p1=80), A("gp", o + j, o + HL, 16), A(wp, w0, w0 + 8 * nw)) for j in range(h, h + 8)], h == 0, False)
-        for h in (0, 8):
-            mmg([(A(ps, 128 + j, 256, 16, p1=80), A("rb", o + j, o + HL, 16), A("wr")) for j in range(h, h + 8)], False, False)
         nb = 2 if look else 1
-        for h in (0, 8):
-            mmg([(A(ps, 256 + j, 256 + 128 * nb, 16, p1=80), A("b1", o + j, o + HL, 16), A("wb", 0, 8 * nb)) for j in range(h, h + 8)], False, h == 8)
-        xt, ht = A("xt", 128 * X, 128 * X + 128, p1=80), A("ht", 128 * X, 128 * X + 128, p1=80)
-        mk["t0"] = len(ops)
-        tt(xt, A(ps, 128, 256, p1=80), A("lc", 128 * X, 128 * X + 128, p1=80), AL.subtract)
-        tt(xt, A(ps, 0, 128, p1=80), xt, AL.max)
-        tt(xt, A(ps, 256, 384, p1=80), xt, AL.max)
-        mk["t1"] = len(ops)
-        ts(ht, xt, CR, AL.add, CR, AL.subtract)
-        mmg([(A(pl, 0, 80), xt, A("idf", 0, 80, p1=80)), (A(pl, 0, 80), ht, ID(-1.0, 80))])
-        ft = A("ft", 128 * X, 128 * X + 128, p1=80)
+        for src, c0, c1, wt in (("gp", 0, 128 * nw, A(wp, w0, w0 + 8 * nw)), ("rb", 128, 256, A("wr")),
+                                ("b1", 256, 256 + 128 * nb, A("wb", 0, 8 * nb))):
+            for h in (0, 8):
+                mmg([(A(ps, c0 + j, c1, 16, p1=80), A(src, o + j, o + HL, 16), wt) for j in range(h, h + 8)],
+                    src == "gp" and h == 0, src == "b1" and h == 8)
+            if src == "gp":
+                mmg([(A(ps, 128, 256, p1=80), ID(1.0, 80), turned("lc", X))]
+                    + [(A(ps, 256 + 128 * u, 384 + 128 * u, p1=80), ID(1.0, 80), turned("lcw", t)) for u in range(nb)], False, False)
+            done(src + "m")
+        if look:
+            ts(turned("ot", X), A(ps, 384, 512, p1=80), 0.0, AL.is_gt)
+            mmg([(A(pl, 128, 208), turned("ot", X), ID(1.0, 80))])
+            src, ini, out = A(pl, 128, 208), A("inc", c, c + 1), A("inc", c + 1, c + 81)
+            op("v", [lambda e: e.tensor_tensor_scan(out[0], T["ones"][:, 0:80], src[0], ini[0], AL.mult, AL.add)], [A("ones"), src, ini], [out], 140)
+            act(A("ovl", c, c + 80), src)
+            done("over")
+        nr = 384 if look else 256
+        act(turned("xa", X, 512, 0, nr), A(ps, 0, nr, p1=80), AF.Relu)
+        done("relu")
+        if look:
+            done("max")
+            unround(pl, X, turned("xa", X, 512, 128, 256), [turned("xa", X, 512, 0, 128), turned("xa", X, 512, 256, 384)])
+            done("rnd")
+            done("ft")
+            ts(A("idx", c, c + 80), A(pl, 0, 80), float(R + t), AL.min)
+            done("off")
+            return mk
+        tt(turned("xt", X), A(ps, 256, 384, p1=80), turned("xa", X, 512, 128, 256), AL.max)
+        done("max")
+        unround(pl, X, turned("xt", X), [turned("xa", X, 512, 0, 128)])
+        done("rnd")
         if fin:
             if k == 0:
-                cp(ft, A(ps, 384, 512, p1=80))
+                act(turned("ft", X), A(ps, 384, 512, p1=80))
             else:
-                tt(ft, A(ps, 384, 512, p1=80), ft, AL.max)
-        if look:
-            ot = A("ot", 128 * X, 128 * X + 128, p1=80)
-            ts(ot, A(ps, 384, 512, p1=80), 0.0, AL.is_gt)
-            ts(A("idx", c, c + 80), A(pl, 0, 80), OFS, AL.add)
-            mmg([(A(pl, 128, 208), ot, ID(1, 80))])
-            cp(A("ovl", c, c + 80), A(pl, 128, 208))
-        else:
-            mk["u"] = len(ops)
-            ts(A("off", c, c + 80), A(pl, 0, 80), OFS, AL.add)
+                tt(turned("ft", X), A(ps, 384, 512, p1=80), turned("ft", X), AL.max)
+        done("ft")
+        cp(A("off", c, c + 80), A(pl, 0, 80))
+        done("off")
         return mk
 
     def looks(t):
-        prev, last = None, None
+        prev, last = None, {}
         for k in range(5):
             for X in (0, 1):
                 m = step(t, k, X)
-                seq = [m["g0"]] + ([prev["t0"], prev["t1"]] if prev else []) + [m["g1"]] + ([prev["u"]] if prev and "u" in prev else [])
-                for a in seq:
-                    if last is not None:
-                        ops[a]["aft"].append(last)
-                    last = a
+                for who, name in (LAST if (k, X) == (4, 1) else SLOT):
+                    for a in (m[name] if who else prev[name] if prev else []):
+                        e = ops[a]["eng"]
+                        if e in last and e in HINT:
+                            ops[a]["aft"].append(last[e])
+                        last[e] = a
                 prev = m
+                if (t, k, X) == POSTBY:
+                    ops[m["g0"][0]]["aft"] += posted
                 if len(late) == 1:
-                    late.append(m["g0"])
+                    late.append(m["g0"][0])
 
     def SM(k, a=0, b=16):
         return A("sm", 16 * k + a, 16 * k + b)
@@ -390,207 +492,219 @@ def build(T, dst, msk):
     def SU(k):
         return A("su", 16 * k, 16 * k + 16)
 
-    def tolist(bank, pairs):
-        mmg([(A(bank, 0, 16), A(z, 15 - j, 143 - j), A(src, j, 256, 16)) for z, src in pairs for j in range(16)])
+    def tolist(out, pairs, start=True, more=(), stop=True):
+        mmg([(out, Z(z, j), A(src, a + j, a + 256, 16)) for z, src, a in pairs for j in range(16)] + list(more), start, stop)
 
-    def slots(t, q):
-        op("v", [lambda e: e.tensor_tensor_scan(T["inc"][:, 1:161], T["ones"][:, 0:160], T["ovl"][:, 0:160], 0.0, AL.mult, AL.add)],
-           [A("ones"), A("ovl")], [A("inc", 1, 161)], 110)
-        mmg([(A("ps4", 0, 160), A("bd"), A("inc", 1, 161))])
+    def slots(t):
+        for h in (0, 8):
+            mmg([(A("ps4", 0, 1), Z(z1, r), A("inc", 10 * r + 10, 10 * r + 11)) for r in range(h, h + 8)], h == 0, h == 8)
+        ts(A("cmp", 0, 256), A("sw"), A("ps4", 0, 1), AL.is_ge)
+        mmg([(A("ps5", 320, 336), Z(z1, r), A("inc", 1 + r, 161, 10)) for r in range(10)])
+        act(A("tb", 0, 80, 5), A("ps5", 320, 336), bias=TBB)
         mmg([(A("ps5", 0, 160), A("tri"), A("ovl")), (A("ps5", 0, 160), A("bd"), A("inc", 0, 160))])
-        cp(A("incl", 0, 160), A("ps5", 0, 160))
-        for c in range(16):
-            act(A("junk", 0, 160) if c % 2 else A("cmp", 0, 160), A("ps4", 0, 160), AF.Sign, bias=A("il", 16 + c, 17 + c), scale=-1.0, acc=SM(0, c, c + 1))
-        ts(SU(0), SM(0), 0.5, AL.mult, 80.0, AL.add)
-        ts(SM(1), SM(0), 8.0, AL.mult, 1280.0, AL.add)
-        tt(A("cmp"), IND(A("incl"), SU(0)), A("sw"), AL.is_le)
-        tolist("ps5", [("z1", "cmp")])
-        tt(SM(2), A("ps5", 0, 16), SM(1), AL.add)
-        cp(SU(1), SM(2))
-        bx = A("box", 256 * t, 256 * t + 256)
-        ts(bx, IND(A(q, 0, L + 16), SU(1)), 16.0, AL.add)
-        rc = A("rcv", 256 * t, 256 * t + 256)
+        act(A("incl", 0, 160), A("ps5", 0, 160))
+        mmg([(A("ps5", 336, 352), A("bd"), A("inc", 145, 161))])
+        b0 = 272 * t
+        act(A("box", b0 + 256, b0 + 272), A("ps5", 336, 352))
+        acc = A("ps4", 16, 32)
+        tolist(acc, [(z160, "cmp", 0)])
+        for u, tab, scale, top, z in ((0, "tb", 1.0 / 32, 80.0, z16), (1, "incl", 0.0625, 160.0, z1)):
+            ts(SU(u), acc, scale, AL.mult, top, AL.min)
+            act(SM(9 + u), acc)
+            mmg([(acc, A("idf"), SM(9 + u))], True, False)
+            tt(A("cmp", 256 * u + 256, 256 * u + 512), IND(A(tab), SU(u)), A("sw"), AL.is_le)
+            tolist(acc, [(z, "cmp", 256 * u + 256)], False)
+        ts(SU(2), acc, float(L), AL.min)
+        tt(SM(0), acc, SPQ, AL.min)
+        if t == 0:
+            act(A("box", b0, b0 + 256), IND(A("qq", 0, SP), SU(2)))
+        else:
+            act(A("box", b0, b0 + 256), IND(A("qb", 0, SP), SU(2)), AF.Relu, bias=7.0 - 1e-4, scale=-1.0 / 33)
+        bx, rc = A("box", b0, b0 + 272), A("rcv", b0, b0 + 272)
         op("g", [lambda e: e.remote_dma(rc[0], bx[0], T.sem["got%d" % t], T.sem["out%d" % t], dst[1], dst[0], msk[0])],
-           [bx], [(None, [("wire%d" % t, 0, 1, None)])], 500, lat=6000 - 1500 * t, sem="remote%d" % t, inc=len(msk[1]))
-        ts(A("own"), bx, -16.0, AL.add)
-        ts(SM(3), SM(2), L - 0.5, AL.is_gt)
-        tt(SM(3), SM(3), A("il", 48, 64), AL.mult)
-        tt(SM(3), SM(3), SM(2), AL.add)
-        cp(SU(2), SM(3))
+           [bx], [(None, [("wire%d" % t, 0, 1, None)])], 500, lat=RLAT[t], sem="remote%d" % t, inc=len(msk[1]))
+        ops[-1]["first"] = True
 
     def arrive(t, qn):
-        rc = (T["rcv"][:, 256 * t:256 * t + 256], [("wire%d" % t, 0, 1, None)], 256, BF)
-        op("v", [lambda e: e.tensor_tensor(T["nw"][:, 0:256], rc[0], T["own"][:, 0:256], AL.max)], [rc, A("own")], [A("nw")], 542)
-        ts(A("nh"), A("nw"), 15.5, AL.is_gt, -16.0, AL.mult)
-        tt(IND(A(qn), SU(2)), A("nw"), A("nh"), AL.add)
+        b0 = 272 * t
+        wire = [("wire%d" % t, 0, 1, None)]
+        ts(SM(1), IL, (T["rcv"][:, b0 + 271:b0 + 272], wire, 1, BF), AL.is_ge, 4096.0, AL.mult)
+        tt(SM(1), SM(1), SPQ, AL.min)
+        tt(SM(1), SM(1), SM(0), AL.max)
+        cp(SU(3), SM(1))
+        cp(IND(A(qn), SU(3)), (T["rcv"][:, b0:b0 + 256], wire, 256, BF))
 
-    def items(t, q, qn):
+    def items(t):
         for k in range(5):
             a, b = 512 * k, 512 * k + 512
-            pa, pb = "ps%d" % (2 * (k % 2)), "ps%d" % (1 + 2 * (k % 2))
-            (cp if VI[k] else act)(A("hh", a, b), IND(A("rct"), A("idx", a // 16, b // 16)))
-            two = lambda bank: [(A(bank), ID(1), A("hh", a, b)), (A(bank), ID(1), A(q, a, b))]
-            mmg(two(pa))
-            act(A("b1", a, b), A(pa), AF.Sign, bias=t - 15.5)
-            mmg(two(pb) + [(A(pb), ID(-8.0), A("b1", a, b))])
-            act(A(qn, a, b), A(pb), bias=t - 8.0)
+            pa, h, lim = A("ps%d" % (0, 2, 1, 3, 0)[k]), A("b1", a, b), -250.0 if t else -290.0
+            (cp if VI[t][k] else act)(A("hh", a, b), IND(A("rct"), A("idx", a // 16, b // 16)))
+            two = [(pa, ID(1.0), A("qb" if t else "qq", a, b)), (pa, ID(-33.0), A("hh", a, b))]
+            mmg(two)
+            if VH[t][k] == 2:
+                ts(h, pa, lim, AL.is_lt, 528.0, AL.mult)
+                tt(h if t else A("qb", a, b), pa, h, AL.add)
+                if t:
+                    ts(A("qa", a, b), h, 264.0, AL.subtract, -1.0 / 33, AL.mult)
+                continue
+            act(h, pa, AF.Sign, bias=lim, scale=-1.0)
+            mmg(two + [(pa, ID(264.0), h)])
+            if t:
+                act(A("qa", a, b), pa, scale=-1.0 / 33)
+            else:
+                act(A("qb", a, b), pa, bias=264.0)
 
-    def keys(s, ofs, wd):
+    def branch(s, banks, ofs, wd, r, gp, m, sel2):
         z = str(s)
-        act(A("kv" + z), IND(A("kt", 0, wd), ofs))
-        act(A("hv" + z), A("kv" + z), bias=HB - 7.5)
-        act(A("hn" + z), A("hv" + z), bias=-HB)
-        act(A("h17" + z), A("hn" + z), scale=1.0625)
-        tt(A("k0" + z), A("kv" + z), A("hn" + z), AL.subtract)
+        kv, hv, sb = A("kv" + z), A("hv" + z), A("sb" + z)
+        act(kv, IND(A("kt", 0, wd), ofs))
+        ts(hv, kv, HB - 7.5, AL.add)
+        lo, hi = A(banks[0], 0, 256), A(banks[0], 256, 512)
+        mmg([(lo, A("bda"), r), (lo, M("sk"), gp), (lo, A("bdb"), m)])
+        act(sb, lo, AF.Sign, bias=7.5)
+        mmg([(lo, ID(1.0), kv), (lo, ID(-1.0), hv), (lo, ID(-1.0), m), (lo, M("k1"), gp), (lo, ID(128.0), sb)], True, False)
+        mmg([(hi, a, b) for a, b in sel2] + [(hi, ID(128.0), sb)], False, True)
+        act(A("rp" + z), A(banks[0]), AF.Relu)
+        lo = A(banks[1], 0, 256)
+        rk = A("rp" + z, 0, 256)
+        mmg([(lo, ID(1.0), m), (lo, ID(16.0), kv), (lo, ID(-16.0), hv), (lo, ID(-15.0), rk), (lo, ID(120.0), sb)])
+        act(A("kn" + z), lo, bias=16 * HB + 120)
 
-    def branch(s, bank, r, gp, m):
+    def lowest(s, bank, sf, gp, n32, ok):
         z = str(s)
-        mmg([(A(bank, 0, 256), A("bda"), r), (A(bank, 0, 256), M("sk"), gp), (A(bank, 0, 256), A("bdb"), m)])
-        ts(A("bw" + z), A(bank, 0, 256), 8.5, AL.is_gt)
-        tt(A("gb" + z), gp, A("bw" + z), AL.mult)
-        mmg([(A(bank, 256, 512), ID(1), A("k0" + z)), (A(bank, 256, 512), ID(-1.0), m)])
-        tt(A("dd" + z), A(bank, 256, 512), A("bw" + z), AL.mult)
-        mmg([(A(bank, 0, 256), ID(1), m), (A(bank, 0, 256), ID(16.0), A("k0" + z)), (A(bank, 0, 256), ID(-15.0), A("dd" + z))])
-        act(A("kn" + z), A(bank, 0, 256))
-
-    def lowest(s, bank, gp, n32, far, base):
-        z = str(s)
-        tt(SM(base), far, n32, AL.add)
-        mmg([(A(bank, 0, 256), M("sf"), gp)])
-        cp(A("kw"), A(bank, 0, 256))
-        mmg([(A(bank, 256, 512), ID(1), A("nd" + z))], True, False)
+        mmg([(A(bank, 0, 256), M(sf), gp)])
+        ts(A("kw"), A(bank, 0, 256), -PH, AL.add)
+        mmg([(A(bank, 256, 272), A("lcw", 0, 128, p1=1), A("ones", 0, 16, p1=1))], True, False)
         for c in range(16):
-            ts(A("eq", 256 * c, 256 * c + 256 - 16 * c), A("kw", 16 * c, 256), SM(base, c, c + 1), AL.is_equal)
+            ts(A("eq", 256 * c, 256 * c + 256 - 16 * c), A("kw", 16 * c, 256), n32(c, c + 1), AL.is_equal, ok(c, c + 1), AL.mult)
             if c < 15:
                 mmg([(A(bank, 272 + 16 * c, 512), A("bd"), A("eq", 256 * c + 16, 256 * c + 256 - 16 * c))], False, False)
-        mmg([(A(bank, 256 + j, 512, 16), A("tl", 128 * j - 128, 128 * j), A("eq", j, 4096, 256)) for j in range(1, 16)], False, True)
-        act(A("ww" + z), A(bank, 256, 512), AF.Relu, bias=1.0, scale=-1.0)
-        tt(SM(base + 1), n32, A("il", 32, 48), AL.subtract)
-        tolist(bank, [("zs", "ww" + z)])
-        tt(SM(base + 2), A(bank, 0, 16), SM(base + 1), AL.mult)
-        tt(SM(base + 2), SM(base + 2), A("il", 32, 48), AL.add)
-        cp(SU(3 + s), SM(base + 2))
+        mmg([(A(bank, 256 + j, 512, 16), A("tl", 128 * j, 128 * j + 128), A("eq", j, 4096, 256)) for j in range(16)], False, True)
+        act(A("ww" + z), A(bank, 256, 512), AF.Relu, scale=-1.0)
+        tolist(A(bank, 0, 16), [(zs, "ww" + z, 0)], True, [(A(bank, 0, 16), A("idf"), n32(0, 16))])
+        tt(SM(2 + s), A(bank, 0, 16), SPN, AL.min)
+        ts(SU(4 + s), SM(2 + s), 8192.0 - (H if s < 2 else 0), AL.add)
 
-    def insert_pre(t, q):
-        G, Q = A("gp", 0, 256), A(q, 0, 256)
-        mmg([(A("ps7", 0, 256), A("bd"), A("b1", 0, 256)), (A("ps7", 0, 256), M("lf"), G)])
-        ts(A("nd0"), A("ps7", 0, 256), -63.5, AL.is_gt)
-        cp(SM(5), A("off", 0, 16))
-        ts(SM(6), A("idx", 0, 16), 1023.5, AL.is_gt, 8192.0, AL.mult)
-        keys(0, A("off", 0, 16), V + I * t)
-        branch(0, "ps6", A("rb", 0, 256), G, Q)
-        if t == 0:
+    def newkeys(s, bank, x):
+        z = str(s)
+        lo = A(bank, 0, 256)
+        mmg([(lo, ID(1.0625), A("hv" + z)), (lo, ID(264.0), A("ww" + z))])
+        act(A("kt", x, x + I), lo, AF.Relu, bias=-1.0625 * HB - 264)
+
+    def insert(t):
+        z = str(t)
+        G, x = A("gp", 0, 256), V + I * t
+        if t:
+            m = A("mq")
+            ts(m, A("qb", 0, 256), 231.0, AL.subtract, -1.0 / 33, AL.mult)
+            cp(A("v32", 0, 16), A("off", 0, 16))
+        else:
+            m = A("qa", 0, 256)
+            cp(A("v32", 0, 80), A("off", 0, 80))
             act(A("gz"), G)
-
-    def insert_post(t, q):
-        G, Q = A("gp", 0, 256), A(q, 0, 256)
-        x = V + I * t
+        ts(SM(5), A("idx", 0, 16), R - 0.5, AL.is_lt)
+        branch(t, ("ps6", "ps6"), A("off", 0, 16), x, A("rb", 0, 256), G, m, [(M("sl"), G)])
+        lowest(t, "ps7", "sfA", G, lambda a, b: A("v32", a, b), lambda a, b: SM(5, a, b))
         lo, hi = A("ps6", 0, 256), A("ps6", 256, 512)
-        lowest(0, "ps7", G, SM(5), SM(6), 7)
+        rk, rp, sb = A("rp" + z, 0, 256), A("rp" + z, 256, 512), A("sb" + z)
         if t == 0:
-            mmg([(hi, ID(1), Q), (hi, ID(32.0), A("k00")), (hi, ID(-31.0), A("dd0"))])
-            act(A("tn0"), hi, bias=HB)
-            tt(A("mk"), A("k00"), A("dd0"), AL.subtract)
-        mmg([(lo, M("n1"), G), (lo, M("n2"), A("gb0")), (lo, M("nx%d" % t), A("xb"))] + ([(lo, M("sum"), A("mk"))] if t == 0 else []))
-        act(A("pn0"), lo)
-        mmg([(hi, M("x1"), G)] + ([(hi, M("xx0"), A("xb"))] if t == 0 else []))
+            mmg([(hi, ID(1.0), A("kv0")), (hi, ID(-1.0), A("hv0")), (hi, ID(-1.0), rk), (hi, ID(8.0), sb)])
+            act(A("mk"), hi, bias=HB + 8)
+            mmg([(hi, ID(1.0), A("kn0")), (hi, ID(16.0), A("mk"))])
+            act(A("tn0"), hi, bias=CP)
+        mmg([(lo, M("n1"), G), (lo, M("n2"), rp), (lo, M("n3"), sb), (lo, M("nx0"), A("x0", I * t, I * t + I)), (lo, M("nx1"), A("x1"))]
+            + ([(lo, M("sum"), A("mk"))] if t == 0 else []))
+        act(A("pn" + z), lo)
+        mmg([(hi, M("x1"), G)] + ([(hi, M("xx0"), A("x0", 0, I)), (hi, M("xx1"), A("x1"))] if t == 0 else []))
         if t == 0:
-            cp(IND(A("tt"), SU(3)), A("tn0"))
-            act(A("tt", x, x + I), A("hn0"), bias=HB, scale=2.0625)
-        cp(IND(A("pt"), SU(3)), A("pn0"))
-        tt(A("pt", x, x + I), hi, A("ww0"), AL.mult)
-        cp(IND(A("kt"), SU(3)), A("kn0"))
-        tt(A("kt", x, x + I), A("h170"), A("ww0"), AL.mult)
-        if t == 0:
-            act(A("wz"), A("ww0"))
+            cp(IND(A("tt", H, 4096), SU(4)), A("tn0"))
+            act(A("tt", x, x + I), A("hv0"), bias=CPX, scale=2.0625)
+        cp(IND(A("pt", H, 4096), SU(4 + t)), A("pn" + z))
+        tt(A("pt", x, x + I), hi, A("ww" + z), AL.mult)
+        cp(IND(A("kt", H, 4096), SU(4 + t)), A("kn" + z))
+        newkeys(t, "ps7", x)
 
     def post_pre():
-        ts(A("thm"), A("mk"), 32.0, AL.mult, HB, AL.add)
-        act(A("qm"), A("mk"), bias=CP, scale=-33.0)
-        cp(SU(5), A("f32", 0, 16))
-        ts(SM(12), A("f32", 0, 16), -OFS, AL.add)
-        tt(A("cm3"), IND(A("tt", 0, V + I), SU(5)), A("thm"), AL.is_lt)
-        act(A("ge"), IND(A("pt", 0, V + I), SU(5)))
-        tolist("ps5", [("z8", "cm3"), ("zr", "ge")])
-        tt(SM(13), A("ps5", 0, 16), SM(12), AL.max)
-        ts(SM(14), SM(13), CR, AL.add, CR, AL.subtract)
-        tt(SM(13), SM(13), SM(14), AL.subtract)
-        ts(SU(6), SM(13), OFS, AL.add)
-        ts(SM(15), SM(13), OFS, AL.add)
-        tt(A("ru"), IND(A("tt", 0, V + I), SU(6)), A("qm"), AL.add)
-        act(A("gu"), IND(A("pt", 0, V + I), SU(6)))
-        keys(1, SU(6), V + I)
-        branch(1, "ps4", A("ru"), A("gu"), A("mk"))
+        wd = V + I
+        act(A("thm"), A("mk"), bias=CP, scale=32.0)
+        ts(A("qm"), A("mk"), -33.0, AL.mult, 231.0, AL.add)
+        cp(SU(7), A("la", 0, 16))
+        tt(A("cm3"), IND(A("tt", 0, wd), SU(7)), A("thm"), AL.is_lt)
+        act(A("ge"), IND(A("pt", 0, wd), SU(7)), AF.Relu, bias=GB, scale=GS)
+        tolist(A("ps5", 0, 16), [(zk, "cm3", 0), (zr, "ge", 0)])
+        tt(SM(6), A("ps5", 0, 16), A("la", 0, 16), AL.max)
+        ts(SM(7), SM(6), CR, AL.add, CR, AL.subtract)
+        tt(SM(6), SM(6), SM(7), AL.subtract)
+        cp(SU(8), SM(6))
+        gu, x0, x1 = A("gu"), A("x0", 0, I), A("x1")
+        tt(A("ru"), IND(A("tt", 0, wd), SU(8)), A("qm"), AL.add)
+        act(gu, IND(A("pt", 0, wd), SU(8)), AF.Relu, bias=GB, scale=GS)
+        branch(2, ("ps4", "ps4"), SU(8), wd, A("ru"), gu, A("mk"), [(M("sp"), gu), (M("xs0"), x0), (M("xs1"), x1)])
+        rp, sb = A("rp2", 256, 512), A("sb2")
         lo, hi = A("ps5", 0, 256), A("ps4", 256, 512)
-        mmg([(lo, M("c0"), A("gu")), (lo, M("cb"), A("gb1")), (lo, M("zz"), A("gz")), (lo, ID(-8192.0), A("wz"))])
-        ts(A("nd1"), lo, -8192.0, AL.not_equal)
-        tolist("ps4", [("z8", "nd1")])
-        lowest(1, "ps5", A("gu"), SM(15), A("ps4", 0, 16), 17)
-        tt(A("xbb"), A("xb"), A("bw1"), AL.mult)
+        mmg([(lo, M("t1"), gu), (lo, M("n2"), rp), (lo, M("n3"), sb), (lo, M("t4"), A("gz")), (lo, ID(-8192.0), A("ww0"))])
+        ts(A("cd"), lo, -8192.0, AL.is_equal)
+        tolist(A("ps5", 0, 16), [(z0, "cd", 0)])
+        act(SM(8), A("ps5", 0, 16))
+        lowest(2, "ps5", "sfS", gu, lambda a, b: SM(6, a, b), lambda a, b: SM(8, a, b))
         lo = A("ps4", 0, 256)
-        mmg([(lo, M("p1"), A("gu")), (lo, M("p2"), A("gb1")), (lo, M("p3"), A("xb")), (lo, M("p4"), A("xbb"))])
-        act(A("pn1"), lo)
-        mmg([(hi, M("x1"), A("gu")), (hi, M("q2"), A("gb1")), (hi, M("q3"), A("xbb"))])
+        mmg([(lo, M("p1"), gu), (lo, M("p2"), rp), (lo, M("n3"), sb), (lo, M("e2"), x0), (lo, M("e2"), x1),
+             (lo, M("nx0"), A("x0", 2 * I, 3 * I)), (lo, M("nx0"), x1)])
+        act(A("pn2"), lo)
+        mmg([(hi, M("x1"), gu), (hi, M("q2"), rp), (hi, M("q3"), sb), (hi, M("q3"), A("ones"))])
         x = V + 2 * I
-        tt(A("pt", x, x + I), hi, A("ww1"), AL.mult)
-        tt(A("kt", x, x + I), A("h171"), A("ww1"), AL.mult)
-        cp(IND(A("kt"), SU(4)), A("kn1"))
+        tt(A("pt", x, x + I), hi, A("ww2"), AL.mult)
+        cp(IND(A("kt"), SU(6)), A("kn2"))
+        newkeys(2, "ps5", x)
 
     def restart_pre():
+        cp(A("v32", 80, 160), A("off", 80, 160))
         for X in (0, 1):
             c = 80 * X
             pl = "ps%d" % (2 + X)
-            ft, ht = A("ft", 128 * X, 128 * X + 128, p1=80), A("ht", 128 * X, 128 * X + 128, p1=80)
-            ts(ht, ft, CR, AL.add, CR, AL.subtract)
-            mmg([(A(pl, 0, 80), ft, A("idf", 0, 80, p1=80)), (A(pl, 0, 80), ht, ID(-1.0, 80))])
-            act(A("f32", c, c + 80), A(pl, 0, 80), bias=OFS)
-        cp(A("v32"), A("off"))
-        ts(A("dn"), A("idx"), 1023.5, AL.is_lt)
-        tt(A("la"), A("f32"), A("v32"), AL.subtract)
-        tt(A("la"), A("la"), A("dn"), AL.mult)
-        tt(A("la"), A("la"), A("v32"), AL.add)
-        ts(A("sl"), A("incl", 0, 160), 256.5, AL.is_lt)
-        tt(A("sl"), A("sl"), A("ovl"), AL.mult)
-        act(A("dn"), A("sl"), bias=1.0, scale=-1.0)
-        tt(A("la"), A("la"), A("dn"), AL.mult)
+            unround(pl, X, turned("ft", X), [turned("xa", X, 512, 256, 384)])
+            tt(A("la", c, c + 80), A(pl, 0, 80), A("v32", c, c + 80), AL.min)
+        sp = A("ps5", 160, 320)
+        mmg([(sp, A("tri"), A("ovl")), (sp, A("bd"), A("inc", 0, 160)), (sp, ID(-8192.0), A("ovl"))])
+        ts(A("sl"), sp, 256.5 - 8192, AL.is_lt, 1024.0, AL.mult)
+        tt(A("lb"), A("la"), A("sl"), AL.max)
 
     def restart():
         for X in (0, 1):
             c = 80 * X
             pl = "ps%d" % (2 + X)
             sums("qb", X, 3)
-            act(A("hs", 256 * X, 256 * X + 256, p1=80), A("ps%d" % X, 128, 384, p1=80))
-            mmg([(A(pl, 0, 80), A("hs", 256 * X + 128 * u, 256 * X + 128 * u + 128, p1=80), A("idf", 0, 80, p1=80)) for u in (0, 1)])
-            cp(A("li", c, c + 80), A(pl, 0, 80))
-            ts(A("li", c, c + 80), A("li", c, c + 80), H - 1, AL.bitwise_and)
-            tt(A("lb", c, c + 80), A("li", c, c + 80), A("sl", c, c + 80), AL.mult)
-            tt(A("lb", c, c + 80), A("lb", c, c + 80), A("la", c, c + 80), AL.add)
-            cp(A("off", c, c + 80), A("lb", c, c + 80))
+            act(turned("hs", X, 256), A("ps%d" % X, 128, 384, p1=80))
+            mmg([(A(pl, 0, 80), turned("hs", X, 256, 128 * u, 128 * u + 128), A("idf", 0, 80, p1=80)) for u in (0, 1)]
+                + [(A(pl, 0, 80), ID(-8192.0), A("sl", c, c + 80))])
+            ts(A("li", c, c + 80), A(pl, 0, 80), HC, AL.add)
+            ts(A("li", c, c + 80), A("li", c, c + 80), 2 ** 23 + H - 1, AL.bitwise_and)
+            tt(A("lh", c, c + 80), A("li", c, c + 80), A("lb", c, c + 80), AL.min)
+            cp(A("off", c, c + 80), A("lh", c, c + 80))
 
     looks(0)
     ops[late[0]]["aft"].append(late[1])
-    insert_pre(0, "qa")
-    slots(0, "qa")
-    insert_post(0, "qa")
+    slots(0)
+    insert(0)
     restart_pre()
-    items(0, "qa", "qb")
-    ms(A("rct", R, R + 16), -1.0)
-    post_pre()
+    items(0)
     arrive(0, "qb")
     restart()
+    post_pre()
+    posted += list(range(len(ops) - 4, len(ops)))
     looks(1)
-    insert_pre(1, "qb")
-    slots(1, "qb")
-    cp(IND(A("pt"), SU(4)), A("pn1"))
-    insert_post(1, "qb")
-    items(1, "qb", "qa")
+    slots(1)
+    cp(IND(A("pt"), SU(6)), A("pn2"))
+    insert(1)
+    items(1)
     arrive(1, "qa")
-    dma("y", D("yk", 0, 1920), A("kt", 0, 1920), 500000)
-    dma("s", D("yk", 1920, W), A("kt", 1920, W), 500000)
-    for n, r in (("y0", rC0), ("y1", rC1), ("yr", rR)):
+    dma("y", D("yk", 0, H), A("kt", 0, H), 262144)
+    dma("y", D("yk", H, W), A("kt", H, W), 720896)
+    dma("y", D("y0", 0, H), A("pt", 0, H, p0=rA, ps=16), 32768)
+    dma("y", D("y0", H, W), A("pt", H, W, p0=rS, ps=16), 90112)
+    for n, r in (("y1", rC), ("yr", rR)):
         dma("y", D(n), A("pt", 0, W, p0=r, ps=16), 122880)
-    dma("y", D("yq", 0, HL), A("qa", 0, HL), 330000)
-    dma("s", D("yq", HL, L), A("qa", HL, L), 330000)
+    dma("y", D("yq"), A("qa", 0, L), 655360)
     return ops
 
 
@@ -617,75 +731,123 @@ def depend(ops):
     return deps
 
 
-def place(ops, pred, gap, key):
-    n = len(ops)
-    succ = [[] for _ in ops]
-    for k, d in enumerate(pred):
-        for j in d:
-            succ[j].append(k)
+def place(eng, cost, pred, succ, first, key):
+    n = len(cost)
     left = [len(d) for d in pred]
-    ready = [k for k in range(n) if left[k] == 0]
-    start = [0.0] * n
-    busy = {}
+    ready = [(key[k], k) for k in range(n) if left[k] == 0]
+    end = [0.0] * n
+    busy = {e: [] for e in eng}
     while ready:
-        k = min(ready, key=lambda j: key[j])
-        ready.remove(k)
-        s = max([start[j] + gap(j, k) for j in pred[k]] + [gap(None, k)])
-        c = ops[k]["cost"]
-        line = busy.setdefault(ops[k]["eng"], [])
+        x = min(ready)
+        ready.remove(x)
+        k = x[1]
+        s = first[k]
+        for j, lag in pred[k]:
+            if end[j] + lag > s:
+                s = end[j] + lag
+        c = cost[k]
+        line = busy[eng[k]]
         at = len(line)
         while at > 0 and line[at - 1][1] > s:
             at -= 1
         while at < len(line) and line[at][0] < s + c:
-            s = max(s, line[at][1])
+            if line[at][1] > s:
+                s = line[at][1]
             at += 1
         line.insert(at, (s, s + c))
-        start[k] = s
-        for j in succ[k]:
+        end[k] = s + c
+        for j, lag in succ[k]:
             left[j] -= 1
             if left[j] == 0:
-                ready.append(j)
-    return start
+                ready.append((key[j], j))
+    return end
+
+
+def replay(seq, eng, cost, pred, tail, more):
+    end, free, last = [0.0] * len(cost), {e: 0.0 for e in eng}, 0.0
+    for k in seq:
+        s = free[eng[k]]
+        for j, lag in pred[k]:
+            x = end[j] + (lag + more if lag > 0 else 0.0)
+            if x > s:
+                s = x
+        end[k] = free[eng[k]] = s + cost[k]
+        if end[k] + tail[k] > last:
+            last = end[k] + tail[k]
+    return last
 
 
 def order(ops, deps):
     n = len(ops)
-    pred = [sorted(set(d) | set(o["aft"])) for d, o in zip(deps, ops)]
-    succ = [[] for _ in ops]
-    for k, d in enumerate(pred):
-        for j in d:
-            succ[j].append(k)
+    eng, cost, tail = [o["eng"] for o in ops], [o["cost"] for o in ops], [o["lat"] for o in ops]
 
     def lag(j, k):
         a, b = ops[j], ops[k]
         if j not in deps[k]:
             return 0.0
         if a["eng"] == b["eng"] and a["sem"] is None:
-            return 0.0 if a["eng"] == "p" else 45.0
+            return SAME.get(a["eng"], 45.0)
         return a["lat"] + 140.0
+    full = [{j: lag(j, k) for j in set(deps[k]) | set(ops[k]["aft"])} for k in range(n)]
+    pred = [[(j, x) for j, x in d.items() if not any(j in full[i] and full[i][j] + cost[i] + y >= x + 300.0 for i, y in d.items())] for d in full]
+    succ = [[] for _ in ops]
+    for k, d in enumerate(pred):
+        for j, x in d:
+            succ[j].append((k, x))
+    others = [[c * f.get(o["kind"], 1.0) for c, o in zip(cost, ops)] for f, more in CASES]
+    zero = [0.0] * n
+    state = [SEED]
 
-    def fw(j, k):
-        return 0.0 if j is None else ops[j]["cost"] + lag(j, k)
-
-    def bw(j, k):
-        return ops[k]["lat"] if j is None else ops[j]["cost"] + lag(k, j)
-    pr = place([dict(o, eng=k) for k, o in enumerate(ops)], succ, bw, [0.0] * n)
-    key = [-(pr[k] + ops[k]["cost"]) for k in range(n)]
-    best, state = None, SEED
-    for _ in range(TRIES):
-        st = place(ops, pred, fw, key)
-        back = place(ops, succ, bw, [-(st[k] + ops[k]["cost"] + ops[k]["lat"]) for k in range(n)])
-        st = place(ops, pred, fw, [-(back[k] + ops[k]["cost"]) for k in range(n)])
-        end = max(st[k] + ops[k]["cost"] + ops[k]["lat"] for k in range(n))
-        if best is None or end <= best[1]:
-            best = (st, end)
-        state = (state * 1103515245 + 12345) % 2147483648
-        mid, amp = best[1] * (state >> 8) / 8388608.0, AMP * (1 + (state >> 4) % 4)
-        key = []
-        for k in range(n):
-            state = (state * 1103515245 + 12345) % 2147483648
-            key.append(best[0][k] + (amp * (state >> 8) / 8388608.0 if abs(best[0][k] - mid) < 12000.0 else 0.0))
-    return sorted([(k, best[0][k]) for k in range(n)], key=lambda x: x[1]), best[1]
+    def draw():
+        state[0] = (state[0] * 1103515245 + 12345) % 2147483648
+        return (state[0] >> 8) / 8388608.0
+    key = [-x for x in place(list(range(n)), cost, succ, pred, tail, zero)]
+    best = cur = None
+    for it in range(TRIES):
+        end = place(eng, cost, pred, succ, zero, key)
+        if it % 50 == 0:
+            back = place(eng, cost, succ, pred, tail, [-(a + b) for a, b in zip(end, tail)])
+            end = place(eng, cost, pred, succ, zero, [-x for x in back])
+        last = max(a + b for a, b in zip(end, tail))
+        slack = AMP * (1.0 - it / TRIES) * draw()
+        if cur is None or last <= cur[1] + 1000.0 + slack:
+            st = [a - b for a, b in zip(end, cost)]
+            seq = [k for x, k in sorted(zip(st, range(n)))]
+            total = last + sum(replay(seq, eng, c, pred, tail, m[1]) for c, m in zip(others, CASES))
+            if cur is None or total <= cur[2] + slack:
+                before, prev, pairs = {}, {}, []
+                for k in seq:
+                    before[k] = prev.get(eng[k])
+                    prev[eng[k]] = k
+                k = max(zip([a + b for a, b in zip(end, tail)], range(n)))[1]
+                while st[k] > 0.5:
+                    ways = [j for j, x in pred[k] if end[j] + x > st[k] - 0.5]
+                    if not ways:
+                        pairs.append((before[k], k))
+                    k = ways[0] if ways else before[k]
+                cur = (st, last, total, pairs)
+                if best is None or total <= best[2]:
+                    best = cur
+        key = list(cur[0])
+        j, k = cur[3][int(draw() * len(cur[3]))]
+        if draw() < 0.5:
+            key[j] = key[k] + 1.0 + 2000.0 * draw() ** 3
+        else:
+            shift, todo, t0 = key[k] - key[j] + 1.0 + 2000.0 * draw() ** 3, [k], key[j]
+            seen = {k}
+            while todo:
+                i = todo.pop()
+                key[i] -= shift
+                for a, x in pred[i]:
+                    if a not in seen and key[a] > t0 - 1500.0:
+                        seen.add(a)
+                        todo.append(a)
+    _PLAN["total"] = best[2] / (1 + len(CASES))
+    st = list(best[0])
+    for k in range(n):
+        if "alias" in ops[k] and ops[k - 1]["eng"] == "y":
+            st[k - 1] = st[k] - 1.0
+    return sorted([(k, st[k]) for k in range(n)], key=lambda x: x[1]), best[1]
 
 
 def rank_program(g, core, T, topo):
@@ -707,6 +869,9 @@ def rank_program(g, core, T, topo):
     known = {e: {} for e in eng}
     for k, _s in _PLAN["seq"]:
         o = ops[k]
+        if "alias" in o:
+            mark[k], clock[k] = mark[o["alias"]], clock[o["alias"]]
+            continue
         e = o["eng"]
         kn = known[e]
         for j in sorted(deps[k], key=lambda j: -mark[j][2]):

@@ -14,19 +14,22 @@ SP = L + 16
 rA, rC, rK, rN, rL, rR, rS, rO, rP, rI = 0, 2, 4, 5, 6, 8, 10, 12, 13, 14
 
 N1, NG = 1024, 896
-VB = (896, 800)
-SLOT = ((1, "g0"), (1, "gpa"), (0, "rbm"), (0, "b1m"), (0, "relu"), (0, "max"), (0, "rnd"), (0, "ft"), (1, "gpb"), (1, "g1"),
-        (1, "gpm"), (0, "off"), (1, "bs"), (1, "bv"))
-LAST = ((1, "g0"), (1, "gpa"), (0, "rbm"), (0, "b1m"), (0, "relu"), (1, "gpb"), (0, "rnd"), (1, "g1"), (0, "off"), (1, "gpm"), (1, "bs"),
-        (1, "bv"), (1, "rbm"), (1, "b1m"))
-TLV = 8
+VB = (256, 768, 768, 768, 512, 640, 640, 640, 640, 512)
+SLOT = ((1, "g0"), (1, "gpa"), (0, "rbm"), (0, "b1m"), (0, "w0m"), (0, "relu"), (0, "max"), (0, "rnd"), (1, "gpb"), (1, "g1"),
+        (1, "gpm"), (0, "off"), (0, "ft"), (1, "bs"), (1, "bv"))
+LAST = ((1, "g0"), (0, "rbm"), (0, "b1m"), (1, "g1"), (1, "bv"))
+TLV = 4
+W0P, PRS, HHS = False, True, ()
+RS = (False, False, False, False)
+IDV, MZ, PS = 20, True, False
+HVS = (0, 0, 0)
 TTV = (2, 3, 4)
 BONUS = 8000.0
 POSTBY = (1, 2, 0)
 VI = ((0, 0, 0, 0, 0), (0, 0, 0, 0, 0))
-VH = ((2, 2, 2, 2, 2), (2, 2, 2, 0, 0))
+VH = ((4, 0, 4, 4, 4), (0, 0, 2, 2, 2))
 
-IDW = (1.0, -1.0, 8.0, 16.0, -16.0, -15.0, 120.0, -33.0, 264.0, 128.0, -8192.0, 1.0625)
+IDW = (1.0, -1.0, 8.0, 16.0, -16.0, -15.0, 120.0, -33.0, 264.0, 128.0, -8192.0, 1.0625, 0.125, 0.5)
 SB = {
     "kt": ([128, 4096], BF), "tt": ([128, 4096], F32), "pt": ([128, 4096], F32), "hh": ([128, V], BF),
     "rct": ([128, 1040], BF), "qa": ([128, 2832], BF), "qb": ([128, 2832], BF), "qq": ([128, 2832], BF),
@@ -34,18 +37,18 @@ SB = {
     "cx": ([128, 1152], I32), "cf": ([128, 1152 + 192], F32), "lo": ([128, 512], F32),
     "v0i": ([128, 160], I32), "wti": ([128, 4], I32), "wcol": ([128, 4], F32), "wcb": ([128, 8], BF),
     "off": ([128, 160], U16), "idx": ([128, 160], U16),
-    "lc": ([128, 256], BF), "lcw": ([128, 256], BF), "xa": ([128, 1024], F32), "xt": ([128, 256], F32), "xr": ([128, 256], F32),
-    "ht": ([128, 256], BF), "ft": ([128, 256], F32), "hs": ([128, 512], F32), "ot": ([128, 256], BF),
-    "ones": ([128, 256], BF), "idf": ([128, 128], F32), "idn": ([128, 128], F32), "ids": ([128, 128 * len(IDW)], BF),
+    "lc": ([128, 256], BF), "lcw": ([128, 128 * len(set(VB))], BF), "xa": ([128, 1024], F32), "xt": ([128, 256], F32), "xr": ([128, 256], F32),
+    "ht": ([128, 256], BF), "ft": ([128, 256], F32), "hs": ([128, 512], F32), "ot": ([128, 256], BF), "crb": ([128, 160], BF),
+    "ones": ([128, 256], BF), "idf": ([128, 128], F32), "idc": ([128, 80], F32), "ids": ([128, 128 * len(IDW)], BF),
     "bd8": ([128, 8], BF), "bd": ([128, 128], BF), "bda": ([128, 128], BF), "bdb": ([128, 128], BF), "tri": ([128, 128], BF),
     "zz": ([128, 144 * 7], BF), "col": ([128, 64], F32),
     "wm": ([128, 128], BF), "wl": ([128, 32], BF), "wr": ([128, 8], BF), "wb": ([128, 16], BF), "wq": ([128, 24], BF),
-    "mm": ([128, 128 * 24], BF), "tl": ([128, 128 * 16], BF), "eq": ([128, 4096], BF), "kw": ([128, 256], U16),
+    "mm": ([128, 128 * 20], BF), "tl": ([128, 128 * 16], BF), "eq": ([128, 4096], BF), "kw": ([128, 256], U16),
     "pi": ([128, 4], I32), "pc": ([128, 24], F32), "pb": ([128, 2], BF), "sw": ([128, 256], BF),
-    "x0": ([128, 768], BF), "x1": ([128, 256], BF), "il": ([128, 64], F32),
+    "x0": ([128, 768], BF), "x1": ([128, 256], BF), "il": ([128, 80], F32),
     "ovl": ([128, 160], BF), "inc": ([128, 176], BF), "incl": ([128, 176], F32), "tb": ([128, 96], F32), "junk": ([128, 64], F32),
     "sm": ([128, 16 * 24], F32), "su": ([128, 16 * 12], U16),
-    "cmp": ([128, 768], BF), "box": ([128, 544], BF), "rcv": ([128, 544], BF),
+    "sa": ([128, 48], BF), "xn": ([128, 256], BF), "cmp": ([128, 768], BF), "box": ([128, 544], BF), "rcv": ([128, 544], BF),
     "v32": ([128, 160], F32), "sl": ([128, 160], BF), "la": ([128, 160], F32), "lb": ([128, 160], F32), "lh": ([128, 160], F32),
     "li": ([128, 160], I32),
     "gz": ([128, 256], BF), "mk": ([128, 256], BF), "thm": ([128, 256], F32), "qm": ([128, 256], BF), "mq": ([128, 256], BF),
@@ -60,11 +63,13 @@ for _k in range(8):
     SCRATCH["ps%d" % _k] = ("psum", [128, 512], F32)
 SEMAPHORES = ["sv", "ss", "sp", "sg", "got0", "got1", "out0", "out1"] + ["d%d" % k for k in range(44)]
 
-GC, SC, PEC = 1.7, 3.8, 0.55
+GT, VF, SF = 1.9, 45.0, 70.0
+GC, SC, PEC = 1.6, 3.8, 0.51
 DROW, DBW, DLAT, RLAT = 300.0, 400.0, 700.0, (3500.0, 2500.0)
-TRIES, SEED, AMP = 5000, 1, 600.0
-SAME = {"p": 0.0, "g": 120.0}
-CASES = (({"sg": 0.75, "vg": 0.8, "vs": 0.6, "g": 1.3, "p": 1.1, "d": 1.3}, 60.0), ({"sg": 1.2, "vs": 1.4, "p": 0.9, "d": 0.7}, 0.0))
+TRIES, SEED, AMP, SHAKE = 19000, 2, 300.0, 0.3
+SAME = {"p": 0.0, "g": 200.0}
+GF = 60.0
+CASES = (({"sg": 0.72, "vs": 0.6, "g": 1.2, "d": 0.7, "p": 1.1}, 60.0), ({"sg": 1.27, "vg": 1.1, "vs": 1.3, "g": 1.1, "d": 1.1}, 60.0))
 HINT = "vsp"
 _PLAN = {}
 
@@ -98,11 +103,11 @@ def build(T, dst, msk):
         if len(out) == 5:
             return 60 + out[2] * SC
         if len(ins[0]) == 5:
-            return 60 + out[2] * (max(GC, 2.0) if two else GC)
+            return 60 + out[2] * (GT if two else GC)
         f = 0.5 if all(x[3] in (BF, U16) for x in [out] + ins) else 1.0
         if two and all(x[1][0][0] in SB for x in ins):
             f = 2.0
-        return 60 + max(64, out[2] * f)
+        return VF + max(64, out[2] * f)
 
     def split(out):
         if len(out) == 5:
@@ -125,14 +130,14 @@ def build(T, dst, msk):
         op("v", [lambda e: e.tensor_copy(out[0], a[0])], [a] + r, w, vcost(out, [a]))
 
     def ms(out, c):
-        op("v", [lambda e: e.memset(out[0], c)], [], [out], 60 + max(64, out[2] * (0.5 if out[3] == BF else 1)))
+        op("v", [lambda e: e.memset(out[0], c)], [], [out], VF + max(64, out[2] * (0.5 if out[3] == BF else 1)))
 
     def act(out, a, fn=AF.Identity, bias=0.0, scale=1.0, acc=None):
         if acc is None:
             f = lambda e: e.activation(out[0], a[0], fn, bias=val(bias), scale=val(scale))
         else:
             f = lambda e: e.activation(out[0], a[0], fn, bias=val(bias), scale=val(scale), accum_out=acc[0])
-        op("s", [f], [a, bias, scale], [out] + ([acc] if acc else []), 80 + out[2] * (GC if len(a) == 5 else 1.0))
+        op("s", [f], [a, bias, scale], [out] + ([acc] if acc else []), (24 if acc else 0) + (78 + out[2] * GC if len(a) == 5 else SF + max(32, out[2])))
 
     def mmg(items, start=True, stop=True, each=False):
         fns, rd, c = [], [], 0.0
@@ -158,31 +163,38 @@ def build(T, dst, msk):
             f = lambda e: e.iota(out[0], pat, base, cm)
         else:
             f = lambda e: e.iota(out[0], pat, base, cm, allow_small_or_imprecise_dtypes=True)
-        op("g", [f], [], [out], 130 + 2 * out[2])
+        op("g", [f], [], [out], GF + 160 + 2 * out[2])
 
     def sel(out, a, pat, cmpop, fill, base, cm):
-        op("g", [lambda e: e.affine_select(out[0], a[0], pat, cmpop, fill, base, cm)], [a], [out], 170 + 2 * out[2])
+        op("g", [lambda e: e.affine_select(out[0], a[0], pat, cmpop, fill, base, cm)], [a], [out], GF + 210 + 2 * out[2])
 
     def put(n, a, b, s, row, w, pat=None, tag=None):
         x = A(n, a, b, s, tag=tag)
         sel(x, x, pat or [[-16, 8]], AL.not_equal, float(w), -row, 1)
 
-    for k in range(3):
-        dma("s" if k == 0 else "y", A("kt", 1024 * k, 1024 * k + 1024), D("kk", 1024 * k, 1024 * k + 1024), 262144)
+    dma("y", A("kt", 0, H), D("kk", 0, H), 262144)
+    dma("y", A("kt", H, V), D("kk", H, V), 524288)
     dma("y", A("cx", 0, 64), D("c0", 0, H), 32768)
-    dma("s", A("cx", 192, 384), D("c1"), 98304)
-    dma("y", A("cx", 384, 576), D("rt"), 98304)
-    dma("s", A("cx", 64, 192), D("c0", H, V), 65536)
+    dma("s", A("cx", 64, 256), D("c1"), 98304)
+    dma("s", A("cx", 256, 448), D("rt"), 98304)
+    dma("y", A("cx", 896, 1024), D("c0", H, V), 65536)
     dma("y", A("v0i"), D("v0"), 81920)
     dma("y", A("qa", 0, HL), D("qs", 0, HL), 327680)
     dma("y", A("qa", HL, L), D("qs", HL, L), 327680)
     dma("y", A("wti", 0, 1), D("wt"), 512)
 
-    iota(A("pt", 0, 512), [[1, 512]], 0, 0)
+    iota(A("pt", 0, 128), [[1, 128]], 0, 0)
+    for k in (128, 256):
+        ts(A("pt", k, 2 * k), A("pt", 0, k), float(k), AL.add)
     ts(A("pt", 512, 1024), A("pt", 0, 512), 512.0, AL.add)
     act(A("pt", 1024, 2048), A("pt", 0, 1024), bias=1024.0)
-    ts(A("pt", 2048, V), A("pt", 0, 1024), 2048.0, AL.add)
-    iota(A("lo", p1=32), [[0, 16], [1, 32]], 0, 0)
+    if PRS:
+        act(A("pt", 2048, V), A("pt", 0, 1024), bias=2048.0)
+    else:
+        ts(A("pt", 2048, V), A("pt", 0, 1024), 2048.0, AL.add)
+    iota(A("lo", 0, 64, p1=32), [[0, 2], [1, 32]], 0, 0)
+    for k in (64, 128, 256):
+        act(A("lo", k, 2 * k, p1=32), A("lo", 0, k, p1=32))
     ms(A("ones"), 1.0)
     ms(A("wm", 0, 32), 0.0)
     iota(A("wl"), [[0, 32]], 0, 0)
@@ -218,13 +230,16 @@ def build(T, dst, msk):
         if j is None:
             return A("zz", 144 * k + 15, 144 * k + 143, 16)
         return A("zz", 144 * k + 15 - j, 144 * k + 143 - j)
-    z1, z16, z160, zs, zk, zr, z0 = range(7)
+    z1, za, z16, zs, zk, zr, z0 = range(7)
     act(Z(z1), A("bd8"))
     act(A("wr"), A("bd8"), scale=-1024.0)
     act(A("wb", 0, 8), A("bd8"), scale=U2 / 2)
     act(A("wb", 8, 16), A("bd8"), scale=U2 / 2)
     act(A("wq", 0, 8), A("bd8"))
     act(A("idf"), A("ids", 0, 128))
+    if RS[0] or RS[1] or RS[3]:
+        sel(A("idc"), A("idf", 0, 80), [[0, 80]], AL.not_equal, -CR, -80, 1)
+        ms(A("xr"), 1.0)
 
     def ID(w, n=128):
         k = IDW.index(w)
@@ -234,39 +249,50 @@ def build(T, dst, msk):
     def ids(*ws):
         for w in ws:
             made.append(w)
-            sel(ID(w), ID(1.0), [[-1, 128]], AL.not_equal, w, 0, 1)
+            if len(made) <= IDV:
+                ts(ID(w), ID(1.0), w, AL.mult)
+            else:
+                sel(ID(w), ID(1.0), [[-1, 128]], AL.not_equal, w, 0, 1)
     for u in (0, 1):
         put("wm", 0, 32, 1, u, 1, [[-8, 2], [-2, 2], [-16, 8]])
         put("wm", 8, 24, 1, rA + u, -1, [[0, 2], [-16, 8]])
-    for w, r, x in ((0, rO, -PH), (1, rK, 32768), (2, rO, -U2 / 2), (3, rO, -PH), (1, rO, -216 * 16384), (2, rN, -2 ** 23), (3, rL, -65536),
+    put("wm", 0, 32, 1, rO, -PH, [[0, 4], [-16, 8]])
+    for w, r, x in ((1, rK, 32768), (2, rO, -U2 / 2), (3, rL, -65536), (1, rO, -216 * 16384), (2, rN, -2 ** 23),
                     (1, rP, -8192), (1, rL, -2 ** 19)):
         put("wm", 8 * w, 8 * w + 8, 1, r, x)
+    act(Z(za), A("wm", 0, 8))
     for k in (1, 2, 3):
         act(A("wm", 32 * k, 32 * k + 32), A("wm", 0, 32))
         put("wm", 32 * k + 24, 32 * k + 32, 1, rP, 8192 * k)
     ms(A("lcw"), 0.0)
-    for t in (0, 1):
-        x = A("lcw", 128 * t, 128 * t + 128)
-        sel(x, x, [[0, 128]], AL.is_gt, -8 * U2, VB[t] // 16, -1)
+    cuts = sorted(set(VB))
+    for u, nv in enumerate(cuts):
+        x = A("lcw", 128 * u, 128 * u + 128)
+        sel(x, x, [[0, 128]], AL.is_gt, -8 * U2, nv // 16, -1)
 
     def row(r, a, b, src):
         dma("y", A("pt", a, b, p0=r, ps=16, tag=r), src, 32 * (b - a))
     for u in (0, 1):
-        o = 576 * u
+        o = 448 * u
         if u:
-            ts(A("cx", 576, 1152), A("cx", 0, 576), 31, AL.bitwise_and)
-        cp(A("cf", o, o + 576), A("cx", o, o + 576))
+            ts(A("cx", 448, 896), A("cx", 0, 448), 31, AL.bitwise_and)
+        cp(A("cf", o, o + 448), A("cx", o, o + 448))
         row(rA + u, 0, H, A("cf", o, o + 64))
-        row(rC + u, 0, V, A("cf", o + 192, o + 384))
-        row(rR + u, 0, V, A("cf", o + 384, o + 576))
+        row(rC + u, 0, V, A("cf", o + 64, o + 256))
+        row(rR + u, 0, V, A("cf", o + 256, o + 448))
         if not u:
-            row(rN, 0, V, A("cf", 384, 576))
+            row(rN, 0, V, A("cf", 256, 448))
             row(rS + 1, 0, H, A("lo", p1=16))
+    ts(A("cx", 1024, 1152), A("cx", 896, 1024), 31, AL.bitwise_and)
+    cp(A("cf", 896, 1152), A("cx", 896, 1152))
     for u in (0, 1):
-        row(rS + u, H, V, A("cf", 576 * u + 64, 576 * u + 192))
+        row(rS + u, H, V, A("cf", 896 + 128 * u, 1024 + 128 * u))
     row(rA + 1, H, V, A("lo", p1=32))
     for k in range(3):
-        ts(A("hh", 1024 * k, 1024 * k + 1024), A("kt", 1024 * k, 1024 * k + 1024), HB - 7.5, AL.add)
+        if k in HHS:
+            act(A("hh", 1024 * k, 1024 * k + 1024), A("kt", 1024 * k, 1024 * k + 1024), bias=HB - 7.5)
+        else:
+            ts(A("hh", 1024 * k, 1024 * k + 1024), A("kt", 1024 * k, 1024 * k + 1024), HB - 7.5, AL.add)
     for a, n, bank, c in ((0, 64, "ps4", 0), (1024, 128, "ps3", 64)):
         mmg([(A(bank, 0, n), Z(z1, s), A("hh", a + n * s, a + n * s + n)) for s in range(16)])
         src = A("cf", 1152 + c, 1152 + c + n)
@@ -301,14 +327,22 @@ def build(T, dst, msk):
     for w, r, x in ((0, rO, -PH), (1, rK, 32768), (1, rO, -216 * 16384), (1, rP, -8192), (2, rO, -U2 / 2), (2, rI, 2 ** 22),
                     (3, rO, -65 * 2 ** 17), (3, rN, 2 ** 23)):
         put("wl", 8 * w, 8 * w + 8, 1, r, x)
-    ids(*[w for w in IDW if w not in made])
-    for k in range(6):
-        iota(A("mm", 512 * k, 512 * k + 512), [[0, 512]], 0, 0)
+    ids(*[w for w in IDW if w not in made and (w != 0.125 or 6 in VH[0] + VH[1]) and (w != 0.5 or RS[2] or PS)])
+    if RS[2]:
+        sel(A("crb", 80, 160, p1=1), A("ones", 0, 80, p1=1), [[0, 80]], AL.is_gt, 0.5, 0, 0)
+    if MZ:
+        ms(A("eq", 0, 640), 0.0)
+        for k in range(4):
+            dma("y", A("mm", 640 * k, 640 * k + 640), A("eq", 0, 640), 163840)
+    else:
+        for k in range(5):
+            iota(A("mm", 512 * k, 512 * k + 512), [[0, 512]], 0, 0)
     sel(A("bd"), A("ones", 0, 128), [[-16, 8], [0, 16]], AL.is_ge, 0.0, 0, 1)
     sel(A("bd"), A("bd"), [[16, 8], [0, 16]], AL.is_ge, 0.0, 15, -1)
     sel(A("tri"), A("bd"), [[1, 128]], AL.is_ge, 0.0, 0, -1)
     iota(A("sw"), [[1, 256]], 0, 0)
-    iota(A("x0"), [[32, 24], [0, 32]], V, 0)
+    for k in range(3):
+        iota(A("x0", I * k, I * k + I), [[32, 8], [0, 32]], V + I * k, 0)
     iota(A("x1"), [[0, 8], [1, 32]], 0, 0)
     ts(A("junk", 0, 16), A("sw", 0, 16), ROW, AL.is_gt)
     ts(A("junk", 16, 32), A("sw", 0, 16), ROW, AL.is_equal)
@@ -319,13 +353,13 @@ def build(T, dst, msk):
         else:
             act(A("tl", 128 * j, 128 * j + 128), A("bd"), scale=A("junk", 32 + j, 33 + j))
     iota(A("il", 48, 64), [[16, 16]], 0, 0)
-    MN = {"sum": 23}
+    MN = {"sum": 0}
 
     def M(name):
         return A("mm", 128 * MN[name], 128 * MN[name] + 128)
 
     def me(name, *ent):
-        MN[name] = len(MN) - 1
+        MN[name] = len(MN)
         b = 128 * MN[name]
         for rin, rout, w in ent:
             if rout is None:
@@ -339,12 +373,10 @@ def build(T, dst, msk):
         return [(rin, rout, 1), (rin + 1, rout, 1), (rO, rout, c)]
     me("sk", (rK, None, 2))
     CS, CS1, LI = (rC, rS), (rC + 1, rS + 1), (rL, rI)
-    me("k1", (rO, None, HB + 16 - 128))
     me("sfA", (rA, None, 1), (rA + 1, None, 1))
     me("sl", (rC, rC, 1 / 32), (rS, rC, -1 / 32), (rC + 1, rC + 1, 1), (rS + 1, rC + 1, -1))
-    me("n1", *(whole(rA, rA) + whole(rS, CS) + [(rA + 1, rA + 1, 1), (rS + 1, CS1, 1), (rP, rC, -2112), (rP, rC + 1, -64), (rO, LI, 2048)]))
-    me("n2", (rC, rC, 32), (rC + 1, rC, 1), (rC + 1, rC + 1, 1))
-    me("n3", (0, rC, -2112), (0, rC + 1, -64))
+    me("n1", *(whole(rA, rA) + whole(rS, CS) + [(rA + 1, rA + 1, 1), (rS + 1, CS1, 1), (rO, LI, 2048)]))
+    me("n2", (rC, rC, 32), (rC + 1, rC, 1), (rC + 1, rC + 1, 1), (0, rC, -33), (0, rC + 1, -1))
     me("nx0", (0, rR, 1))
     me("nx1", (0, rR, 1), (0, rR + 1, 1))
     me("x1", *(whole(rC, CS) + whole(rR, rR) + [(rC + 1, CS1, 1), (rR + 1, rR + 1, 1), (rK, rK, 1), (rN, rN, -1), (rO, LI, 2048)]))
@@ -355,23 +387,25 @@ def build(T, dst, msk):
     me("xs0", (0, rS, -1 / 32))
     me("xs1", (0, rS + 1, -1))
     me("t1", (rA, rC, 1), (rA + 1, rC, 1))
-    me("t4", (rA, rC, -1), (rA + 1, rC, -1), (rO, rC, -2112))
-    me("p1", *(whole(rA, rA) + [(rO, rC, -2112)]))
-    me("p2", (rS, rC, 32), (rS + 1, rC, 1))
+    me("p1", *whole(rA, rA))
+    me("p2", (rS, rC, 32), (rS + 1, rC, 1), (0, rC, -33))
     me("e2", (0, rC, 1))
-    me("q2", (rS, CS, -32), (rS + 1, CS, -1))
-    me("q3", (0, CS, 2112))
-    for r, w in ((rR, 1), (rR + 1, 1), (rO, -PH), (rP, -17 * 8192), (rN, -2 ** 23)):
+    me("q2", (rS, CS, -32), (rS + 1, CS, -1), (0, CS, 33))
+    for r, w in ((rR, 1), (rR + 1, 1), (rO, -PH), (rP, -8192 if PS else -17 * 8192), (rN, -2 ** 23)):
         put("zz", 144 * zr + 15, 144 * zr + 143, 16, r, w)
     put("zz", 144 * z0 + 15, 144 * z0 + 143, 16, rC, 1)
-    act(A("mm", 128 * 23 + rK, 128 * 24, 16), A("bd8"))
+    act(A("mm", rK, 128, 16), A("bd8"))
     act(A("bda"), A("bd"), scale=-0.0625)
     act(A("bdb"), A("bd"), scale=-2.0)
-    for z, w in ((z16, 16.0), (z160, 160.0), (zs, -512.0), (zk, 16384.0)):
+    for z, w in ((z16, 16.0), (zs, -512.0), (zk, 8192.0 if PS else 16384.0)):
         act(Z(z), A("bd8"), scale=w)
-    put("zz", 144 * z160 + 15, 144 * z160 + 143, 16, 15, 160 + 4096)
     IL, SPN, SPQ = A("il", 0, 16), A("il", 16, 32), A("il", 32, 48)
     act(IL, A("il", 48, 64), bias=ROW)
+    CPN, CPP = PC(9), PC(10)
+    if PS:
+        act(CPN, CP, bias=-240.0, scale=-1.0)
+        act(CPP, CP, bias=240.0)
+    act(A("il", 64, 80), IL, bias=0.5)
     act(SPN, IL, bias=W - 8192.0)
     act(SPQ, IL, bias=float(SP))
     ts(TBB, ROW, 9.5, AL.is_gt, 9999.0, AL.mult)
@@ -389,14 +423,20 @@ def build(T, dst, msk):
     iota(A("tb"), [[0, 96]], 9999, 0)
     late = [len(ops)]
     dma("y", A("rct", 0, R), D("rec"), 262144)
-    posted = []
+    posted, early = [], []
 
     def turned(n, X, w=128, a=0, b=None):
         return A(n, w * X + a, w * X + (w if b is None else b), p1=80)
 
-    def unround(pl, X, x, more):
+    def unround(pl, X, x, more, scalar=False):
         out, idf = A(pl, 0, 80), A("idf", 0, 80, p1=80)
-        mmg([(out, y, idf) for y in more], True, False)
+        if more:
+            mmg([(out, y, idf if y[3] == F32 else ID(1.0, 80)) for y in more], True, False)
+        if scalar:
+            act(turned("xr", X), x, bias=CR, scale=-1.0)
+            mmg([(out, x, idf)], False, False)
+            mmg([(out, A("xr", 128 * X, 128 * X + 128, p1=81), A("idc", p1=81))], False, True)
+            return
         ts(turned("ht", X), x, CR, AL.add, CR, AL.subtract)
         mmg([(out, x, idf)], False, False)
         mmg([(out, turned("ht", X), ID(-1.0, 80))], False, True)
@@ -415,41 +455,54 @@ def build(T, dst, msk):
             mk[name] = list(range(at[0], len(ops)))
             at[0] = len(ops)
         for a, b, name in ((0, N1, "g0"), (N1, HL, "g1")):
-            tt(A("rb", o + a, o + b), IND(A("tt", 0, wd), A("off", c + a // 16, c + b // 16)), A(q, o + a, o + b), AL.add)
+            if a < b:
+                tt(A("rb", o + a, o + b), IND(A("tt", 0, wd), A("off", c + a // 16, c + b // 16)), A(q, o + a, o + b), AL.add)
             done(name)
         for a, b, name in ((0, NG, "gpa"), (NG, HL, "gpb")):
-            act(A("gp", o + a, o + b), IND(A("pt", 0, wd), A("off", c + a // 16, c + b // 16)), AF.Relu, bias=GB, scale=GS)
+            if a < b:
+                act(A("gp", o + a, o + b), IND(A("pt", 0, wd), A("off", c + a // 16, c + b // 16)), AF.Relu, bias=GB, scale=GS)
             done(name)
-        nv = VB[t]
-        ts(A("b1", o + nv, o + HL), A("rb", o + nv, o + HL), THV, AL.is_lt, 2.0, AL.mult)
+        nv = VB[5 * t + k]
+        if nv < HL:
+            ts(A("b1", o + nv, o + HL), A("rb", o + nv, o + HL), THV, AL.is_lt, 2.0, AL.mult)
         done("bv")
         if nv:
             act(A("b1", o, o + nv), A("rb", o, o + nv), AF.Sign, bias=THS, scale=-1.0)
         done("bs")
         wp, w0 = ("wl", 0) if look else ("wm", 32 * k if fin else 0)
         nb = 2 if look else 1
-        for src, c0, c1, wt in (("gp", 0, 128 * nw, A(wp, w0, w0 + 8 * nw)), ("rb", 128, 256, A("wr")),
+        f = 0 if look or not W0P else 1
+        for src, c0, c1, wt in (("gp", 128 * f, 128 * nw, A(wp, w0 + 8 * f, w0 + 8 * nw)), ("rb", 128, 256, A("wr")),
                                 ("b1", 256, 256 + 128 * nb, A("wb", 0, 8 * nb))):
             for h in (0, 8):
                 mmg([(A(ps, c0 + j, c1, 16, p1=80), A(src, o + j, o + HL, 16), wt) for j in range(h, h + 8)],
                     src == "gp" and h == 0, src == "b1" and h == 8)
             if src == "gp":
                 mmg([(A(ps, 128, 256, p1=80), ID(1.0, 80), turned("lc", X))]
-                    + [(A(ps, 256 + 128 * u, 384 + 128 * u, p1=80), ID(1.0, 80), turned("lcw", t)) for u in range(nb)], False, False)
+                    + [(A(ps, 256 + 128 * u, 384 + 128 * u, p1=80), ID(1.0, 80), turned("lcw", cuts.index(nv))) for u in range(nb)], False, False)
             done(src + "m")
         if look:
-            ts(turned("ot", X), A(ps, 384, 512, p1=80), 0.0, AL.is_gt)
-            mmg([(A(pl, 128, 208), turned("ot", X), ID(1.0, 80))])
+            if RS[2]:
+                act(turned("ot", X), A(ps, 384, 512, p1=80), AF.Sign)
+                mmg([(A(pl, 128, 208), turned("ot", X), ID(0.5, 80)), (A(pl, 128, 208), A("ones", 0, 128, p1=1), A("crb", 80, 160, p1=1))])
+            else:
+                ts(turned("ot", X), A(ps, 384, 512, p1=80), 0.0, AL.is_gt)
+                mmg([(A(pl, 128, 208), turned("ot", X), ID(1.0, 80))])
             src, ini, out = A(pl, 128, 208), A("inc", c, c + 1), A("inc", c + 1, c + 81)
-            op("v", [lambda e: e.tensor_tensor_scan(out[0], T["ones"][:, 0:80], src[0], ini[0], AL.mult, AL.add)], [A("ones"), src, ini], [out], 140)
+            op("v", [lambda e: e.tensor_tensor_scan(out[0], T["ones"][:, 0:80], src[0], ini[0], AL.mult, AL.add)], [A("ones"), src, ini], [out], VF + 80)
             act(A("ovl", c, c + 80), src)
             done("over")
-        nr = 384 if look else 256
-        act(turned("xa", X, 512, 0, nr), A(ps, 0, nr, p1=80), AF.Relu)
+        if f:
+            for h in (0, 8):
+                mmg([(A(pl, 0, 80), Z(za, j), A("gp", o + j, o + HL, 16)) for j in range(h, h + 8)], h == 0, False)
+        done("w0m")
+        act(turned("xa", X, 512, 128 * f, 256), A(ps, 128 * f, 256, p1=80), AF.Relu)
+        if look:
+            act(turned("xn", X), A(ps, 256, 384, p1=80), AF.Relu)
         done("relu")
         if look:
             done("max")
-            unround(pl, X, turned("xa", X, 512, 128, 256), [turned("xa", X, 512, 0, 128), turned("xa", X, 512, 256, 384)])
+            unround(pl, X, turned("xa", X, 512, 128, 256), [turned("xa", X, 512, 0, 128), turned("xn", X)], RS[0])
             done("rnd")
             done("ft")
             ts(A("idx", c, c + 80), A(pl, 0, 80), float(R + t), AL.min)
@@ -457,7 +510,7 @@ def build(T, dst, msk):
             return mk
         tt(turned("xt", X), A(ps, 256, 384, p1=80), turned("xa", X, 512, 128, 256), AL.max)
         done("max")
-        unround(pl, X, turned("xt", X), [turned("xa", X, 512, 0, 128)])
+        unround(pl, X, turned("xt", X), [] if f else [turned("xa", X, 512, 0, 128)], RS[3])
         done("rnd")
         if fin:
             if k == 0:
@@ -496,22 +549,26 @@ def build(T, dst, msk):
         mmg([(out, Z(z, j), A(src, a + j, a + 256, 16)) for z, src, a in pairs for j in range(16)] + list(more), start, stop)
 
     def slots(t):
-        for h in (0, 8):
-            mmg([(A("ps4", 0, 1), Z(z1, r), A("inc", 10 * r + 10, 10 * r + 11)) for r in range(h, h + 8)], h == 0, h == 8)
-        ts(A("cmp", 0, 256), A("sw"), A("ps4", 0, 1), AL.is_ge)
+        b0 = 272 * t
+        acc, bnd = A("ps4", 16, 32), A("ps4", 0, 16)
+        mmg([(bnd, A("bd"), A("inc", 10, 161, 10))])
+        for c in range(16):
+            act(A("junk", 16 * (c % 4), 16 * (c % 4) + 16), bnd, AF.Sign, bias=A("il", 64 + c, 65 + c), scale=-1.0, acc=SM(9, c, c + 1))
+        act(A("box", b0 + 256, b0 + 272), bnd)
         mmg([(A("ps5", 320, 336), Z(z1, r), A("inc", 1 + r, 161, 10)) for r in range(10)])
         act(A("tb", 0, 80, 5), A("ps5", 320, 336), bias=TBB)
         mmg([(A("ps5", 0, 160), A("tri"), A("ovl")), (A("ps5", 0, 160), A("bd"), A("inc", 0, 160))])
         act(A("incl", 0, 160), A("ps5", 0, 160))
-        mmg([(A("ps5", 336, 352), A("bd"), A("inc", 145, 161))])
-        b0 = 272 * t
-        act(A("box", b0 + 256, b0 + 272), A("ps5", 336, 352))
-        acc = A("ps4", 16, 32)
-        tolist(acc, [(z160, "cmp", 0)])
-        for u, tab, scale, top, z in ((0, "tb", 1.0 / 32, 80.0, z16), (1, "incl", 0.0625, 160.0, z1)):
-            ts(SU(u), acc, scale, AL.mult, top, AL.min)
-            act(SM(9 + u), acc)
-            mmg([(acc, A("idf"), SM(9 + u))], True, False)
+        for u, tab, z in ((0, "tb", z16), (1, "incl", z1)):
+            if u:
+                ts(SU(1), acc, 0.0625, AL.mult, 160.0, AL.min)
+                act(A("sa", 32, 48), acc)
+                mmg([(acc, ID(1.0), A("sa", 32, 48))], True, False)
+            else:
+                ts(SU(0), SM(9), 2.5, AL.mult, 40.0, AL.add)
+                act(A("sa", 0, 16), SM(9), bias=1280.0, scale=80.0)
+                act(A("sa", 16, 32), SM(9), AF.Relu, bias=-15 * 4096.0, scale=4096.0)
+                mmg([(acc, ID(1.0), A("sa", 0, 16)), (acc, ID(1.0), A("sa", 16, 32))], True, False)
             tt(A("cmp", 256 * u + 256, 256 * u + 512), IND(A(tab), SU(u)), A("sw"), AL.is_le)
             tolist(acc, [(z, "cmp", 256 * u + 256)], False)
         ts(SU(2), acc, float(L), AL.min)
@@ -538,6 +595,21 @@ def build(T, dst, msk):
         for k in range(5):
             a, b = 512 * k, 512 * k + 512
             pa, h, lim = A("ps%d" % (0, 2, 1, 3, 0)[k]), A("b1", a, b), -250.0 if t else -290.0
+            if t and VH[t][k] >= 4:
+                ts(A("qa", a, b), A("qb", a, b), 231.0, AL.subtract, -1.0 / 33, AL.mult)
+            if VH[t][k] == 6:
+                act(A("hh", a, b), IND(A("rct"), A("idx", a // 16, b // 16)))
+                mmg([(pa, ID(0.125), A("qa", a, b)), (pa, ID(0.125), A("hh", a, b))])
+                act(h, pa, AF.Sign, bias=(t - 15.5) / 8)
+                tt(h, pa, h, AL.subtract)
+                ts(A("qa" if t else "qb", a, b), h, 8.0 if t else -264.0, AL.mult, -7.0 if t else 495.0, AL.add)
+                continue
+            if VH[t][k] == 4:
+                tt(A("hh", a, b), IND(A("rct"), A("idx", a // 16, b // 16)), A("qa", a, b), AL.add)
+                ts(h, A("hh", a, b), 15.5 - t, AL.is_gt, 1.0 if t else 2.0, AL.mult)
+                mmg([(pa, ID(1.0 if t else -33.0), A("hh", a, b)), (pa, ID(-16.0 if t else 264.0), h)])
+                act(A("qa" if t else "qb", a, b), pa, bias=1.0 if t else 231.0)
+                continue
             (cp if VI[t][k] else act)(A("hh", a, b), IND(A("rct"), A("idx", a // 16, b // 16)))
             two = [(pa, ID(1.0), A("qb" if t else "qq", a, b)), (pa, ID(-33.0), A("hh", a, b))]
             mmg(two)
@@ -558,13 +630,17 @@ def build(T, dst, msk):
         z = str(s)
         kv, hv, sb = A("kv" + z), A("hv" + z), A("sb" + z)
         act(kv, IND(A("kt", 0, wd), ofs))
-        ts(hv, kv, HB - 7.5, AL.add)
+        if HVS[s]:
+            act(hv, kv, bias=HB - 7.5)
+        else:
+            ts(hv, kv, HB - 7.5, AL.add)
         lo, hi = A(banks[0], 0, 256), A(banks[0], 256, 512)
         mmg([(lo, A("bda"), r), (lo, M("sk"), gp), (lo, A("bdb"), m)])
         act(sb, lo, AF.Sign, bias=7.5)
-        mmg([(lo, ID(1.0), kv), (lo, ID(-1.0), hv), (lo, ID(-1.0), m), (lo, M("k1"), gp), (lo, ID(128.0), sb)], True, False)
-        mmg([(hi, a, b) for a, b in sel2] + [(hi, ID(128.0), sb)], False, True)
-        act(A("rp" + z), A(banks[0]), AF.Relu)
+        mmg([(lo, ID(1.0), kv), (lo, ID(-1.0), hv), (lo, ID(-1.0), m), (lo, ID(128.0), sb)])
+        act(A("rp" + z, 0, 256), lo, AF.Relu, bias=HB + 16 - 128)
+        mmg([(hi, a, b) for a, b in sel2] + [(hi, ID(128.0), sb)])
+        act(A("rp" + z, 256, 512), hi, AF.Relu)
         lo = A(banks[1], 0, 256)
         rk = A("rp" + z, 0, 256)
         mmg([(lo, ID(1.0), m), (lo, ID(16.0), kv), (lo, ID(-16.0), hv), (lo, ID(-15.0), rk), (lo, ID(120.0), sb)])
@@ -574,7 +650,7 @@ def build(T, dst, msk):
         z = str(s)
         mmg([(A(bank, 0, 256), M(sf), gp)])
         ts(A("kw"), A(bank, 0, 256), -PH, AL.add)
-        mmg([(A(bank, 256, 272), A("lcw", 0, 128, p1=1), A("ones", 0, 16, p1=1))], True, False)
+        mmg([(A(bank, 256, 272), A("zz", 16, 144, p1=1), A("ones", 0, 16, p1=1))], True, False)
         for c in range(16):
             ts(A("eq", 256 * c, 256 * c + 256 - 16 * c), A("kw", 16 * c, 256), n32(c, c + 1), AL.is_equal, ok(c, c + 1), AL.mult)
             if c < 15:
@@ -601,7 +677,7 @@ def build(T, dst, msk):
         else:
             m = A("qa", 0, 256)
             cp(A("v32", 0, 80), A("off", 0, 80))
-            act(A("gz"), G)
+            act(A("gz"), G, scale=-1.0)
         ts(SM(5), A("idx", 0, 16), R - 0.5, AL.is_lt)
         branch(t, ("ps6", "ps6"), A("off", 0, 16), x, A("rb", 0, 256), G, m, [(M("sl"), G)])
         lowest(t, "ps7", "sfA", G, lambda a, b: A("v32", a, b), lambda a, b: SM(5, a, b))
@@ -612,7 +688,7 @@ def build(T, dst, msk):
             act(A("mk"), hi, bias=HB + 8)
             mmg([(hi, ID(1.0), A("kn0")), (hi, ID(16.0), A("mk"))])
             act(A("tn0"), hi, bias=CP)
-        mmg([(lo, M("n1"), G), (lo, M("n2"), rp), (lo, M("n3"), sb), (lo, M("nx0"), A("x0", I * t, I * t + I)), (lo, M("nx1"), A("x1"))]
+        mmg([(lo, M("n1"), G), (lo, M("n2"), rp), (lo, M("nx0"), A("x0", I * t, I * t + I)), (lo, M("nx1"), A("x1"))]
             + ([(lo, M("sum"), A("mk"))] if t == 0 else []))
         act(A("pn" + z), lo)
         mmg([(hi, M("x1"), G)] + ([(hi, M("xx0"), A("x0", 0, I)), (hi, M("xx1"), A("x1"))] if t == 0 else []))
@@ -626,10 +702,16 @@ def build(T, dst, msk):
 
     def post_pre():
         wd = V + I
-        act(A("thm"), A("mk"), bias=CP, scale=32.0)
-        ts(A("qm"), A("mk"), -33.0, AL.mult, 231.0, AL.add)
         cp(SU(7), A("la", 0, 16))
-        tt(A("cm3"), IND(A("tt", 0, wd), SU(7)), A("thm"), AL.is_lt)
+        if PS:
+            act(A("qm"), A("mk"), bias=231.0, scale=-33.0)
+            act(A("cm3"), IND(A("tt", 0, wd), SU(7)), bias=CPN)
+            mmg([(A("ps4", 0, 256), ID(0.5), A("cm3")), (A("ps4", 0, 256), ID(-16.0), A("mk"))])
+            act(A("cm3"), A("ps4", 0, 256), AF.Sign, bias=-120.25, scale=-1.0)
+        else:
+            ts(A("qm"), A("mk"), -33.0, AL.mult, 231.0, AL.add)
+            act(A("thm"), A("mk"), bias=CP, scale=32.0)
+            tt(A("cm3"), IND(A("tt", 0, wd), SU(7)), A("thm"), AL.is_lt)
         act(A("ge"), IND(A("pt", 0, wd), SU(7)), AF.Relu, bias=GB, scale=GS)
         tolist(A("ps5", 0, 16), [(zk, "cm3", 0), (zr, "ge", 0)])
         tt(SM(6), A("ps5", 0, 16), A("la", 0, 16), AL.max)
@@ -637,21 +719,26 @@ def build(T, dst, msk):
         tt(SM(6), SM(6), SM(7), AL.subtract)
         cp(SU(8), SM(6))
         gu, x0, x1 = A("gu"), A("x0", 0, I), A("x1")
-        tt(A("ru"), IND(A("tt", 0, wd), SU(8)), A("qm"), AL.add)
+        if PS:
+            act(A("ru"), IND(A("tt", 0, wd), SU(8)), bias=CPN)
+            mmg([(A("ps5", 0, 256), ID(1.0), A("ru")), (A("ps5", 0, 256), ID(1.0), A("qm"))])
+            act(A("ru"), A("ps5", 0, 256), bias=CPP)
+        else:
+            tt(A("ru"), IND(A("tt", 0, wd), SU(8)), A("qm"), AL.add)
         act(gu, IND(A("pt", 0, wd), SU(8)), AF.Relu, bias=GB, scale=GS)
         branch(2, ("ps4", "ps4"), SU(8), wd, A("ru"), gu, A("mk"), [(M("sp"), gu), (M("xs0"), x0), (M("xs1"), x1)])
-        rp, sb = A("rp2", 256, 512), A("sb2")
+        rp = A("rp2", 256, 512)
         lo, hi = A("ps5", 0, 256), A("ps4", 256, 512)
-        mmg([(lo, M("t1"), gu), (lo, M("n2"), rp), (lo, M("n3"), sb), (lo, M("t4"), A("gz")), (lo, ID(-8192.0), A("ww0"))])
+        mmg([(lo, M("t1"), gu), (lo, M("n2"), rp), (lo, M("t1"), A("gz")), (lo, ID(-8192.0), A("ww0"))])
         ts(A("cd"), lo, -8192.0, AL.is_equal)
         tolist(A("ps5", 0, 16), [(z0, "cd", 0)])
         act(SM(8), A("ps5", 0, 16))
         lowest(2, "ps5", "sfS", gu, lambda a, b: SM(6, a, b), lambda a, b: SM(8, a, b))
         lo = A("ps4", 0, 256)
-        mmg([(lo, M("p1"), gu), (lo, M("p2"), rp), (lo, M("n3"), sb), (lo, M("e2"), x0), (lo, M("e2"), x1),
+        mmg([(lo, M("p1"), gu), (lo, M("p2"), rp), (lo, M("e2"), x0), (lo, M("e2"), x1),
              (lo, M("nx0"), A("x0", 2 * I, 3 * I)), (lo, M("nx0"), x1)])
         act(A("pn2"), lo)
-        mmg([(hi, M("x1"), gu), (hi, M("q2"), rp), (hi, M("q3"), sb), (hi, M("q3"), A("ones"))])
+        mmg([(hi, M("x1"), gu), (hi, M("q2"), rp)])
         x = V + 2 * I
         tt(A("pt", x, x + I), hi, A("ww2"), AL.mult)
         cp(IND(A("kt"), SU(6)), A("kn2"))
@@ -662,7 +749,7 @@ def build(T, dst, msk):
         for X in (0, 1):
             c = 80 * X
             pl = "ps%d" % (2 + X)
-            unround(pl, X, turned("ft", X), [turned("xa", X, 512, 256, 384)])
+            unround(pl, X, turned("ft", X), [turned("xn", X)], RS[1])
             tt(A("la", c, c + 80), A(pl, 0, 80), A("v32", c, c + 80), AL.min)
         sp = A("ps5", 160, 320)
         mmg([(sp, A("tri"), A("ovl")), (sp, A("bd"), A("inc", 0, 160)), (sp, ID(-8192.0), A("ovl"))])
@@ -830,7 +917,13 @@ def order(ops, deps):
                     best = cur
         key = list(cur[0])
         j, k = cur[3][int(draw() * len(cur[3]))]
-        if draw() < 0.5:
+        way = draw()
+        if way < SHAKE:
+            mid, wide, amp = key[k], 500.0 + 2500.0 * draw(), 300.0 + 1500.0 * draw()
+            for i in range(n):
+                if abs(key[i] - mid) < wide:
+                    key[i] += amp * draw()
+        elif way < 0.5 + SHAKE / 2:
             key[j] = key[k] + 1.0 + 2000.0 * draw() ** 3
         else:
             shift, todo, t0 = key[k] - key[j] + 1.0 + 2000.0 * draw() ** 3, [k], key[j]
@@ -843,6 +936,7 @@ def order(ops, deps):
                         seen.add(a)
                         todo.append(a)
     _PLAN["total"] = best[2] / (1 + len(CASES))
+    _PLAN["cases"] = [int(replay([k for x, k in sorted(zip(best[0], range(n)))], eng, c, pred, tail, m[1])) for c, m in zip(others, CASES)]
     st = list(best[0])
     for k in range(n):
         if "alias" in ops[k] and ops[k - 1]["eng"] == "y":

from concourse.mybir import AluOpType, ActivationFunctionType

AL = AluOpType
AF = ActivationFunctionType
BF, F32, I32, U16 = "bfloat16", "float32", "int32", "uint16"
V, H, I, L, R = 3072, 1024, 256, 2560, 1024
W = 3840
HL = 1280
CR = 1.5 * 2.0 ** 36
HB = 2064.0
PH = 4128.0
U2 = 2.0 ** 18
SP = L + 16
rA, rC, rK, rN, rL, rR, rS, rO, rP, rI = 0, 2, 4, 5, 6, 8, 10, 12, 13, 14

N1, NG = 1024, 896
VB = (256, 768, 768, 768, 512, 640, 640, 640, 640, 512)
SLOT = ((1, "g0"), (1, "gpa"), (0, "rbm"), (0, "b1m"), (0, "w0m"), (0, "relu"), (0, "max"), (0, "rnd"), (1, "gpb"), (1, "g1"),
        (1, "gpm"), (0, "off"), (0, "ft"), (1, "bs"), (1, "bv"))
LAST = ((1, "g0"), (0, "rbm"), (0, "b1m"), (1, "g1"), (1, "bv"))
TLV = 4
W0P, PRS, HHS = False, True, ()
RS = (False, False, False, False)
IDV, MZ, PS = 20, True, False
HVS = (0, 0, 0)
TTV = (2, 3, 4)
BONUS = 8000.0
POSTBY = (1, 2, 0)
VI = ((0, 0, 0, 0, 0), (0, 0, 0, 0, 0))
VH = ((4, 0, 4, 4, 4), (0, 0, 2, 2, 2))

IDW = (1.0, -1.0, 8.0, 16.0, -16.0, -15.0, 120.0, -33.0, 264.0, 128.0, -8192.0, 1.0625, 0.125, 0.5)
SB = {
    "kt": ([128, 4096], BF), "tt": ([128, 4096], F32), "pt": ([128, 4096], F32), "hh": ([128, V], BF),
    "rct": ([128, 1040], BF), "qa": ([128, 2832], BF), "qb": ([128, 2832], BF), "qq": ([128, 2832], BF),
    "rb": ([128, L], BF), "b1": ([128, L], BF), "gp": ([128, L], BF),
    "cx": ([128, 1152], I32), "cf": ([128, 1152 + 192], F32), "lo": ([128, 512], F32),
    "v0i": ([128, 160], I32), "wti": ([128, 4], I32), "wcol": ([128, 4], F32), "wcb": ([128, 8], BF),
    "off": ([128, 160], U16), "idx": ([128, 160], U16),
    "lc": ([128, 256], BF), "lcw": ([128, 128 * len(set(VB))], BF), "xa": ([128, 1024], F32), "xt": ([128, 256], F32), "xr": ([128, 256], F32),
    "ht": ([128, 256], BF), "ft": ([128, 256], F32), "hs": ([128, 512], F32), "ot": ([128, 256], BF), "crb": ([128, 160], BF),
    "ones": ([128, 256], BF), "idf": ([128, 128], F32), "idc": ([128, 80], F32), "ids": ([128, 128 * len(IDW)], BF),
    "bd8": ([128, 8], BF), "bd": ([128, 128], BF), "bda": ([128, 128], BF), "bdb": ([128, 128], BF), "tri": ([128, 128], BF),
    "zz": ([128, 144 * 7], BF), "col": ([128, 64], F32),
    "wm": ([128, 128], BF), "wl": ([128, 32], BF), "wr": ([128, 8], BF), "wb": ([128, 16], BF), "wq": ([128, 24], BF),
    "mm": ([128, 128 * 20], BF), "tl": ([128, 128 * 16], BF), "eq": ([128, 4096], BF), "kw": ([128, 256], U16),
    "pi": ([128, 4], I32), "pc": ([128, 24], F32), "pb": ([128, 2], BF), "sw": ([128, 256], BF),
    "x0": ([128, 768], BF), "x1": ([128, 256], BF), "il": ([128, 80], F32),
    "ovl": ([128, 160], BF), "inc": ([128, 176], BF), "incl": ([128, 176], F32), "tb": ([128, 96], F32), "junk": ([128, 64], F32),
    "sm": ([128, 16 * 24], F32), "su": ([128, 16 * 12], U16),
    "sa": ([128, 48], BF), "xn": ([128, 256], BF), "cmp": ([128, 768], BF), "box": ([128, 544], BF), "rcv": ([128, 544], BF),
    "v32": ([128, 160], F32), "sl": ([128, 160], BF), "la": ([128, 160], F32), "lb": ([128, 160], F32), "lh": ([128, 160], F32),
    "li": ([128, 160], I32),
    "gz": ([128, 256], BF), "mk": ([128, 256], BF), "thm": ([128, 256], F32), "qm": ([128, 256], BF), "mq": ([128, 256], BF),
    "cm3": ([128, 256], BF), "ge": ([128, 256], BF), "ru": ([128, 256], BF), "gu": ([128, 256], BF), "cd": ([128, 256], BF),
    "tn0": ([128, 256], F32),
}
for _k in (0, 1, 2):
    for _n, _w, _d in (("kv", 256, BF), ("hv", 256, BF), ("sb", 256, BF), ("rp", 512, BF), ("kn", 256, BF), ("pn", 256, F32), ("ww", 256, BF)):
        SB["%s%d" % (_n, _k)] = ([128, _w], _d)
SCRATCH = {k: ("sbuf", s, d) for k, (s, d) in SB.items()}
for _k in range(8):
    SCRATCH["ps%d" % _k] = ("psum", [128, 512], F32)
SEMAPHORES = ["sv", "ss", "sp", "sg", "got0", "got1", "out0", "out1"] + ["d%d" % k for k in range(44)]

GT, VF, SF = 1.9, 45.0, 70.0
GC, SC, PEC = 1.6, 3.8, 0.51
DROW, DBW, DLAT, RLAT = 300.0, 400.0, 700.0, (3500.0, 2500.0)
TRIES, SEED, AMP, SHAKE = 19000, 2, 300.0, 0.3
SAME = {"p": 0.0, "g": 200.0}
GF = 60.0
CASES = (({"sg": 0.72, "vs": 0.6, "g": 1.2, "d": 0.7, "p": 1.1}, 60.0), ({"sg": 1.27, "vg": 1.1, "vs": 1.3, "g": 1.1, "d": 1.1}, 60.0))
HINT = "vsp"
_PLAN = {}


def build(T, dst, msk):
    ops = []
    nd = [0]

    def A(n, a=None, b=None, s=1, p0=0, p1=128, ps=1, tag=None):
        if a is None:
            a, b = 0, (SB[n][0][1] if n in SB else 512)
        t = T[n]
        rows = slice(p0, p1) if ps == 1 else slice(p0, p1, ps)
        ap = t[rows, a:b] if s == 1 else t[rows, a:b:s]
        reg = (n, 0, 512, None) if n not in SB else (n, a, b, tag)
        return (ap, [reg], len(range(a, b, s)), SB[n][1] if n in SB else F32)

    def IND(w, o):
        return (w[0].indirect(o[0]), w[1] + o[1], o[2] * 16, w[3], "ind")

    def op(eng, fns, rd, wr, cost, lat=0.0, sem=None, inc=1):
        rr = [r for x in rd if isinstance(x, tuple) for r in x[1]]
        ww = [r for x in wr for r in x[1]]
        kind = eng + ("g" if len(rd) > 0 and isinstance(rd[0], tuple) and len(rd[0]) == 5 else "s" if wr[0][0] is None and eng == "v" else "")
        ops.append({"eng": eng, "fns": fns, "rd": rr, "wr": ww, "cost": cost, "lat": lat, "sem": sem, "inc": inc, "aft": [], "kind": kind})

    def val(x):
        return x[0] if isinstance(x, tuple) else x

    def vcost(out, ins, two=False):
        if len(out) == 5:
            return 60 + out[2] * SC
        if len(ins[0]) == 5:
            return 60 + out[2] * (GT if two else GC)
        f = 0.5 if all(x[3] in (BF, U16) for x in [out] + ins) else 1.0
        if two and all(x[1][0][0] in SB for x in ins):
            f = 2.0
        return VF + max(64, out[2] * f)

    def split(out):
        if len(out) == 5:
            return [(None, out[1][:1])], [(None, out[1][1:])]
        return [out], []

    def tt(out, a, b, o):
        w, r = split(out)
        op("v", [lambda e: e.tensor_tensor(out[0], a[0], b[0], o)], [a, b] + r, w, vcost(out, [a, b], True))

    def ts(out, a, s1, o0, s2=None, o1=None):
        if s2 is None:
            f = lambda e: e.tensor_scalar(out[0], a[0], val(s1), None, o0)
        else:
            f = lambda e: e.tensor_scalar(out[0], a[0], val(s1), val(s2), o0, o1)
        op("v", [f], [a, s1, s2], [out], vcost(out, [a]))

    def cp(out, a):
        w, r = split(out)
        op("v", [lambda e: e.tensor_copy(out[0], a[0])], [a] + r, w, vcost(out, [a]))

    def ms(out, c):
        op("v", [lambda e: e.memset(out[0], c)], [], [out], VF + max(64, out[2] * (0.5 if out[3] == BF else 1)))

    def act(out, a, fn=AF.Identity, bias=0.0, scale=1.0, acc=None):
        if acc is None:
            f = lambda e: e.activation(out[0], a[0], fn, bias=val(bias), scale=val(scale))
        else:
            f = lambda e: e.activation(out[0], a[0], fn, bias=val(bias), scale=val(scale), accum_out=acc[0])
        op("s", [f], [a, bias, scale], [out] + ([acc] if acc else []), (24 if acc else 0) + (78 + out[2] * GC if len(a) == 5 else SF + max(32, out[2])))

    def mmg(items, start=True, stop=True, each=False):
        fns, rd, c = [], [], 0.0
        for k, (o, l, r) in enumerate(items):
            s, t = each or (start and k == 0), each or (stop and k == len(items) - 1)
            fns.append(lambda e, o=o, l=l, r=r, s=s, t=t: e.matmul(o[0], l[0], r[0], s, t))
            rd += [l, r]
            c += 2 + PEC * max(min(64, l[2]), r[2]) * (4 if l[3] == F32 else 1)
        op("p", fns, rd, [items[0][0]], c, lat=60)

    def dma(q, out, a, nbytes):
        s = "d%d" % nd[0]
        nd[0] += 1
        op(q, [lambda e: e.dma_start(out[0], a[0])], [a], [out], 90, lat=0.0, sem=s, inc=16)
        op("d", [], [a], [out], DROW + nbytes / DBW, lat=DLAT, sem=s)
        ops[-1]["alias"] = len(ops) - 2

    def D(n, a=None, b=None):
        return (T[n][:] if a is None else T[n][:, a:b], [(n + "_hbm", 0, 1, len(ops))], 0, None)

    def iota(out, pat, base, cm):
        if out[3] == I32:
            f = lambda e: e.iota(out[0], pat, base, cm)
        else:
            f = lambda e: e.iota(out[0], pat, base, cm, allow_small_or_imprecise_dtypes=True)
        op("g", [f], [], [out], GF + 160 + 2 * out[2])

    def sel(out, a, pat, cmpop, fill, base, cm):
        op("g", [lambda e: e.affine_select(out[0], a[0], pat, cmpop, fill, base, cm)], [a], [out], GF + 210 + 2 * out[2])

    def put(n, a, b, s, row, w, pat=None, tag=None):
        x = A(n, a, b, s, tag=tag)
        sel(x, x, pat or [[-16, 8]], AL.not_equal, float(w), -row, 1)

    dma("y", A("kt", 0, H), D("kk", 0, H), 262144)
    dma("y", A("kt", H, V), D("kk", H, V), 524288)
    dma("y", A("cx", 0, 64), D("c0", 0, H), 32768)
    dma("s", A("cx", 64, 256), D("c1"), 98304)
    dma("s", A("cx", 256, 448), D("rt"), 98304)
    dma("y", A("cx", 896, 1024), D("c0", H, V), 65536)
    dma("y", A("v0i"), D("v0"), 81920)
    dma("y", A("qa", 0, HL), D("qs", 0, HL), 327680)
    dma("y", A("qa", HL, L), D("qs", HL, L), 327680)
    dma("y", A("wti", 0, 1), D("wt"), 512)

    iota(A("pt", 0, 128), [[1, 128]], 0, 0)
    for k in (128, 256):
        ts(A("pt", k, 2 * k), A("pt", 0, k), float(k), AL.add)
    ts(A("pt", 512, 1024), A("pt", 0, 512), 512.0, AL.add)
    act(A("pt", 1024, 2048), A("pt", 0, 1024), bias=1024.0)
    if PRS:
        act(A("pt", 2048, V), A("pt", 0, 1024), bias=2048.0)
    else:
        ts(A("pt", 2048, V), A("pt", 0, 1024), 2048.0, AL.add)
    iota(A("lo", 0, 64, p1=32), [[0, 2], [1, 32]], 0, 0)
    for k in (64, 128, 256):
        act(A("lo", k, 2 * k, p1=32), A("lo", 0, k, p1=32))
    ms(A("ones"), 1.0)
    ms(A("wm", 0, 32), 0.0)
    iota(A("wl"), [[0, 32]], 0, 0)
    ms(A("zz"), 0.0)
    ms(A("col"), 0.0)
    sel(A("bd8"), A("ones", 0, 8), [[-16, 8]], AL.is_ge, 0.0, 0, 1)
    sel(A("bd8"), A("bd8"), [[16, 8]], AL.is_ge, 0.0, 15, -1)
    iota(A("pi", 0, 1), [[0, 1]], 0, 1)
    sel(A("ids", 0, 128), A("ones", 0, 128), [[-1, 128]], AL.is_equal, 0.0, 0, 1)
    ts(A("pi", 1, 2), A("pi", 0, 1), 15, AL.bitwise_and)
    ts(A("pi", 2, 3), A("pi", 0, 1), 1, AL.bitwise_and)

    def PC(k):
        return A("pc", k, k + 1)
    ROW, CP, CPH, CPX, THS, GS, GB, TBB, HC = [PC(k) for k in range(9)]
    THV = A("pb", 0, 1)
    cp(ROW, A("pi", 1, 2))
    ts(CP, A("pi", 2, 3), -6144.0, AL.mult, 3072.0 - 222.5, AL.add)
    act(CPH, CP, bias=-HB)
    act(CPX, CP, bias=-2.0625 * HB)
    act(THS, CP, bias=222.5 - 8.0)
    act(THV, CP, bias=222.5)
    put("col", 0, 16, 1, rN, -2, [[rN - rI, 2], [-16, 8]])
    put("col", 32, 64, 1, 0, PH - 15.5, [[-8, 2], [-2, 2], [-16, 8]])
    put("col", 16, 32, 1, rO, -1, [[-1, 2], [-16, 8]])
    put("col", 32, 40, 1, rL, 1 - H)
    put("col", 40, 48, 1, rI, H)
    put("col", 48, 64, 1, rO, 1, [[-1, 2], [-16, 8]])
    act(A("junk", 0, 32), A("col", 0, 32), bias=1.0 / 32, acc=GS)
    act(A("junk", 32, 64), A("col", 32, 64), acc=GB)

    def Z(k, j=None):
        if j is None:
            return A("zz", 144 * k + 15, 144 * k + 143, 16)
        return A("zz", 144 * k + 15 - j, 144 * k + 143 - j)
    z1, za, z16, zs, zk, zr, z0 = range(7)
    act(Z(z1), A("bd8"))
    act(A("wr"), A("bd8"), scale=-1024.0)
    act(A("wb", 0, 8), A("bd8"), scale=U2 / 2)
    act(A("wb", 8, 16), A("bd8"), scale=U2 / 2)
    act(A("wq", 0, 8), A("bd8"))
    act(A("idf"), A("ids", 0, 128))
    if RS[0] or RS[1] or RS[3]:
        sel(A("idc"), A("idf", 0, 80), [[0, 80]], AL.not_equal, -CR, -80, 1)
        ms(A("xr"), 1.0)

    def ID(w, n=128):
        k = IDW.index(w)
        return A("ids", 128 * k, 128 * k + n, p1=n)
    made = [1.0]

    def ids(*ws):
        for w in ws:
            made.append(w)
            if len(made) <= IDV:
                ts(ID(w), ID(1.0), w, AL.mult)
            else:
                sel(ID(w), ID(1.0), [[-1, 128]], AL.not_equal, w, 0, 1)
    for u in (0, 1):
        put("wm", 0, 32, 1, u, 1, [[-8, 2], [-2, 2], [-16, 8]])
        put("wm", 8, 24, 1, rA + u, -1, [[0, 2], [-16, 8]])
    put("wm", 0, 32, 1, rO, -PH, [[0, 4], [-16, 8]])
    for w, r, x in ((1, rK, 32768), (2, rO, -U2 / 2), (3, rL, -65536), (1, rO, -216 * 16384), (2, rN, -2 ** 23),
                    (1, rP, -8192), (1, rL, -2 ** 19)):
        put("wm", 8 * w, 8 * w + 8, 1, r, x)
    act(Z(za), A("wm", 0, 8))
    for k in (1, 2, 3):
        act(A("wm", 32 * k, 32 * k + 32), A("wm", 0, 32))
        put("wm", 32 * k + 24, 32 * k + 32, 1, rP, 8192 * k)
    ms(A("lcw"), 0.0)
    cuts = sorted(set(VB))
    for u, nv in enumerate(cuts):
        x = A("lcw", 128 * u, 128 * u + 128)
        sel(x, x, [[0, 128]], AL.is_gt, -8 * U2, nv // 16, -1)

    def row(r, a, b, src):
        dma("y", A("pt", a, b, p0=r, ps=16, tag=r), src, 32 * (b - a))
    for u in (0, 1):
        o = 448 * u
        if u:
            ts(A("cx", 448, 896), A("cx", 0, 448), 31, AL.bitwise_and)
        cp(A("cf", o, o + 448), A("cx", o, o + 448))
        row(rA + u, 0, H, A("cf", o, o + 64))
        row(rC + u, 0, V, A("cf", o + 64, o + 256))
        row(rR + u, 0, V, A("cf", o + 256, o + 448))
        if not u:
            row(rN, 0, V, A("cf", 256, 448))
            row(rS + 1, 0, H, A("lo", p1=16))
    ts(A("cx", 1024, 1152), A("cx", 896, 1024), 31, AL.bitwise_and)
    cp(A("cf", 896, 1152), A("cx", 896, 1152))
    for u in (0, 1):
        row(rS + u, H, V, A("cf", 896 + 128 * u, 1024 + 128 * u))
    row(rA + 1, H, V, A("lo", p1=32))
    for k in range(3):
        if k in HHS:
            act(A("hh", 1024 * k, 1024 * k + 1024), A("kt", 1024 * k, 1024 * k + 1024), bias=HB - 7.5)
        else:
            ts(A("hh", 1024 * k, 1024 * k + 1024), A("kt", 1024 * k, 1024 * k + 1024), HB - 7.5, AL.add)
    for a, n, bank, c in ((0, 64, "ps4", 0), (1024, 128, "ps3", 64)):
        mmg([(A(bank, 0, n), Z(z1, s), A("hh", a + n * s, a + n * s + n)) for s in range(16)])
        src = A("cf", 1152 + c, 1152 + c + n)
        act(src, A(bank, 0, n), bias=-HB, scale=0.0625)
        dma("y", A("pt", a, a + 16 * n, p0=rK, ps=16, tag=rK), src, 512 * n)
    for k in range(6):
        a = 512 * k
        b = "ps%d" % (5 + k % 3)
        mmg([(A(b), ID(1.0), A("kt", a, a + 512)), (A(b), ID(1.0), A("hh", a, a + 512))])
        if k in TTV:
            ts(A("tt", a, a + 512), A(b), CPH, AL.add)
        else:
            act(A("tt", a, a + 512), A(b), bias=CPH)
    cp(A("off"), A("v0i"))
    for X in (0, 1):
        ts(A("qq", HL * X, HL * X + HL), A("qa", HL * X, HL * X + HL), -33.0, AL.mult, 231.0, AL.add)
    iota(A("qq", L, L + 16), [[0, 16]], 0, 0)
    iota(A("qb", L, L + 16), [[0, 16]], 0, 0)
    iota(A("rct", R, R + 16), [[-1, 16]], 0, 0)

    def sums(q, X, nw):
        o = HL * X
        mmg([(A("ps%d" % X, j, 128 * nw, 16, p1=80), A(q, o + j, o + HL, 16), A("wq", 0, 8 * nw)) for j in range(16)], each=True)
        act(A("lc", 128 * X, 128 * X + 128, p1=80), A("ps%d" % X, 0, 128, p1=80), scale=32768.0 / 33)
    for X in (0, 1):
        sums("qq", X, 1)

    ids(-1.0)
    for u in (0, 1):
        put("wl", 0, 16, 1, rS + u, 1, [[rS - rC, 2], [-16, 8]])
        put("wl", 8, 16, 1, rS + u, -1)
    for w, r, x in ((0, rO, -PH), (1, rK, 32768), (1, rO, -216 * 16384), (1, rP, -8192), (2, rO, -U2 / 2), (2, rI, 2 ** 22),
                    (3, rO, -65 * 2 ** 17), (3, rN, 2 ** 23)):
        put("wl", 8 * w, 8 * w + 8, 1, r, x)
    ids(*[w for w in IDW if w not in made and (w != 0.125 or 6 in VH[0] + VH[1]) and (w != 0.5 or RS[2] or PS)])
    if RS[2]:
        sel(A("crb", 80, 160, p1=1), A("ones", 0, 80, p1=1), [[0, 80]], AL.is_gt, 0.5, 0, 0)
    if MZ:
        ms(A("eq", 0, 640), 0.0)
        for k in range(4):
            dma("y", A("mm", 640 * k, 640 * k + 640), A("eq", 0, 640), 163840)
    else:
        for k in range(5):
            iota(A("mm", 512 * k, 512 * k + 512), [[0, 512]], 0, 0)
    sel(A("bd"), A("ones", 0, 128), [[-16, 8], [0, 16]], AL.is_ge, 0.0, 0, 1)
    sel(A("bd"), A("bd"), [[16, 8], [0, 16]], AL.is_ge, 0.0, 15, -1)
    sel(A("tri"), A("bd"), [[1, 128]], AL.is_ge, 0.0, 0, -1)
    iota(A("sw"), [[1, 256]], 0, 0)
    for k in range(3):
        iota(A("x0", I * k, I * k + I), [[32, 8], [0, 32]], V + I * k, 0)
    iota(A("x1"), [[0, 8], [1, 32]], 0, 0)
    ts(A("junk", 0, 16), A("sw", 0, 16), ROW, AL.is_gt)
    ts(A("junk", 16, 32), A("sw", 0, 16), ROW, AL.is_equal)
    tt(A("junk", 32, 48), A("junk", 0, 16), A("junk", 16, 32), AL.subtract)
    for j in range(16):
        if j < TLV:
            ts(A("tl", 128 * j, 128 * j + 128), A("bd"), A("junk", 32 + j, 33 + j), AL.mult)
        else:
            act(A("tl", 128 * j, 128 * j + 128), A("bd"), scale=A("junk", 32 + j, 33 + j))
    iota(A("il", 48, 64), [[16, 16]], 0, 0)
    MN = {"sum": 0}

    def M(name):
        return A("mm", 128 * MN[name], 128 * MN[name] + 128)

    def me(name, *ent):
        MN[name] = len(MN)
        b = 128 * MN[name]
        for rin, rout, w in ent:
            if rout is None:
                put("mm", b, b + 128, 1, rin, w, [[-16, 8], [0, 16]])
            elif isinstance(rout, tuple):
                put("mm", b + rout[0], b + 128, 8, rin, w, [[-16, 8], [0, 2]], rout[0] % 8)
            else:
                put("mm", b + rout, b + 128, 16, rin, w, None, rout % 8)

    def whole(rin, rout, c=-PH):
        return [(rin, rout, 1), (rin + 1, rout, 1), (rO, rout, c)]
    me("sk", (rK, None, 2))
    CS, CS1, LI = (rC, rS), (rC + 1, rS + 1), (rL, rI)
    me("sfA", (rA, None, 1), (rA + 1, None, 1))
    me("sl", (rC, rC, 1 / 32), (rS, rC, -1 / 32), (rC + 1, rC + 1, 1), (rS + 1, rC + 1, -1))
    me("n1", *(whole(rA, rA) + whole(rS, CS) + [(rA + 1, rA + 1, 1), (rS + 1, CS1, 1), (rO, LI, 2048)]))
    me("n2", (rC, rC, 32), (rC + 1, rC, 1), (rC + 1, rC + 1, 1), (0, rC, -33), (0, rC + 1, -1))
    me("nx0", (0, rR, 1))
    me("nx1", (0, rR, 1), (0, rR + 1, 1))
    me("x1", *(whole(rC, CS) + whole(rR, rR) + [(rC + 1, CS1, 1), (rR + 1, rR + 1, 1), (rK, rK, 1), (rN, rN, -1), (rO, LI, 2048)]))
    me("xx0", (0, rA, 1))
    me("xx1", (0, rA, 1), (0, rA + 1, 1))
    me("sfS", (rS, None, 1), (rS + 1, None, 1))
    me("sp", (rC, CS, 1 / 32), (rA, rC, -1 / 32), (rC + 1, CS1, 1), (rA + 1, rC + 1, -1), (rO, rS, -PH / 32))
    me("xs0", (0, rS, -1 / 32))
    me("xs1", (0, rS + 1, -1))
    me("t1", (rA, rC, 1), (rA + 1, rC, 1))
    me("p1", *whole(rA, rA))
    me("p2", (rS, rC, 32), (rS + 1, rC, 1), (0, rC, -33))
    me("e2", (0, rC, 1))
    me("q2", (rS, CS, -32), (rS + 1, CS, -1), (0, CS, 33))
    for r, w in ((rR, 1), (rR + 1, 1), (rO, -PH), (rP, -8192 if PS else -17 * 8192), (rN, -2 ** 23)):
        put("zz", 144 * zr + 15, 144 * zr + 143, 16, r, w)
    put("zz", 144 * z0 + 15, 144 * z0 + 143, 16, rC, 1)
    act(A("mm", rK, 128, 16), A("bd8"))
    act(A("bda"), A("bd"), scale=-0.0625)
    act(A("bdb"), A("bd"), scale=-2.0)
    for z, w in ((z16, 16.0), (zs, -512.0), (zk, 8192.0 if PS else 16384.0)):
        act(Z(z), A("bd8"), scale=w)
    IL, SPN, SPQ = A("il", 0, 16), A("il", 16, 32), A("il", 32, 48)
    act(IL, A("il", 48, 64), bias=ROW)
    CPN, CPP = PC(9), PC(10)
    if PS:
        act(CPN, CP, bias=-240.0, scale=-1.0)
        act(CPP, CP, bias=240.0)
    act(A("il", 64, 80), IL, bias=0.5)
    act(SPN, IL, bias=W - 8192.0)
    act(SPQ, IL, bias=float(SP))
    ts(TBB, ROW, 9.5, AL.is_gt, 9999.0, AL.mult)
    ts(A("wti", 1, 2), A("wti", 0, 1), 31.0, AL.mult)
    ts(A("wti", 2, 3), A("wti", 1, 2), 1023 - 31, AL.bitwise_and)
    ts(A("wti", 3, 4), A("wti", 1, 2), 31, AL.bitwise_and)
    cp(A("wcol", 0, 2), A("wti", 2, 4))
    act(A("wq", 8, 16), A("bd8"), scale=A("wcol", 0, 1))
    act(A("wq", 16, 24), A("bd8"), scale=A("wcol", 1, 2))
    act(A("wcb", 0, 2), A("wcol", 0, 2))
    mmg([(A("ps7", 0, 1), A("bd"), A("wcb", u, u + 1)) for u in (0, 1)])
    act(HC, A("ps7", 0, 1), bias=2.0 ** 24 - 1024, scale=-231.0)
    iota(A("inc", 0, 1), [[0, 1]], 0, 0)
    iota(A("incl", 160, 176), [[0, 16]], 9999, 0)
    iota(A("tb"), [[0, 96]], 9999, 0)
    late = [len(ops)]
    dma("y", A("rct", 0, R), D("rec"), 262144)
    posted, early = [], []

    def turned(n, X, w=128, a=0, b=None):
        return A(n, w * X + a, w * X + (w if b is None else b), p1=80)

    def unround(pl, X, x, more, scalar=False):
        out, idf = A(pl, 0, 80), A("idf", 0, 80, p1=80)
        if more:
            mmg([(out, y, idf if y[3] == F32 else ID(1.0, 80)) for y in more], True, False)
        if scalar:
            act(turned("xr", X), x, bias=CR, scale=-1.0)
            mmg([(out, x, idf)], False, False)
            mmg([(out, A("xr", 128 * X, 128 * X + 128, p1=81), A("idc", p1=81))], False, True)
            return
        ts(turned("ht", X), x, CR, AL.add, CR, AL.subtract)
        mmg([(out, x, idf)], False, False)
        mmg([(out, turned("ht", X), ID(-1.0, 80))], False, True)

    def step(t, k, X):
        look = k == 4
        fin = t == 0 and not look
        o, c = HL * X, 80 * X
        wd = 1024 if (t == 0 and k == 0) else (V if t == 0 else V + I)
        ps, pl = "ps%d" % X, "ps%d" % (2 + X)
        nw = 4 if (look or fin) else 3
        q = "qb" if t else "qq"
        mk, at = {}, [len(ops)]

        def done(name):
            mk[name] = list(range(at[0], len(ops)))
            at[0] = len(ops)
        for a, b, name in ((0, N1, "g0"), (N1, HL, "g1")):
            if a < b:
                tt(A("rb", o + a, o + b), IND(A("tt", 0, wd), A("off", c + a // 16, c + b // 16)), A(q, o + a, o + b), AL.add)
            done(name)
        for a, b, name in ((0, NG, "gpa"), (NG, HL, "gpb")):
            if a < b:
                act(A("gp", o + a, o + b), IND(A("pt", 0, wd), A("off", c + a // 16, c + b // 16)), AF.Relu, bias=GB, scale=GS)
            done(name)
        nv = VB[5 * t + k]
        if nv < HL:
            ts(A("b1", o + nv, o + HL), A("rb", o + nv, o + HL), THV, AL.is_lt, 2.0, AL.mult)
        done("bv")
        if nv:
            act(A("b1", o, o + nv), A("rb", o, o + nv), AF.Sign, bias=THS, scale=-1.0)
        done("bs")
        wp, w0 = ("wl", 0) if look else ("wm", 32 * k if fin else 0)
        nb = 2 if look else 1
        f = 0 if look or not W0P else 1
        for src, c0, c1, wt in (("gp", 128 * f, 128 * nw, A(wp, w0 + 8 * f, w0 + 8 * nw)), ("rb", 128, 256, A("wr")),
                                ("b1", 256, 256 + 128 * nb, A("wb", 0, 8 * nb))):
            for h in (0, 8):
                mmg([(A(ps, c0 + j, c1, 16, p1=80), A(src, o + j, o + HL, 16), wt) for j in range(h, h + 8)],
                    src == "gp" and h == 0, src == "b1" and h == 8)
            if src == "gp":
                mmg([(A(ps, 128, 256, p1=80), ID(1.0, 80), turned("lc", X))]
                    + [(A(ps, 256 + 128 * u, 384 + 128 * u, p1=80), ID(1.0, 80), turned("lcw", cuts.index(nv))) for u in range(nb)], False, False)
            done(src + "m")
        if look:
            if RS[2]:
                act(turned("ot", X), A(ps, 384, 512, p1=80), AF.Sign)
                mmg([(A(pl, 128, 208), turned("ot", X), ID(0.5, 80)), (A(pl, 128, 208), A("ones", 0, 128, p1=1), A("crb", 80, 160, p1=1))])
            else:
                ts(turned("ot", X), A(ps, 384, 512, p1=80), 0.0, AL.is_gt)
                mmg([(A(pl, 128, 208), turned("ot", X), ID(1.0, 80))])
            src, ini, out = A(pl, 128, 208), A("inc", c, c + 1), A("inc", c + 1, c + 81)
            op("v", [lambda e: e.tensor_tensor_scan(out[0], T["ones"][:, 0:80], src[0], ini[0], AL.mult, AL.add)], [A("ones"), src, ini], [out], VF + 80)
            act(A("ovl", c, c + 80), src)
            done("over")
        if f:
            for h in (0, 8):
                mmg([(A(pl, 0, 80), Z(za, j), A("gp", o + j, o + HL, 16)) for j in range(h, h + 8)], h == 0, False)
        done("w0m")
        act(turned("xa", X, 512, 128 * f, 256), A(ps, 128 * f, 256, p1=80), AF.Relu)
        if look:
            act(turned("xn", X), A(ps, 256, 384, p1=80), AF.Relu)
        done("relu")
        if look:
            done("max")
            unround(pl, X, turned("xa", X, 512, 128, 256), [turned("xa", X, 512, 0, 128), turned("xn", X)], RS[0])
            done("rnd")
            done("ft")
            ts(A("idx", c, c + 80), A(pl, 0, 80), float(R + t), AL.min)
            done("off")
            return mk
        tt(turned("xt", X), A(ps, 256, 384, p1=80), turned("xa", X, 512, 128, 256), AL.max)
        done("max")
        unround(pl, X, turned("xt", X), [] if f else [turned("xa", X, 512, 0, 128)], RS[3])
        done("rnd")
        if fin:
            if k == 0:
                act(turned("ft", X), A(ps, 384, 512, p1=80))
            else:
                tt(turned("ft", X), A(ps, 384, 512, p1=80), turned("ft", X), AL.max)
        done("ft")
        cp(A("off", c, c + 80), A(pl, 0, 80))
        done("off")
        return mk

    def looks(t):
        prev, last = None, {}
        for k in range(5):
            for X in (0, 1):
                m = step(t, k, X)
                for who, name in (LAST if (k, X) == (4, 1) else SLOT):
                    for a in (m[name] if who else prev[name] if prev else []):
                        e = ops[a]["eng"]
                        if e in last and e in HINT:
                            ops[a]["aft"].append(last[e])
                        last[e] = a
                prev = m
                if (t, k, X) == POSTBY:
                    ops[m["g0"][0]]["aft"] += posted
                if len(late) == 1:
                    late.append(m["g0"][0])

    def SM(k, a=0, b=16):
        return A("sm", 16 * k + a, 16 * k + b)

    def SU(k):
        return A("su", 16 * k, 16 * k + 16)

    def tolist(out, pairs, start=True, more=(), stop=True):
        mmg([(out, Z(z, j), A(src, a + j, a + 256, 16)) for z, src, a in pairs for j in range(16)] + list(more), start, stop)

    def slots(t):
        b0 = 272 * t
        acc, bnd = A("ps4", 16, 32), A("ps4", 0, 16)
        mmg([(bnd, A("bd"), A("inc", 10, 161, 10))])
        for c in range(16):
            act(A("junk", 16 * (c % 4), 16 * (c % 4) + 16), bnd, AF.Sign, bias=A("il", 64 + c, 65 + c), scale=-1.0, acc=SM(9, c, c + 1))
        act(A("box", b0 + 256, b0 + 272), bnd)
        mmg([(A("ps5", 320, 336), Z(z1, r), A("inc", 1 + r, 161, 10)) for r in range(10)])
        act(A("tb", 0, 80, 5), A("ps5", 320, 336), bias=TBB)
        mmg([(A("ps5", 0, 160), A("tri"), A("ovl")), (A("ps5", 0, 160), A("bd"), A("inc", 0, 160))])
        act(A("incl", 0, 160), A("ps5", 0, 160))
        for u, tab, z in ((0, "tb", z16), (1, "incl", z1)):
            if u:
                ts(SU(1), acc, 0.0625, AL.mult, 160.0, AL.min)
                act(A("sa", 32, 48), acc)
                mmg([(acc, ID(1.0), A("sa", 32, 48))], True, False)
            else:
                ts(SU(0), SM(9), 2.5, AL.mult, 40.0, AL.add)
                act(A("sa", 0, 16), SM(9), bias=1280.0, scale=80.0)
                act(A("sa", 16, 32), SM(9), AF.Relu, bias=-15 * 4096.0, scale=4096.0)
                mmg([(acc, ID(1.0), A("sa", 0, 16)), (acc, ID(1.0), A("sa", 16, 32))], True, False)
            tt(A("cmp", 256 * u + 256, 256 * u + 512), IND(A(tab), SU(u)), A("sw"), AL.is_le)
            tolist(acc, [(z, "cmp", 256 * u + 256)], False)
        ts(SU(2), acc, float(L), AL.min)
        tt(SM(0), acc, SPQ, AL.min)
        if t == 0:
            act(A("box", b0, b0 + 256), IND(A("qq", 0, SP), SU(2)))
        else:
            act(A("box", b0, b0 + 256), IND(A("qb", 0, SP), SU(2)), AF.Relu, bias=7.0 - 1e-4, scale=-1.0 / 33)
        bx, rc = A("box", b0, b0 + 272), A("rcv", b0, b0 + 272)
        op("g", [lambda e: e.remote_dma(rc[0], bx[0], T.sem["got%d" % t], T.sem["out%d" % t], dst[1], dst[0], msk[0])],
           [bx], [(None, [("wire%d" % t, 0, 1, None)])], 500, lat=RLAT[t], sem="remote%d" % t, inc=len(msk[1]))
        ops[-1]["first"] = True

    def arrive(t, qn):
        b0 = 272 * t
        wire = [("wire%d" % t, 0, 1, None)]
        ts(SM(1), IL, (T["rcv"][:, b0 + 271:b0 + 272], wire, 1, BF), AL.is_ge, 4096.0, AL.mult)
        tt(SM(1), SM(1), SPQ, AL.min)
        tt(SM(1), SM(1), SM(0), AL.max)
        cp(SU(3), SM(1))
        cp(IND(A(qn), SU(3)), (T["rcv"][:, b0:b0 + 256], wire, 256, BF))

    def items(t):
        for k in range(5):
            a, b = 512 * k, 512 * k + 512
            pa, h, lim = A("ps%d" % (0, 2, 1, 3, 0)[k]), A("b1", a, b), -250.0 if t else -290.0
            if t and VH[t][k] >= 4:
                ts(A("qa", a, b), A("qb", a, b), 231.0, AL.subtract, -1.0 / 33, AL.mult)
            if VH[t][k] == 6:
                act(A("hh", a, b), IND(A("rct"), A("idx", a // 16, b // 16)))
                mmg([(pa, ID(0.125), A("qa", a, b)), (pa, ID(0.125), A("hh", a, b))])
                act(h, pa, AF.Sign, bias=(t - 15.5) / 8)
                tt(h, pa, h, AL.subtract)
                ts(A("qa" if t else "qb", a, b), h, 8.0 if t else -264.0, AL.mult, -7.0 if t else 495.0, AL.add)
                continue
            if VH[t][k] == 4:
                tt(A("hh", a, b), IND(A("rct"), A("idx", a // 16, b // 16)), A("qa", a, b), AL.add)
                ts(h, A("hh", a, b), 15.5 - t, AL.is_gt, 1.0 if t else 2.0, AL.mult)
                mmg([(pa, ID(1.0 if t else -33.0), A("hh", a, b)), (pa, ID(-16.0 if t else 264.0), h)])
                act(A("qa" if t else "qb", a, b), pa, bias=1.0 if t else 231.0)
                continue
            (cp if VI[t][k] else act)(A("hh", a, b), IND(A("rct"), A("idx", a // 16, b // 16)))
            two = [(pa, ID(1.0), A("qb" if t else "qq", a, b)), (pa, ID(-33.0), A("hh", a, b))]
            mmg(two)
            if VH[t][k] == 2:
                ts(h, pa, lim, AL.is_lt, 528.0, AL.mult)
                tt(h if t else A("qb", a, b), pa, h, AL.add)
                if t:
                    ts(A("qa", a, b), h, 264.0, AL.subtract, -1.0 / 33, AL.mult)
                continue
            act(h, pa, AF.Sign, bias=lim, scale=-1.0)
            mmg(two + [(pa, ID(264.0), h)])
            if t:
                act(A("qa", a, b), pa, scale=-1.0 / 33)
            else:
                act(A("qb", a, b), pa, bias=264.0)

    def branch(s, banks, ofs, wd, r, gp, m, sel2):
        z = str(s)
        kv, hv, sb = A("kv" + z), A("hv" + z), A("sb" + z)
        act(kv, IND(A("kt", 0, wd), ofs))
        if HVS[s]:
            act(hv, kv, bias=HB - 7.5)
        else:
            ts(hv, kv, HB - 7.5, AL.add)
        lo, hi = A(banks[0], 0, 256), A(banks[0], 256, 512)
        mmg([(lo, A("bda"), r), (lo, M("sk"), gp), (lo, A("bdb"), m)])
        act(sb, lo, AF.Sign, bias=7.5)
        mmg([(lo, ID(1.0), kv), (lo, ID(-1.0), hv), (lo, ID(-1.0), m), (lo, ID(128.0), sb)])
        act(A("rp" + z, 0, 256), lo, AF.Relu, bias=HB + 16 - 128)
        mmg([(hi, a, b) for a, b in sel2] + [(hi, ID(128.0), sb)])
        act(A("rp" + z, 256, 512), hi, AF.Relu)
        lo = A(banks[1], 0, 256)
        rk = A("rp" + z, 0, 256)
        mmg([(lo, ID(1.0), m), (lo, ID(16.0), kv), (lo, ID(-16.0), hv), (lo, ID(-15.0), rk), (lo, ID(120.0), sb)])
        act(A("kn" + z), lo, bias=16 * HB + 120)

    def lowest(s, bank, sf, gp, n32, ok):
        z = str(s)
        mmg([(A(bank, 0, 256), M(sf), gp)])
        ts(A("kw"), A(bank, 0, 256), -PH, AL.add)
        mmg([(A(bank, 256, 272), A("zz", 16, 144, p1=1), A("ones", 0, 16, p1=1))], True, False)
        for c in range(16):
            ts(A("eq", 256 * c, 256 * c + 256 - 16 * c), A("kw", 16 * c, 256), n32(c, c + 1), AL.is_equal, ok(c, c + 1), AL.mult)
            if c < 15:
                mmg([(A(bank, 272 + 16 * c, 512), A("bd"), A("eq", 256 * c + 16, 256 * c + 256 - 16 * c))], False, False)
        mmg([(A(bank, 256 + j, 512, 16), A("tl", 128 * j, 128 * j + 128), A("eq", j, 4096, 256)) for j in range(16)], False, True)
        act(A("ww" + z), A(bank, 256, 512), AF.Relu, scale=-1.0)
        tolist(A(bank, 0, 16), [(zs, "ww" + z, 0)], True, [(A(bank, 0, 16), A("idf"), n32(0, 16))])
        tt(SM(2 + s), A(bank, 0, 16), SPN, AL.min)
        ts(SU(4 + s), SM(2 + s), 8192.0 - (H if s < 2 else 0), AL.add)

    def newkeys(s, bank, x):
        z = str(s)
        lo = A(bank, 0, 256)
        mmg([(lo, ID(1.0625), A("hv" + z)), (lo, ID(264.0), A("ww" + z))])
        act(A("kt", x, x + I), lo, AF.Relu, bias=-1.0625 * HB - 264)

    def insert(t):
        z = str(t)
        G, x = A("gp", 0, 256), V + I * t
        if t:
            m = A("mq")
            ts(m, A("qb", 0, 256), 231.0, AL.subtract, -1.0 / 33, AL.mult)
            cp(A("v32", 0, 16), A("off", 0, 16))
        else:
            m = A("qa", 0, 256)
            cp(A("v32", 0, 80), A("off", 0, 80))
            act(A("gz"), G, scale=-1.0)
        ts(SM(5), A("idx", 0, 16), R - 0.5, AL.is_lt)
        branch(t, ("ps6", "ps6"), A("off", 0, 16), x, A("rb", 0, 256), G, m, [(M("sl"), G)])
        lowest(t, "ps7", "sfA", G, lambda a, b: A("v32", a, b), lambda a, b: SM(5, a, b))
        lo, hi = A("ps6", 0, 256), A("ps6", 256, 512)
        rk, rp, sb = A("rp" + z, 0, 256), A("rp" + z, 256, 512), A("sb" + z)
        if t == 0:
            mmg([(hi, ID(1.0), A("kv0")), (hi, ID(-1.0), A("hv0")), (hi, ID(-1.0), rk), (hi, ID(8.0), sb)])
            act(A("mk"), hi, bias=HB + 8)
            mmg([(hi, ID(1.0), A("kn0")), (hi, ID(16.0), A("mk"))])
            act(A("tn0"), hi, bias=CP)
        mmg([(lo, M("n1"), G), (lo, M("n2"), rp), (lo, M("nx0"), A("x0", I * t, I * t + I)), (lo, M("nx1"), A("x1"))]
            + ([(lo, M("sum"), A("mk"))] if t == 0 else []))
        act(A("pn" + z), lo)
        mmg([(hi, M("x1"), G)] + ([(hi, M("xx0"), A("x0", 0, I)), (hi, M("xx1"), A("x1"))] if t == 0 else []))
        if t == 0:
            cp(IND(A("tt", H, 4096), SU(4)), A("tn0"))
            act(A("tt", x, x + I), A("hv0"), bias=CPX, scale=2.0625)
        cp(IND(A("pt", H, 4096), SU(4 + t)), A("pn" + z))
        tt(A("pt", x, x + I), hi, A("ww" + z), AL.mult)
        cp(IND(A("kt", H, 4096), SU(4 + t)), A("kn" + z))
        newkeys(t, "ps7", x)

    def post_pre():
        wd = V + I
        cp(SU(7), A("la", 0, 16))
        if PS:
            act(A("qm"), A("mk"), bias=231.0, scale=-33.0)
            act(A("cm3"), IND(A("tt", 0, wd), SU(7)), bias=CPN)
            mmg([(A("ps4", 0, 256), ID(0.5), A("cm3")), (A("ps4", 0, 256), ID(-16.0), A("mk"))])
            act(A("cm3"), A("ps4", 0, 256), AF.Sign, bias=-120.25, scale=-1.0)
        else:
            ts(A("qm"), A("mk"), -33.0, AL.mult, 231.0, AL.add)
            act(A("thm"), A("mk"), bias=CP, scale=32.0)
            tt(A("cm3"), IND(A("tt", 0, wd), SU(7)), A("thm"), AL.is_lt)
        act(A("ge"), IND(A("pt", 0, wd), SU(7)), AF.Relu, bias=GB, scale=GS)
        tolist(A("ps5", 0, 16), [(zk, "cm3", 0), (zr, "ge", 0)])
        tt(SM(6), A("ps5", 0, 16), A("la", 0, 16), AL.max)
        ts(SM(7), SM(6), CR, AL.add, CR, AL.subtract)
        tt(SM(6), SM(6), SM(7), AL.subtract)
        cp(SU(8), SM(6))
        gu, x0, x1 = A("gu"), A("x0", 0, I), A("x1")
        if PS:
            act(A("ru"), IND(A("tt", 0, wd), SU(8)), bias=CPN)
            mmg([(A("ps5", 0, 256), ID(1.0), A("ru")), (A("ps5", 0, 256), ID(1.0), A("qm"))])
            act(A("ru"), A("ps5", 0, 256), bias=CPP)
        else:
            tt(A("ru"), IND(A("tt", 0, wd), SU(8)), A("qm"), AL.add)
        act(gu, IND(A("pt", 0, wd), SU(8)), AF.Relu, bias=GB, scale=GS)
        branch(2, ("ps4", "ps4"), SU(8), wd, A("ru"), gu, A("mk"), [(M("sp"), gu), (M("xs0"), x0), (M("xs1"), x1)])
        rp = A("rp2", 256, 512)
        lo, hi = A("ps5", 0, 256), A("ps4", 256, 512)
        mmg([(lo, M("t1"), gu), (lo, M("n2"), rp), (lo, M("t1"), A("gz")), (lo, ID(-8192.0), A("ww0"))])
        ts(A("cd"), lo, -8192.0, AL.is_equal)
        tolist(A("ps5", 0, 16), [(z0, "cd", 0)])
        act(SM(8), A("ps5", 0, 16))
        lowest(2, "ps5", "sfS", gu, lambda a, b: SM(6, a, b), lambda a, b: SM(8, a, b))
        lo = A("ps4", 0, 256)
        mmg([(lo, M("p1"), gu), (lo, M("p2"), rp), (lo, M("e2"), x0), (lo, M("e2"), x1),
             (lo, M("nx0"), A("x0", 2 * I, 3 * I)), (lo, M("nx0"), x1)])
        act(A("pn2"), lo)
        mmg([(hi, M("x1"), gu), (hi, M("q2"), rp)])
        x = V + 2 * I
        tt(A("pt", x, x + I), hi, A("ww2"), AL.mult)
        cp(IND(A("kt"), SU(6)), A("kn2"))
        newkeys(2, "ps5", x)

    def restart_pre():
        cp(A("v32", 80, 160), A("off", 80, 160))
        for X in (0, 1):
            c = 80 * X
            pl = "ps%d" % (2 + X)
            unround(pl, X, turned("ft", X), [turned("xn", X)], RS[1])
            tt(A("la", c, c + 80), A(pl, 0, 80), A("v32", c, c + 80), AL.min)
        sp = A("ps5", 160, 320)
        mmg([(sp, A("tri"), A("ovl")), (sp, A("bd"), A("inc", 0, 160)), (sp, ID(-8192.0), A("ovl"))])
        ts(A("sl"), sp, 256.5 - 8192, AL.is_lt, 1024.0, AL.mult)
        tt(A("lb"), A("la"), A("sl"), AL.max)

    def restart():
        for X in (0, 1):
            c = 80 * X
            pl = "ps%d" % (2 + X)
            sums("qb", X, 3)
            act(turned("hs", X, 256), A("ps%d" % X, 128, 384, p1=80))
            mmg([(A(pl, 0, 80), turned("hs", X, 256, 128 * u, 128 * u + 128), A("idf", 0, 80, p1=80)) for u in (0, 1)]
                + [(A(pl, 0, 80), ID(-8192.0), A("sl", c, c + 80))])
            ts(A("li", c, c + 80), A(pl, 0, 80), HC, AL.add)
            ts(A("li", c, c + 80), A("li", c, c + 80), 2 ** 23 + H - 1, AL.bitwise_and)
            tt(A("lh", c, c + 80), A("li", c, c + 80), A("lb", c, c + 80), AL.min)
            cp(A("off", c, c + 80), A("lh", c, c + 80))

    looks(0)
    ops[late[0]]["aft"].append(late[1])
    slots(0)
    insert(0)
    restart_pre()
    items(0)
    arrive(0, "qb")
    restart()
    post_pre()
    posted += list(range(len(ops) - 4, len(ops)))
    looks(1)
    slots(1)
    cp(IND(A("pt"), SU(6)), A("pn2"))
    insert(1)
    items(1)
    arrive(1, "qa")
    dma("y", D("yk", 0, H), A("kt", 0, H), 262144)
    dma("y", D("yk", H, W), A("kt", H, W), 720896)
    dma("y", D("y0", 0, H), A("pt", 0, H, p0=rA, ps=16), 32768)
    dma("y", D("y0", H, W), A("pt", H, W, p0=rS, ps=16), 90112)
    for n, r in (("y1", rC), ("yr", rR)):
        dma("y", D(n), A("pt", 0, W, p0=r, ps=16), 122880)
    dma("y", D("yq"), A("qa", 0, L), 655360)
    return ops


def depend(ops):
    last = {}
    deps = []
    for k, o in enumerate(ops):
        d = set()
        for rs, w in ((o["rd"], False), (o["wr"], True)):
            for (n, a, b, tag) in rs:
                ps = n.startswith("ps")
                for (k2, a2, b2, tag2, w2) in last.get(n, []):
                    if a < b2 and a2 < b and (tag is None or tag2 is None or tag == tag2):
                        if w or w2 or (ps and ops[k2]["eng"] != o["eng"]):
                            d.add(k2)
        for rs, w in ((o["rd"], False), (o["wr"], True)):
            for (n, a, b, tag) in rs:
                ent = last.setdefault(n, [])
                if w and tag is None:
                    ent[:] = [e for e in ent if not (a <= e[1] and e[2] <= b)]
                ent.append((k, a, b, tag, w))
        d.discard(k)
        deps.append(sorted(d))
    return deps


def place(eng, cost, pred, succ, first, key):
    n = len(cost)
    left = [len(d) for d in pred]
    ready = [(key[k], k) for k in range(n) if left[k] == 0]
    end = [0.0] * n
    busy = {e: [] for e in eng}
    while ready:
        x = min(ready)
        ready.remove(x)
        k = x[1]
        s = first[k]
        for j, lag in pred[k]:
            if end[j] + lag > s:
                s = end[j] + lag
        c = cost[k]
        line = busy[eng[k]]
        at = len(line)
        while at > 0 and line[at - 1][1] > s:
            at -= 1
        while at < len(line) and line[at][0] < s + c:
            if line[at][1] > s:
                s = line[at][1]
            at += 1
        line.insert(at, (s, s + c))
        end[k] = s + c
        for j, lag in succ[k]:
            left[j] -= 1
            if left[j] == 0:
                ready.append((key[j], j))
    return end


def replay(seq, eng, cost, pred, tail, more):
    end, free, last = [0.0] * len(cost), {e: 0.0 for e in eng}, 0.0
    for k in seq:
        s = free[eng[k]]
        for j, lag in pred[k]:
            x = end[j] + (lag + more if lag > 0 else 0.0)
            if x > s:
                s = x
        end[k] = free[eng[k]] = s + cost[k]
        if end[k] + tail[k] > last:
            last = end[k] + tail[k]
    return last


def order(ops, deps):
    n = len(ops)
    eng, cost, tail = [o["eng"] for o in ops], [o["cost"] for o in ops], [o["lat"] for o in ops]

    def lag(j, k):
        a, b = ops[j], ops[k]
        if j not in deps[k]:
            return 0.0
        if a["eng"] == b["eng"] and a["sem"] is None:
            return SAME.get(a["eng"], 45.0)
        return a["lat"] + 140.0
    full = [{j: lag(j, k) for j in set(deps[k]) | set(ops[k]["aft"])} for k in range(n)]
    pred = [[(j, x) for j, x in d.items() if not any(j in full[i] and full[i][j] + cost[i] + y >= x + 300.0 for i, y in d.items())] for d in full]
    succ = [[] for _ in ops]
    for k, d in enumerate(pred):
        for j, x in d:
            succ[j].append((k, x))
    others = [[c * f.get(o["kind"], 1.0) for c, o in zip(cost, ops)] for f, more in CASES]
    zero = [0.0] * n
    state = [SEED]

    def draw():
        state[0] = (state[0] * 1103515245 + 12345) % 2147483648
        return (state[0] >> 8) / 8388608.0
    key = [-x for x in place(list(range(n)), cost, succ, pred, tail, zero)]
    best = cur = None
    for it in range(TRIES):
        end = place(eng, cost, pred, succ, zero, key)
        if it % 50 == 0:
            back = place(eng, cost, succ, pred, tail, [-(a + b) for a, b in zip(end, tail)])
            end = place(eng, cost, pred, succ, zero, [-x for x in back])
        last = max(a + b for a, b in zip(end, tail))
        slack = AMP * (1.0 - it / TRIES) * draw()
        if cur is None or last <= cur[1] + 1000.0 + slack:
            st = [a - b for a, b in zip(end, cost)]
            seq = [k for x, k in sorted(zip(st, range(n)))]
            total = last + sum(replay(seq, eng, c, pred, tail, m[1]) for c, m in zip(others, CASES))
            if cur is None or total <= cur[2] + slack:
                before, prev, pairs = {}, {}, []
                for k in seq:
                    before[k] = prev.get(eng[k])
                    prev[eng[k]] = k
                k = max(zip([a + b for a, b in zip(end, tail)], range(n)))[1]
                while st[k] > 0.5:
                    ways = [j for j, x in pred[k] if end[j] + x > st[k] - 0.5]
                    if not ways:
                        pairs.append((before[k], k))
                    k = ways[0] if ways else before[k]
                cur = (st, last, total, pairs)
                if best is None or total <= best[2]:
                    best = cur
        key = list(cur[0])
        j, k = cur[3][int(draw() * len(cur[3]))]
        way = draw()
        if way < SHAKE:
            mid, wide, amp = key[k], 500.0 + 2500.0 * draw(), 300.0 + 1500.0 * draw()
            for i in range(n):
                if abs(key[i] - mid) < wide:
                    key[i] += amp * draw()
        elif way < 0.5 + SHAKE / 2:
            key[j] = key[k] + 1.0 + 2000.0 * draw() ** 3
        else:
            shift, todo, t0 = key[k] - key[j] + 1.0 + 2000.0 * draw() ** 3, [k], key[j]
            seen = {k}
            while todo:
                i = todo.pop()
                key[i] -= shift
                for a, x in pred[i]:
                    if a not in seen and key[a] > t0 - 1500.0:
                        seen.add(a)
                        todo.append(a)
    _PLAN["total"] = best[2] / (1 + len(CASES))
    _PLAN["cases"] = [int(replay([k for x, k in sorted(zip(best[0], range(n)))], eng, c, pred, tail, m[1])) for c, m in zip(others, CASES)]
    st = list(best[0])
    for k in range(n):
        if "alias" in ops[k] and ops[k - 1]["eng"] == "y":
            st[k - 1] = st[k] - 1.0
    return sorted([(k, st[k]) for k in range(n)], key=lambda x: x[1]), best[1]


def rank_program(g, core, T, topo):
    rank = T.rank_of(core)
    if rank is None:
        return
    cores = list(T.cores)
    nxt, prv = cores[(rank + 1) % len(cores)], cores[(rank - 1) % len(cores)]
    rid, pid, _ = topo.addr(nxt)
    ops = build(T, (rid, pid), (topo.mask(core, nxt), topo.engines(core, nxt)))
    nin = len(topo.engines(prv, core))
    if "seq" not in _PLAN:
        _PLAN["deps"] = depend(ops)
        _PLAN["seq"], _PLAN["end"] = order(ops, _PLAN["deps"])
    deps = _PLAN["deps"]
    eng = {"v": g.vector, "s": g.scalar, "p": g.tensor, "g": g, "y": g.sync}
    own = {"v": "sv", "s": "ss", "p": "sp", "g": "sg"}
    count, mark, clock = {}, {}, {}
    known = {e: {} for e in eng}
    for k, _s in _PLAN["seq"]:
        o = ops[k]
        if "alias" in o:
            mark[k], clock[k] = mark[o["alias"]], clock[o["alias"]]
            continue
        e = o["eng"]
        kn = known[e]
        for j in sorted(deps[k], key=lambda j: -mark[j][2]):
            if e == "p" and ops[j]["eng"] == "p":
                continue
            sem, v, _t = mark[j]
            if kn.get(sem, 0) < v:
                eng[e].wait_ge(T.sem[sem], v)
                kn[sem] = v
                for s2, v2 in clock[j].items():
                    if kn.get(s2, 0) < v2:
                        kn[s2] = v2
        sem = o["sem"]
        if sem is not None and sem.startswith("remote"):
            o["fns"][0](eng[e])
            t = sem[6:]
            count["out" + t] = o["inc"]
            count["got" + t] = nin
            mark[k] = ("got" + t, nin, len(mark))
            clock[k] = {}
            continue
        sem = sem or own[e]
        for f in o["fns"]:
            f(eng[e]).then_inc(T.sem[sem], o["inc"])
            count[sem] = count.get(sem, 0) + o["inc"]
        mark[k] = (sem, count[sem], len(mark))
        clock[k] = dict(kn)
    for sem in sorted(count):
        if known["g"].get(sem, 0) < count[sem] or sem in own.values():
            g.wait_ge(T.sem[sem], count[sem])
